import numpy as np, ml_dtypes
CORES = [51,54,179,182]
N = 4
BF = ml_dtypes.bfloat16
def gentries(a):
    return np.ascontiguousarray(a.reshape(8, 16, -1).transpose(0, 2, 1)).reshape(8, -1)
def gtable(e):
    e = np.asarray(e); return np.ascontiguousarray(e.reshape(8, -1, 16).transpose(0, 2, 1)).reshape(128, -1).astype(np.int32)
G, C, K, RO, SH = 512, 2048, 256, 5, 9
NONE = N * G
def batch(rng, keep=(), high=()):
    key = rng.random((8, C)) * np.where(np.arange(C) >> SH == 0, 3.0, 1.0)
    for c in keep: key[:, c] += 4
    for g in high: key[g, :1 << SH] += 4
    s = np.ascontiguousarray(np.argsort(key, axis=1)[:, :N * K]); w = rng.integers(0, NONE, (8, 16, 4)); ro = np.zeros((8, 16, N * K), np.int64)
    for r in range(N):
        for t in range(16):
            if t < RO: ro[:, t, r * K:(r + 1) * K] = (r + t) % N * G + np.argsort(rng.random((8, G)), axis=1)[:, :K]
            else: ro[:, t, r * K:(r + 1) * K] = np.take_along_axis(w[:, t], rng.integers(0, 4, (8, K)), 1)
    return s, ro, w
def living(rng, s, ro, w, share):
    pa = np.full((8, 16, C), NONE, np.int64); live, dead = [], []
    for g in range(8):
        rest = rng.permutation(np.setdiff1d(np.arange(C), s[g])); h = max(int(len(rest) * share), 8)
        a = rest[h:]; m = len(a); v = rng.integers(0, NONE, (16, m))
        for k in range(RO, 16): v[k] = w[g, k][rng.integers(0, 4, m)]
        v = np.where(rng.random((16, m)) < 0.8 * rng.random((1, m)), ro[g][:, np.arange(m) % (N * K)], v)
        no = rng.random((16, m)) < 0.9 * rng.random((1, m)); no[rng.integers(0, 16, m), np.arange(m)] = False
        pa[g][:, a] = np.where(no, NONE, v); live.append(a); dead.append(rest[:h])
    return pa, live, dead
def trunks(rng, s, ro, live, dead):
    op = rng.integers(0, N * K, (N, 8, G))
    for t in rng.permutation(RO):
        for q in range(N):
            r = int((q - t) % N); np.put_along_axis(op[q], ro[:, t, r * K:(r + 1) * K] - q * G, np.ascontiguousarray(np.broadcast_to(r * K + np.arange(K), (8, K))), 1)
    tr = np.zeros((N, 8, 16, G), np.int64); sh = (N, 16, G)
    for g in range(8):
        a = live[g]; m = len(a); top = np.sort(a)[-(m >> 3):]; x = a[rng.integers(0, m, sh)]
        x = np.where(rng.random(sh) < rng.choice(np.array([0.3, 0.6, 0.8, 0.9, 1.0]), (N, 1, G)), top[rng.integers(0, len(top), sh)], x)
        x = np.where(rng.random(sh) < rng.choice(np.array([0.0, 0.1, 0.25]), (N, 1, G)), a[(op[:, g][:, None, :] + N * K * rng.integers(0, 2, sh)) % m], x)
        gone = np.concatenate([dead[g], s[g][::4]])
        tr[:, g] = np.where(rng.random(sh) < rng.choice(np.array([0.0, 0.0, 0.1, 0.3]), (N, 1, G)), gone[rng.integers(0, len(gone), sh)], x)
    return tr
def pack(tr, pa, s, ro):
    return {"trunk": np.ascontiguousarray(tr.reshape(N, 128, G)).astype(np.int32), "paths": np.stack([pa.reshape(128, C)] * N).astype(np.int32),
            "calls": np.stack([gtable(s[:, r * K:(r + 1) * K]) for r in range(N)]), "routes": np.stack([ro[:, :, r * K:(r + 1) * K].reshape(128, K) for r in range(N)]).astype(np.int32)}
def setup_inputs(rng):
    s, ro, w = batch(rng); pa, live, dead = living(rng, s, ro, w, 0.05)
    return pack(trunks(rng, s, ro, live, dead), pa, s, ro)
def setup_inputs_ties(rng):
    edge = np.array([0, C - 1] + [e for b in range(1, C >> SH) for e in ((b << SH) - 1, b << SH)])
    s, ro, w = batch(rng, edge); pa, live, dead = living(rng, s, ro, w, 0.05); tr = trunks(rng, s, ro, live, dead); sh = (N, 16, G); k = np.arange(16)[None, :, None]
    for g in range(8):
        a = np.union1d(live[g], edge); d = np.setdiff1d(np.append(dead[g], s[g][0]), edge)
        few = pa[g][:, live[g][:3]]; pa[g][:, a] = few[:, rng.integers(0, 3, len(a))]
        x = tr[:, g].copy(); x[:, 8:] = x[:, :8][:, ::-1].copy()
        kind = rng.integers(0, 5, (N, 1, G)); end = rng.choice(np.array([0, 15]), (N, 1, G)); z = a[rng.integers(0, len(a), sh)]
        x = np.where(kind == 1, edge[rng.integers(0, len(edge), sh)], np.where(kind == 2, z, x))
        tr[:, g] = np.where(kind == 3, np.where(k == end, d[rng.integers(0, len(d), sh)], z), x)
        j = rng.permutation(N * K)[:64]; r = j // K; c = rng.permutation(live[g])[:64]
        pa[g][:, c] = ro[g][:, j]; tr[r, g, rng.integers(0, 16, 64), ro[g, 0, j] - r * G] = c
        u = rng.permutation(np.setdiff1d(np.nonzero(s[g] >> SH == (C - 1) >> SH)[0], j))[:16]; q = u // K; at = ro[g, 0, u] - q * G
        b = np.sort(rng.permutation(np.setdiff1d(live[g][live[g] >> SH == 0], np.append(edge, c)))[:32].reshape(2, 16), axis=0)
        pa[g][:, b[0]] = ro[g][:, u]; pa[g][:, b[1]] = ro[g][:, u]; h = rng.integers(0, 16, 16)
        pa[g, h, b[0]] = np.where(rng.random(16) < 0.5, NONE, (ro[g, h, u] + 1) % NONE)
        y = tr[:, g]; e = rng.integers(0, 16, 16)
        y[q, :, at] = b[rng.integers(0, 2, (16, 16)), np.arange(16)[:, None]]
        y[q, e, at] = b[1]; y[q, (e + 8) & 15, at] = b[0]
    return pack(tr, pa, s, ro)
def setup_inputs_same(rng):
    few = np.array([0, 1, 2, (1 << SH) - 1]); keep = np.append(few, C - 1)
    s, ro, w = batch(rng, keep, (5, 6, 7)); pa, live, dead = living(rng, s, ro, w, 0.05); tr = trunks(rng, s, ro, live, dead); sh = (N, 16, G)
    for g in range(8):
        pa[g][:, keep] = ro[g][:, rng.integers(0, N * K, len(keep))]
        top = np.union1d(live[g][live[g] >> SH == (C - 1) >> SH], np.array([C - 1])); x = top[rng.integers(0, len(top), sh)]
        if g > 4:
            low = rng.permutation(live[g][live[g] >> SH == 0]); n = rng.permutation(N * K); q = np.arange(N * K) // K; at = ro[g, 0] - q * G
            if g == 5: i = (n >= 256).astype(np.int64) + (n >= 768)
            elif g == 6: i = (n >= 1024).astype(np.int64)
            else: i = np.arange(N * K) % len(low)
            y = np.where(tr[:, g] >> SH == 0, x, tr[:, g]); y[q, :, at] = x[q, :, at]
            y[q, rng.integers(0, 16, N * K), at] = low[i]; tr[:, g] = y
            continue
        one = few[rng.integers(0, (1, 2, 4)[g % 3], (N, 1, G))]
        x = np.where(np.arange(16)[None, :, None] == rng.integers(0, 16, (N, 1, G)), one, x)
        tr[:, g] = np.where(rng.random((N, 1, G)) < (1.0 if g < 4 else 0.6), x, tr[:, g])
    return pack(tr, pa, s, ro)
def setup_inputs_block(rng):
    s, ro, w = batch(rng, [C - 1]); o = rng.permutation(8); f = int(o[4])
    if not np.any(s[f] == 0): s[f, int(rng.integers(0, N * K))] = 0
    for r in range(N):
        p = rng.permutation(G); v = (r - 1) % N
        ro[f, 0, r * K:(r + 1) * K] = r * G + p[:K]; ro[f, 1, v * K:(v + 1) * K] = r * G + p[K:2 * K]
    pa, live, dead = living(rng, s, ro, w, 0.05); tr = trunks(rng, s, ro, live, dead); sh = (N, 16, G); q = int(rng.integers(0, N))
    for h in range(5):
        g = int(o[h]); pa[g][:, C - 1] = ro[g][:, 0]
        top = np.union1d(live[g][live[g] >> SH == (C - 1) >> SH], np.array([C - 1])); d = np.setdiff1d(dead[g], np.array([C - 1]))
        full = top[rng.integers(0, len(top), sh)]; free = d[rng.integers(0, len(d), sh)]
        if h == 0: tr[:, g] = full
        if h == 1 or h == 2: tr[:, g] = free
        if h == 2: tr[q, g] = full[q]
        if h == 3: pa[g] = NONE
        if h == 4:
            a = np.arange(N * K) // K; b = (a + 1) % N; u = ro[g, 0] - a * G; v = ro[g, 1] - b * G; y = tr[:, g]
            y[a, rng.integers(0, 16, N * K), u] = d[rng.integers(0, len(d), N * K)]
            y[b, :, v] = full[b, :, v]; y[b[::4], rng.integers(0, 16, len(b[::4])), v[::4]] = s[g][::4]
    return pack(tr, pa, s, ro)
def setup_inputs_late(rng):
    s, ro, w = batch(rng); pa, live, dead = living(rng, s, ro, w, 0.05); tr = trunks(rng, s, ro, live, dead); sh = (N, 16, G)
    for g in range(8):
        tr[:, g] = np.where(rng.random(sh) < rng.choice(np.array([0.0, 0.5, 1.0]), (N, 1, G)), s[g][rng.integers(0, N * K, sh)], tr[:, g])
        u = np.argsort(s[g, :K])[:16]; v = K + np.argsort(s[g, K:2 * K])[-16:]
        y = tr[2, g]; y[:, ro[g, 1, v] - 2 * G] = s[g][u]
        for a, r, t in ((u, 0, 0), (v, 1, 0), (u, 0, 1)):
            y = tr[r + t, g]; y[:2, ro[g, t, a] - (r + t) * G] = dead[g][0]
        e = np.argsort(s[g, :K])[16:]; e = e[np.isin(ro[g, 1, e], ro[g, 0, K:2 * K], invert=True)]; lo, hi = e[:16], e[-16:]
        top = live[g][live[g] >> SH == (C - 1) >> SH]
        assert len(e) >= 32 and len(top) > 0 and np.all((s[g][lo] >> SH) < (s[g][hi] >> SH))
        assert np.all(np.any(pa[g][:, top] != NONE, axis=0)) and np.all(pa[g][:, dead[g][0]] == NONE)
        y = tr[0, g]; y[:2, ro[g, 0, np.append(lo, hi)]] = dead[g][0]
        y = tr[1, g]; y[:, ro[g, 1, lo] - G] = top[rng.integers(0, len(top), 16)]; y[:, ro[g, 1, hi] - G] = s[g][lo]
    return pack(tr, pa, s, ro)
def setup_inputs_spread(rng):
    s, ro, w = batch(rng); late = ro[:, RO:]; ro[:, RO:] = np.where(rng.random(late.shape) < 0.5, rng.integers(0, NONE, late.shape), late)
    pa, live, dead = living(rng, s, ro, w, 0.02); tr = trunks(rng, s, ro, live, dead)
    pa = np.where((pa != NONE) & (rng.random(pa.shape) < 0.5), np.minimum((NONE * rng.random(pa.shape) ** 4).astype(np.int64), NONE - 1), pa)
    x = np.minimum((C * rng.random(tr.shape) ** rng.choice(np.array([0.25, 1.0, 4.0]), (N, 8, 1, G))).astype(np.int64), C - 1)
    return pack(np.where(rng.random((N, 8, 1, G)) < 0.5, x, tr), pa, s, ro)
def check_inputs(d):
    bad = []
    for k, lo, hi in (("trunk", 0, C - 1), ("paths", 0, NONE), ("calls", 0, C - 1), ("routes", 0, NONE - 1)):
        if np.min(d[k]) < lo or np.max(d[k]) > hi: bad.append("range of " + k)
    if bad: return bad
    if np.any(d["paths"] != d["paths"][:1]): bad.append("paths alike on all ranks")
    s = np.concatenate([gentries(a) for a in d["calls"]], axis=1).astype(np.int64)
    if np.any(np.diff(np.sort(s, axis=1), axis=1) == 0): bad.append("calls of a group all different")
    if np.any(np.take_along_axis(d["paths"][0].reshape(8, 16, C), s[:, None, :], 2) != NONE): bad.append("paths of the seekers are none")
    own = (np.arange(N)[:, None] + np.arange(RO)[None, :]) % N
    at = d["routes"].astype(np.int64).reshape(N, 8, 16, K)[:, :, :RO] - own[:, None, :, None] * G
    if np.min(at) < 0 or np.max(at) > G - 1: bad.append("row t of routes names bundles of rank (r + t) mod N")
    if np.any(np.diff(np.sort(at, axis=3), axis=3) == 0): bad.append("row t of routes names different bundles")
    return bad
def reference(trunk, paths, calls, routes):
    tr = trunk.astype(np.int64).reshape(N, 8, 16, G); pa = paths[0].astype(np.int64).reshape(8, 16, C)
    sl = np.stack([gentries(a) for a in calls]).astype(np.int64); ro = routes.astype(np.int64).reshape(N, 8, 16, K)
    row = np.arange(16)[None, :, None]; D = C // N
    for t in range(RO):
        new = pa.copy(); gone = np.zeros((8, C), bool)
        for q in range(N):
            r = (q - t) % N; s = sl[r]; at = ro[r, :, t] - q * G
            hold = np.take_along_axis(tr[q], at[:, None, :], 2)
            hop = np.take_along_axis(pa, hold.reshape(8, 1, 16 * K), 2).reshape(8, 16, 16, K)
            dead = np.logical_not(np.any(hop != NONE, axis=1))
            like = np.add.reduce((hop == ro[r][:, :, None, :]).astype(np.int64), axis=1)
            may = (hold >> SH) < (s >> SH)[:, None, :]
            key = np.where(dead, 2 ** 22 + 15 - row, np.where(may, (like * C + C - 1 - hold) * 16 + 15 - row, -1))
            best = np.max(key, axis=1); p = 15 - (best & 15)
            go = np.any(np.take_along_axis(pa, s[:, None, :], 2) != NONE, axis=1) | (t == 0)
            won = go & (best >= 0); vic = np.take_along_axis(hold, p[:, None, :], 1)[:, 0]
            b, i = np.nonzero(won); tr[q, b, p[b, i], at[b, i]] = s[b, i]; new[b, t, s[b, i]] = ro[r, b, t, i]
            b, i = np.nonzero(won & (best < 2 ** 22)); gone[b, vic[b, i]] = True
            b, i = np.nonzero(go & (best < 0)); gone[b, s[b, i]] = True
        pa = np.where(gone[:, None, :], NONE, new)
    return {"yt": tr.reshape(N, 128, G).astype(np.float32), "yp": np.stack([pa[:, :, r * D:(r + 1) * D].reshape(128, D) for r in range(N)]).astype(np.float32)}

@@ -1,0 +1,457 @@
+from concourse.bass import DstId, RemoteDMATransfer
+from concourse.mybir import AluOpType as A, ActivationFunctionType as AF
+
+N, G, C, K, RO = 4, 512, 2048, 256, 5
+NONE = N * G
+f32, b16, i32, u16 = "float32", "bfloat16", "int32", "uint16"
+PR, PSK, PTF, PCF, PSL, PL, PW = 0, 256, 272, 288, 304, 320, 368
+LK = 65536.0
+OUT = 6400.0
+PIECES = [(0, 0, 128, "s"), (1, 0, 64, "s"), (1, 64, 96, "s"), (1, 96, 128, "v")]
+DORD = [0, 3, 1, 2]
+LIKE = [(0, 0, 128, True, True), (1, 96, 128, True, False), (1, 0, 96, False, True)]
+PRE = 2
+WS = 5
+FK = ["Fa", "Fb"]
+FSK = ["FS%d" % t for t in range(RO)]
+
+
+def sb(names, cols, dtype):
+    return {n: ("sbuf", [128, cols], dtype) for n in names.split()}
+
+
+SCRATCH = {
+    **sb("iA", 1, i32), **sb("BP", 1, f32), **sb("MB", 2, f32), **sb("CC", 8, i32), **sb("CCf", 8, f32),
+    **sb("iX", 144, f32), **sb("Z Z0", 144, b16), **sb("iG16 iG8 iWT Idf Idm BO IND", 128, f32), **sb("IREV Idb Idn BW Yf", 128, b16),
+    **sb("i16t MK T1 HIF", 16, f32), **sb("CI TH BI HI LOI PPI T2", 16, i32), **sb("BL BD", 8, b16),
+    **sb("iS SM0 Hf KH DIFF DM SC1 SD", 256, f32), **sb("iOF RI", 256, i32), **sb("OFFS H16", 256, u16),
+    **sb("SMb ELIG Gs LOD SED LOS LOO SES SEO", 256, b16), **sb("iFI", 64, f32), **sb("OFI", 64, u16),
+    **sb("LI", 80, i32), **sb("TI", 512, i32), **sb("XB XT", 32, f32), **sb("TR S0 YO", 512, f32), **sb("BS", 512, b16),
+    **sb("F FS", 2048, i32), **sb("NI W OH", 2048, b16), **sb("E Gd", 4096, b16), **sb("RB0 RB1", 4096, f32),
+    **sb("PK0 PK1 PK2 PK3", PW, f32), **sb("UL", 4 * 112, u16), **sb("KS", RO * N * 128, b16),
+    **{n: ("psum", [128, 512], f32) for n in "pK pD pX pY pT pR pM".split()},
+}
+SEMAPHORES = (["cv", "cs", "ct", "cg", "lset"] + ["set%d" % r for r in range(N)] + ["kill%d" % t for t in range(RO)]
+              + ["lk%d" % t for t in range(RO)] + ["d%d" % i for i in range(36)])
+
+
+def rank_program(g, core, T, topo):
+    q = T.rank_of(core)
+    if q is None:
+        return
+    others = [(q + i) % N for i in (1, 2, 3)]
+
+    def plan(a):
+        chip = topo.cores_of(T.cores[a])
+        away = [r for r in range(N) if T.cores[r] not in chip]
+        near = [r for r in range(N) if r != a and T.cores[r] in chip]
+        out = topo.engines(T.cores[a], T.cores[away[0]])
+        res = {}
+        for n, r in enumerate(away):
+            k = len(out) // len(away)
+            res[r] = out[n * k:(n + 1) * k]
+        for n, r in enumerate(near):
+            rest = [e for e in topo.engines(T.cores[a], T.cores[r]) if e not in out]
+            k = len(rest) // len(near)
+            res[r] = rest[n * k:(n + 1) * k]
+        return res
+    plans = [plan(r) for r in range(N)]
+
+    queue = {"v": g.vector, "s": g.scalar, "t": g.tensor, "g": g, "y": g.sync}
+    cnt, waited, lastw, readers, total, nd = {}, {}, {}, {}, {}, [0]
+
+    def need(qn, toks):
+        best = {}
+        for s, v in toks:
+            best[s] = max(best.get(s, 0), v)
+        for s, v in sorted(best.items()):
+            if waited.get((qn, s), 0) < v:
+                queue[qn].wait_ge(T.sem[s], v)
+                waited[(qn, s)] = v
+
+    def hazards(qn, reads, writes):
+        toks = []
+        for k in reads + writes:
+            ps = k[0] == "p"
+            for (oq, s, v, far) in lastw.get(k, []):
+                if not (ps and oq == qn):
+                    toks.append((s, v))
+            if ps or k in writes:
+                for (oq, s, v, far) in readers.get(k, []):
+                    if far or oq != qn:
+                        toks.append((s, v))
+        return toks
+
+    def record(tok, reads, writes):
+        for k in reads:
+            if k not in writes:
+                readers.setdefault(k, []).append(tok)
+        for k in writes:
+            lastw[k] = [tok]
+            readers[k] = []
+
+    def op(qn, fn, reads, writes):
+        need(qn, hazards(qn, reads, writes))
+        s = "c" + qn
+        cnt[s] = cnt.get(s, 0) + 1
+        fn().then_inc(T.sem[s], 1)
+        total[s] = cnt[s]
+        record((qn, s, cnt[s], False), reads, writes)
+
+    def dma(qn, out_, in_, reads, writes):
+        need(qn, hazards(qn, reads, writes))
+        s = "d%d" % nd[0]
+        nd[0] += 1
+        queue[qn].dma_start(out_, in_).then_inc(T.sem[s], 16)
+        total[s] = 16
+        record((qn, s, 16, True), reads, writes)
+
+    def arrive(key, s, v):
+        lastw[key] = [("remote", s, v, True)]
+        readers[key] = []
+        total[s] = v
+
+    def send(ap, reads, rsem, lsem):
+        need("g", hazards("g", reads, []))
+        tr = []
+        for r in others:
+            rid, pid = topo.addr(T.cores[r], core)
+            tr.append(RemoteDMATransfer(dst_ids=[DstId(rid=rid, pnc=pid)], dma_engine_mask=sum(1 << e for e in plans[q][r]),
+                                        remote_sem=T.sem[rsem], src=ap, dst=ap))
+        g.remote_dma_fused(tr, local_sem=T.sem[lsem])
+        total[lsem] = sum(len(plans[q][r]) for r in others)
+        for k in reads:
+            readers.setdefault(k, []).append(("g", lsem, total[lsem], True))
+
+    V, S, E_ = g.vector, g.scalar, g.tensor
+
+    def ts(o, i, s1, s2, a, b, reads, writes):
+        if b is None:
+            op("v", lambda: V.tensor_scalar(o, i, s1, None, a), reads, writes)
+        else:
+            op("v", lambda: V.tensor_scalar(o, i, s1, s2, a, b), reads, writes)
+
+    def tt(o, i0, i1, a, reads, writes):
+        op("v", lambda: V.tensor_tensor(o, i0, i1, a), reads, writes)
+
+    def cp(o, i, reads, writes):
+        op("v", lambda: V.tensor_copy(o, i), reads, writes)
+
+    def fill(o, c, w):
+        op("v", lambda: V.memset(o, c), [], [w])
+
+    def act(o, i, reads, writes, func=AF.Copy, **kw):
+        op("s", lambda: S.activation(o, i, func, **kw), reads, writes)
+
+    def mm(o, l, r, st, sp, reads, writes):
+        op("t", lambda: E_.matmul(o, l, r, st, sp), reads, writes)
+
+    def scan(o, d0, d1, a, b, reads, writes):
+        op("v", lambda: V.tensor_tensor_scan(o, d0, d1, 0.0, a, b), reads, writes)
+
+    def iota(n, pat, base=0, cm=0, keys=None):
+        o = T[n]
+        if o.dtype == T.iA.dtype:
+            op("g", lambda: g.iota(o[:], pat, base, cm), [], keys or [n])
+        else:
+            op("g", lambda: g.iota(o[:], pat, base, cm, allow_small_or_imprecise_dtypes=True), [], keys or [n])
+
+    PKb = [T["PK%d" % r] for r in range(N)]
+    own = PKb[q]
+    pk = ["PK%d" % r for r in range(N)]
+    ul = ["UL%d" % r for r in range(N)]
+    for r in others:
+        arrive(pk[r], "set%d" % r, len(plans[r][q]))
+
+    def UL(r, a):
+        return T.UL[:, 112 * r + a:112 * r + a + 16]
+
+    def set_list(r):
+        cp(T.UL[:, 112 * r:112 * r + 80], PKb[r][:, PCF:PW], [pk[r]] if r != q else ["OC", "OS", "OL1", "OL2", "OL3"], [ul[r]])
+
+    rbuf = {0: "RB0", 1: "RB1", 2: "RB1", 3: "RB1", 4: "RB0"}
+
+    def expand(t, *parts):
+        r = (q - t) % N
+        for i in parts:
+            act(T[rbuf[t]][:, 1024 * i:1024 * i + 1024], PKb[r][:, PR:PR + 256].indirect(T.OFFS[:, 64 * i:64 * i + 64]),
+                ["OR" if r == q else pk[r], "OFFS"], ["%s%d" % (rbuf[t], i)])
+
+    def blist(t):
+        if t == 0:
+            return UL(q, 80), "ULa"
+        if t == 4:
+            return UL(q, 96), "ULb"
+        r = (q - t) % N
+        return UL(r, 16 + 16 * t), ul[r]
+
+    def hold_v(t):
+        L, lk = blist(t)
+        cp(T.H16[:], T.TR[:].indirect(L), ["TR", lk], ["H16"])
+
+    def hold_s(t):
+        L, lk = blist(t)
+        act(T.Hf[:], T.TR[:].indirect(L), ["TR", lk], ["Hf"])
+        act(T.KH[:], T.TR[:].indirect(L), ["TR", lk, "BP"], ["KH"], func=AF.Identity, bias=T.BP[:], scale=-32.0)
+
+    def hold_d(t):
+        for h in range(2):
+            mm(T.pR[:, 256 * h:256 * h + 256], T.Idm[:], T.Hf[:], False, h == 1, ["Idm", "Hf"], ["pR"])
+        act(T.ELIG[:], T.pR[:, 256:512], ["pR", "MB1"], ["ELIG"], func=AF.Sign, bias=T.MB[:, 1:2])
+        act(T.DIFF[:], T.pR[:, 0:256], ["pR"], ["DIFF"])
+
+    def like(t, parts):
+        for i in parts:
+            b, j0, j1, first, last = LIKE[i]
+            u, w = 2048 * b + 16 * j0, 2048 * b + 16 * j1
+            tt(T.E[:, u:w], T.F[:].indirect(T.H16[:, 128 * b + j0:128 * b + j1]), T[rbuf[t]][:, u:w], A.is_equal,
+               FK + ["H16"] + ["%s%d" % (rbuf[t], n) for n in range((128 * b + j0) // 64, (128 * b + j1 + 63) // 64)], ["E%d" % i])
+            full = T.pK[:, 128 * b:128 * b + 128]
+            if first:
+                mm(full, T.KH[:, 128 * b:128 * b + 128], T.Idf[:], True, False, ["KH", "Idf"], ["pK"])
+            for p in range(16):
+                mm(T.pK[j0:j1, 128 * b + p:128 * b + 128:16], T.E[:, u + p:w:16], T.BL[:], False, False, ["E%d" % i, "BL"], ["pK"])
+            if last:
+                mm(full, T.ELIG[:, 128 * b:128 * b + 128], T.Idn[:], False, True, ["ELIG", "Idn"], ["pK"])
+
+    WK = ["W%d" % l for l in range(16)]
+
+    def build_w():
+        for l in range(16):
+            o, m = T.W[:, 128 * l:128 * l + 128], T.MK[:, 15 - l:16 - l]
+            if l < WS:
+                act(o, T.Yf[:], ["Yf", "MK"], [WK[l]], scale=m)
+            else:
+                ts(o, T.Yf[:], m, None, A.mult, None, ["Yf", "MK"], [WK[l]])
+
+    def kills_t(t):
+        mm(T.pY[:, 0:128], T.Idb[:], T.Yf[:], True, False, ["Idb", "Yf"], ["pY"])
+        for n, r in enumerate([q] + others):
+            c = ((t - 1) * N + r) * 128
+            mm(T.pY[:, 0:128], T.KS[:, c:c + 128], T.Idb[:], False, n == N - 1, ["KS%d_%d" % (t - 1, r), "Idb"], ["pY"])
+
+    def kills_v():
+        ts(T.Yf[:], T.pY[:, 0:128], 1.0, None, A.min, None, ["pY"], ["Yf"])
+
+    def dead_pass(t, qn):
+        if t > 0 and qn == "v":
+            r = (q - t) % N
+            cp(T.Gs[:], T.W[:].indirect(UL(r, 16)), WK + [ul[r]], ["Gs"])
+        for i, (b, j0, j1, e) in enumerate(PIECES):
+            if e != qn:
+                continue
+            win = T.W[:].indirect(T.H16[:, 128 * b + j0:128 * b + j1])
+            o = T.Gd[:, 2048 * b + 16 * j0:2048 * b + 16 * j1]
+            if e == "s":
+                act(o, win, WK + ["H16"], ["Gd%d" % i])
+            else:
+                cp(o, win, WK + ["H16"], ["Gd%d" % i])
+
+    def dead_t(t):
+        for i in DORD:
+            b, j0, j1, e = PIECES[i]
+            for p in range(16):
+                o = T.pD[j0:j1, 128 * b + p:128 * b + 128:16]
+                last = p == 15 and t > 0
+                mm(o, T.Gd[:, 2048 * b + 16 * j0 + p:2048 * b + 16 * j1:16], T.BW[:, 8 * p:8 * p + 8], True, not last, ["Gd%d" % i, "BW"], ["pD"])
+                if last:
+                    mm(o, T.Gs[:, 128 * b + j0:128 * b + j1], T.BD[:], False, True, ["Gs", "BD"], ["pD"])
+
+    def candidates(t):
+        r = (q - t) % N
+        scan(T.SC1[:], T.SM0[:], T.pK[:, 0:256], A.mult, A.max, ["SM0", "pK"], ["SC1"])
+        tt(T.BI[:], T.SC1[:, 15::16], PKb[r][:, PSK:PSK + 16], A.max, ["SC1", pk[r]], ["BI"])
+        ts(T.HI[:], T.BI[:], 5, 127, A.logical_shift_right, A.bitwise_and, ["BI"], ["HI"])
+        ts(T.LOI[:], T.BI[:], 12, 15, A.logical_shift_right, A.bitwise_and, ["BI"], ["LOI"])
+        ts(T.PPI[:], T.BI[:], 31, None, A.bitwise_and, None, ["BI"], ["PPI"])
+        cp(T.HIF[:], T.HI[:], ["HI"], ["HIF"])
+        for c in range(16):
+            ts(T.OH[:, 128 * c:128 * c + 128], T.IREV[:], T.HIF[:, c:c + 1], None, A.is_equal, None, ["IREV", "HIF"], ["OH%d" % c])
+
+    def decide(t):
+        scan(T.SD[:], T.SM0[:], T.pD[:, 0:256], A.mult, A.max, ["SM0", "pD"], ["SD"])
+        d = T.SD[:, 15::16]
+        tt(T.LOD[:, 0::16], d, T.LOI[:], A.add, ["SD", "LOI"], ["LOD"])
+        scan(T.LOS[:], T.SMb[:], T.LOD[:], A.mult, A.add, ["SMb", "LOD"], ["LOS"])
+        ts(T.LOO[:], T.LOS[:], 0.0, None, A.is_equal, None, ["LOS"], ["LOO"])
+        for gg in range(8):
+            for b in range(2):
+                c = 8 * b + gg
+                mm(T.pX[:, 16 * gg:16 * gg + 16], T.OH[:, 128 * c:128 * c + 128], T.LOO[:, 16 * c:16 * c + 16], b == 0, b == 1, ["OH%d" % c, "LOO"], ["pX"])
+        c = (t * N + q) * 128
+        if t < 3:
+            expand(t + 1, 0)
+        act(T.KS[:, c:c + 128], T.pX[:, 0:128], ["pX"], ["KS%d_%d" % (t, q)])
+        if t < 3:
+            expand(t + 1, 1)
+        send(T.KS[:, c:c + 128], ["KS%d_%d" % (t, q)], "kill%d" % t, "lk%d" % t)
+        n = sum(len(plans[r][q]) for r in others)
+        for r in others:
+            arrive("KS%d_%d" % (t, r), "kill%d" % t, n)
+        ts(T.T1[:], d, 0.0, None, A.is_equal, None, ["SD"], ["T1"])
+        ts(T.T2[:], d, 1.0 / 64, None, A.mult, None, ["SD"], ["T2"])
+        tt(T.T1[:], T.T1[:], T.PPI[:], A.mult, ["T1", "PPI"], ["T1"])
+        tt(T.SED[:, 0::16], T.T1[:], T.T2[:], A.add, ["T1", "T2"], ["SED"])
+        scan(T.SES[:], T.SMb[:], T.SED[:], A.mult, A.add, ["SMb", "SED"], ["SES"])
+        ts(T.SEO[:], T.SES[:], 15.0, None, A.is_equal, None, ["SES"], ["SEO"])
+        for b in range(2):
+            mm(T.pT[:, 128 * b:128 * b + 128], T.SEO[:, 128 * b:128 * b + 128], T.Idb[:], True, True, ["SEO", "Idb"], ["pT"])
+        tt(T.DM[:], T.pT[:, 0:256], T.DIFF[:], A.mult, ["pT", "DIFF"], ["DM"])
+        L, lk = blist(t)
+        tt(T.TR[:].indirect(L), T.Hf[:], T.DM[:], A.add, ["Hf", "DM", lk], ["TR"])
+
+    dma("y", T.CI[:], T.calls[:], [], ["CI"])
+    dma("s", T.RI[:], T.routes[:], [], ["RI"])
+    dma("y", T.LI[:, 0:16], T.routes[0::16, :], [], ["LI0"])
+    dma("s", T.TI[:], T.trunk[:], [], ["TI"])
+    for h in range(2):
+        dma("y", T.F[:, 1024 * h:1024 * h + 1024], T.paths[:, 1024 * h:1024 * h + 1024], [], [FK[h]])
+    for t in range(1, RO):
+        dma("s", T.LI[:, 16 * t:16 * t + 16], T.routes[t::16, :], [], ["LI%d" % t])
+    iota("iOF", [[1, 16], [16, 16]])
+    iota("iA", [[0, 1]], 0, 1)
+    iota("iG16", [[1, 8], [0, 16]])
+    iota("iX", [[1, 144]])
+    iota("iG8", [[0, 16], [1, 8]])
+    iota("i16t", [[1, 16]])
+    iota("iS", [[0, 16], [1, 16]])
+    iota("iWT", [[-64, 16], [0, 8]], 976)
+    iota("iFI", [[16, 64]])
+    iota("IREV", [[-1, 128]], 127)
+    iota("FS", [[0, 2048]], 0, 0, FSK)
+    fill(T.S0[:], 0.0, "S0")
+    cp(T.OFFS[:], T.iOF[:], ["iOF"], ["OFFS"])
+    ts(T.CC[:, 0:1], T.iA[:], 15, None, A.bitwise_and, None, ["iA"], ["CC0"])
+    ts(T.CC[:, 1:2], T.iA[:], 4, None, A.logical_shift_right, None, ["iA"], ["CC1"])
+    ts(T.CC[:, 2:3], T.iA[:], 4, 1, A.logical_shift_right, A.bitwise_and, ["iA"], ["CC2"])
+    cp(T.CC[:, 3:4], T.iA[:], ["iA"], ["CC3"])
+    ts(T.CC[:, 4:5], T.iA[:], 112, None, A.bitwise_and, None, ["iA"], ["CC4"])
+    cp(T.CCf[:, 0:5], T.CC[:, 0:5], ["CC%d" % i for i in range(5)], ["CCf"])
+    kc, gc, par, pc, g16 = [T.CCf[:, i:i + 1] for i in range(5)]
+    ts(T.BP[:], kc, -1.0, -8 * LK + 2047 * 32 + 15, A.mult, A.add, ["CCf"], ["BP"])
+    ts(T.BO[:], T.iG16[:], gc, None, A.is_equal, None, ["iG16", "CCf"], ["BO"])
+    cp(own[:, PCF:PCF + 16], T.CI[:], ["CI"], ["OC"])
+    ts(T.TH[:], T.CI[:], 3584, None, A.bitwise_and, None, ["CI"], ["TH"])
+    cp(own[:, PTF:PTF + 16], T.TH[:], ["TH"], ["OT"])
+
+    def load_s0(r):
+        dma("y", T.S0[0::16, 0:256], PKb[r][:, PCF:PCF + 16], ["OC" if r == q else pk[r]], ["S0"])
+        dma("y", T.S0[0::16, 256:512], PKb[r][:, PTF:PTF + 16], ["OT" if r == q else pk[r]], ["S0"])
+
+    def load_sr():
+        mm(T.pR[:, 0:512], T.BO[:], T.S0[:], True, False, ["BO", "S0"], ["pR"])
+
+    def none_s(tab, keys):
+        act(T.NI[:, 1024:2048], tab[:, 1024:2048].indirect(T.OFI[:]), keys + ["OFI", "MB"], ["NI1"], func=AF.Relu, bias=T.MB[:, 0:1])
+
+    def none_v(tab, keys):
+        ts(T.NI[:, 0:1024], tab[:, 0:1024], float(NONE), None, A.is_equal, None, keys, ["NI0"])
+
+    load_s0(q)
+    for t in range(RO):
+        dma("y", T.FS[t::16, :], T.paths[t::16, :], [], ["FS%d" % t])
+    cp(own[:, PR:PR + 256], T.RI[:], ["RI"], ["OR"])
+    expand(0, 0, 1)
+    ts(UL(q, 80), T.LI[:, 0:16], -q * G, None, A.add, None, ["LI0"], ["ULa"])
+    cp(T.TR[:], T.TI[:], ["TI"], ["TR"])
+    hold_v(0)
+    hold_s(0)
+    expand(0, 3)
+    ts(T.IND[:], T.iG8[:], gc, None, A.is_equal, None, ["iG8", "CCf"], ["IND"])
+    ts(T.XB[:, 16:32], T.CI[:], par, None, A.mult, None, ["CI", "CCf"], ["XBo"])
+    tt(T.XB[:, 0:16], own[:, PCF:PCF + 16], T.XB[:, 16:32], A.subtract, ["OC", "XBo"], ["XBe"])
+    op("v", lambda: V.transpose(T.XT[:], T.XB[:]), ["XBo", "XBe"], ["XT"])
+    for t in (1, 2, 3):
+        ts(own[:, PL + 16 * t - 16:PL + 16 * t], T.LI[:, 16 * t:16 * t + 16], -((q + t) % N * G), None, A.add, None, ["LI%d" % t], ["OL%d" % t])
+    tt(own[:, PSL:PSL + 16], T.XT[:, 0:16], T.XT[:, 16:32], A.add, ["XT"], ["OS"])
+    for b in range(2):
+        mm(T.pM[:, 8 * b:8 * b + 8], T.S0[:, 128 * b:128 * b + 128], T.IND[:, 0:8], True, True, ["S0", "IND"], ["pM"])
+    load_sr()
+    ts(T.Idf[:], T.iX[:, 0:128], pc, None, A.is_equal, None, ["iX", "CCf"], ["Idf"])
+    ts(T.Idb[:], T.iX[:, 0:128], pc, None, A.is_equal, None, ["iX", "CCf"], ["Idb"])
+    ts(T.Idm[:], T.Idf[:], -1.0, None, A.mult, None, ["Idf"], ["Idm"])
+    fill(T.MB[:, 1:2], -0.5, "MB1")
+    ts(own[:, PSK:PSK + 16], T.pM[:, 0:16], -32.0, 2047.0 * 32 + 16, A.mult, A.add, ["pM"], [pk[q]])
+    send(own[:], [pk[q], "OC", "OT", "OR", "OS", "OL1", "OL2", "OL3"], "set%d" % q, "lset")
+    ts(T.CCf[:, 5:6], g16, 15.0, None, A.add, None, ["CCf"], ["CCf5"])
+    ts(T.Z[:], T.iX[:], T.CCf[:, 5:6], None, A.is_equal, None, ["iX", "CCf5"], ["Z"])
+    ts(T.MK[:], T.i16t[:], kc, None, A.is_equal, None, ["i16t", "CCf"], ["MK"])
+    ts(T.Idn[:], T.Idb[:], 9.0 * LK, None, A.mult, None, ["Idb"], ["Idn"])
+    tt(T.BW[:], T.IND[:], T.iWT[:], A.mult, ["IND", "iWT"], ["BW"])
+    ts(T.BL[:], T.IND[:, 0:8], LK, None, A.mult, None, ["IND"], ["BL"])
+    ts(T.BD[:], T.IND[:, 0:8], OUT, None, A.mult, None, ["IND"], ["BD"])
+    ts(T.SM0[:], T.iS[:], 1.0, None, A.min, None, ["iS"], ["SM0"])
+    ts(T.SMb[:], T.iS[:], 1.0, None, A.min, None, ["iS"], ["SMb"])
+    fill(T.LOD[:], -1.0, "LOD")
+    fill(T.SED[:], 1.0, "SED")
+    fill(T.MB[:, 0:1], -2047.0, "MB")
+    ts(T.OFI[:], T.iFI[:], kc, None, A.add, None, ["iFI", "CCf"], ["OFI"])
+    none_s(T.F, ["Fb"])
+    hold_d(0)
+    expand(0, 2)
+    ts(UL(q, 96), T.LI[:, 64:80], -q * G, None, A.add, None, ["LI4"], ["ULb"])
+    set_list(q)
+    ts(T.Z0[:], T.Z[:], T.MK[:, 0:1], None, A.mult, None, ["Z", "MK"], ["Z0"])
+
+    none_v(T.F, ["Fa"])
+    for l in range(16):
+        mm(T.pY[:, 0:128], T.Z[:, l:l + 128], T.NI[:, 128 * l:128 * l + 128], l == 0, l == 15, ["Z", "NI%d" % (l // 8)], ["pY"])
+    like(0, range(PRE))
+    ts(T.Yf[:], T.pY[:, 0:128], 16.0, None, A.is_ge, None, ["pY"], ["Yf"])
+    build_w()
+    dead_pass(0, "s")
+    like(0, range(PRE, 3))
+    dead_pass(0, "v")
+    for t in range(RO):
+        if t < 4:
+            load_s0((q - t - 1) % N)
+        dead_t(t)
+        candidates(t)
+        if t > 0:
+            dma("y", T.F[t::16, :], T.FS[t::16, :], ["FS%d" % t], FK)
+        decide(t)
+        if t == 4:
+            break
+        load_sr()
+        if t == 0:
+            set_list(others[2])
+        hold_v(t + 1)
+        hold_s(t + 1)
+        if t < 3:
+            expand(t + 1, 3)
+        hold_d(t + 1)
+        if t < 3:
+            expand(t + 1, 2)
+        if t == 0:
+            cp(T.FS[:].indirect(UL(q, 0)), own[:, PR:PR + 256], [ul[q], "OR"], FSK)
+            for r in [others[2], others[1], others[0]]:
+                if r != others[2]:
+                    set_list(r)
+                cp(T.FS[:].indirect(UL(r, 0)), PKb[r][:, PR:PR + 256], [ul[r], pk[r]], FSK)
+            dma("y", T.F[0::16, :], T.FS[0::16, :], ["FS0"], FK)
+            none_s(T.FS, FSK)
+            none_v(T.FS, FSK)
+            mm(T.pY[:, 0:128], T.Idb[:], T.Yf[:], True, False, ["Idb", "Yf"], ["pY"])
+            for l in range(16):
+                mm(T.pY[:, 0:128], T.Z0[:, l:l + 128], T.NI[:, 128 * l:128 * l + 128], False, l == 15, ["Z0", "NI%d" % (l // 8)], ["pY"])
+            ts(T.Yf[:], T.pY[:, 0:128], 2.0, None, A.is_ge, None, ["pY"], ["Yf"])
+            kills_t(1)
+        else:
+            kills_t(t + 1)
+            like(t + 1, range(PRE))
+        kills_v()
+        build_w()
+        dead_pass(t + 1, "s")
+        like(t + 1, range(3) if t == 0 else range(PRE, 3))
+        dead_pass(t + 1, "v")
+    dma("y", T.yt[:], T.TR[:], ["TR"], ["yt"])
+    for l in range(4):
+        m = 15 - 4 * q - l
+        ts(T.BS[:, 128 * l:128 * l + 128], T.BO[:], T.MK[:, m:m + 1], float(NONE), A.mult, A.mult, ["BO", "MK"], ["BS"])
+    kills_t(RO)
+    kills_v()
+    for l in range(4):
+        mm(T.pM[:, 128 * l:128 * l + 128], T.BS[:, 128 * l:128 * l + 128], T.Yf[:], True, True, ["BS", "Yf"], ["pM"])
+    tt(T.YO[:], T.pM[:, 0:512], T.F[:, G * q:G * q + G], A.max, ["pM"] + FK, ["YO"])
+    dma("y", T.yp[:], T.YO[:], ["YO"], ["yp"])
+    need("g", [(s, v) for s, v in total.items()])

@@ -3,17 +3,20 @@ from concourse.mybir import AluOpType as A, ActivationFunctionType as AF
 
 N, G, C, K, RO = 4, 512, 2048, 256, 5
 NONE = N * G
-f32, b16, i32, u16 = "float32", "bfloat16", "int32", "uint16"
-PR, PSK, PTF, PCF, PSL, PL, PW = 0, 256, 272, 288, 304, 320, 368
+f32, f16, b16, i32, u16 = "float32", "float16", "bfloat16", "int32", "uint16"
 LK = 65536.0
-OUT = 6400.0
-PIECES = [(0, 0, 128, "s"), (1, 0, 64, "s"), (1, 64, 96, "s"), (1, 96, 128, "v")]
-DORD = [0, 3, 1, 2]
-LIKE = [(0, 0, 128, True, True), (1, 96, 128, True, False), (1, 0, 96, False, True)]
-PRE = 2
-WS = 5
-FK = ["Fa", "Fb"]
-FSK = ["FS%d" % t for t in range(RO)]
+W1, W2 = 176, 384
+LCH = [4, 4, 4, 2, 1, 1]
+DCH = [4, 4, 4, 2, 2, 1]
+LCH0 = [1, 1, 2, 4, 4, 2, 1, 1]
+DOFF = 5.0
+KAT = 1
+EAT = 12
+HAT = 4
+OH0 = 16
+VD = 0
+FS = 4
+HAV = False
 
 
 def sb(names, cols, dtype):
@@ -21,18 +24,21 @@ def sb(names, cols, dtype):
 
 
 SCRATCH = {
-    **sb("iA", 1, i32), **sb("BP", 1, f32), **sb("MB", 2, f32), **sb("CC", 8, i32), **sb("CCf", 8, f32),
-    **sb("iX", 144, f32), **sb("Z Z0", 144, b16), **sb("iG16 iG8 iWT Idf Idm BO IND", 128, f32), **sb("IREV Idb Idn BW Yf", 128, b16),
-    **sb("i16t MK T1 HIF", 16, f32), **sb("CI TH BI HI LOI PPI T2", 16, i32), **sb("BL BD", 8, b16),
-    **sb("iS SM0 Hf KH DIFF DM SC1 SD", 256, f32), **sb("iOF RI", 256, i32), **sb("OFFS H16", 256, u16),
-    **sb("SMb ELIG Gs LOD SED LOS LOO SES SEO", 256, b16), **sb("iFI", 64, f32), **sb("OFI", 64, u16),
-    **sb("LI", 80, i32), **sb("TI", 512, i32), **sb("XB XT", 32, f32), **sb("TR S0 YO", 512, f32), **sb("BS", 512, b16),
-    **sb("F FS", 2048, i32), **sb("NI W OH", 2048, b16), **sb("E Gd", 4096, b16), **sb("RB0 RB1", 4096, f32),
-    **sb("PK0 PK1 PK2 PK3", PW, f32), **sb("UL", 4 * 112, u16), **sb("KS", RO * N * 128, b16),
-    **{n: ("psum", [128, 512], f32) for n in "pK pD pX pY pT pR pM".split()},
+    **sb("iA", 1, i32), **sb("CC", 12, i32), **sb("CF", 32, f32), **sb("iB", 4, f32), **sb("OFS", 28, u16),
+    **sb("iX", 144, b16), **sb("SelR ONE", 192, f16), **sb("Zq", 48, f16), **sb("ST SD", 144, f16),
+    **sb("Id16 Idm NK", 128, f16), **sb("Idb Idn TO Yf YfB BIG", 128, b16), **sb("KS", 32, b16), **sb("ZD", 512, b16),
+    **sb("SM0 Hb DIFF DM SC1", 256, f32), **sb("iC iCa MKa MKb", 256, b16), **sb("BOw CMa CMb Ha Hc", 256, f16),
+    **sb("ZER CKf BND BN0 ELIG LO SEO LOO", 256, b16), **sb("SMb LOS", 512, b16), **sb("LOD", 768, b16), **sb("OT", 512, f16),
+    **sb("CQ SK NF", 16, f32), **sb("SH", 48, f32), **sb("NI32 BD BI", 16, i32), **sb("XI", 48, i32), **sb("REP", 16, u16),
+    **sb("BL", 8, b16), **sb("IND", 8, f16), **sb("R", 1024, f32),
+    **sb("IN", 352, i32), **sb("TI", 608, i32), **sb("TS", 608, f16), **sb("FB", 512, i32), **sb("FB16 NI YD TR16", 512, f16),
+    **sb("X1", N * W1, f16), **sb("X2", N * W2, f16),
+    **sb("UL", 160, u16), **sb("O16", 272, u16), **sb("TR OY OP RY RP", 512, f32),
+    **sb("F DS", 2048, f32), **sb("SelF", 512, f16), **sb("W OH", 2048, b16), **sb("E", 4096, b16), **sb("Gd", 4352, b16),
+    **sb("Ta Tb", 32, f32), **sb("GM", 8, f32), **sb("D16", 2048, f16), "TT": ("sbuf", [128, 8, 32], b16),
+    **{n: ("psum", [128, 512], f32) for n in "pK pV pX pY pO pT pR pM".split()},
 }
-SEMAPHORES = (["cv", "cs", "ct", "cg", "lset"] + ["set%d" % r for r in range(N)] + ["kill%d" % t for t in range(RO)]
-              + ["lk%d" % t for t in range(RO)] + ["d%d" % i for i in range(36)])
+SEMAPHORES = ["cv", "cs", "ct", "cg", "ra", "rb", "ry", "rp", "la", "lb", "ly", "lp"] + ["d%d" % i for i in range(56)]
 
 
 def rank_program(g, core, T, topo):
@@ -56,6 +62,7 @@ def rank_program(g, core, T, topo):
             res[r] = rest[n * k:(n + 1) * k]
         return res
     plans = [plan(r) for r in range(N)]
+    landing = sum(len(plans[r][q]) for r in others)
 
     queue = {"v": g.vector, "s": g.scalar, "t": g.tensor, "g": g, "y": g.sync}
     cnt, waited, lastw, readers, total, nd = {}, {}, {}, {}, {}, [0]
@@ -106,22 +113,20 @@ def rank_program(g, core, T, topo):
         total[s] = 16
         record((qn, s, 16, True), reads, writes)
 
-    def arrive(key, s, v):
-        lastw[key] = [("remote", s, v, True)]
-        readers[key] = []
-        total[s] = v
-
-    def send(ap, reads, rsem, lsem):
+    def send(src, dst, reads, lands, rsem, lsem):
         need("g", hazards("g", reads, []))
         tr = []
         for r in others:
             rid, pid = topo.addr(T.cores[r], core)
             tr.append(RemoteDMATransfer(dst_ids=[DstId(rid=rid, pnc=pid)], dma_engine_mask=sum(1 << e for e in plans[q][r]),
-                                        remote_sem=T.sem[rsem], src=ap, dst=ap))
+                                        remote_sem=T.sem[rsem], src=src(r), dst=dst(r)))
         g.remote_dma_fused(tr, local_sem=T.sem[lsem])
         total[lsem] = sum(len(plans[q][r]) for r in others)
         for k in reads:
             readers.setdefault(k, []).append(("g", lsem, total[lsem], True))
+        lastw[lands] = [("remote", rsem, landing, True)]
+        readers[lands] = []
+        total[rsem] = landing
 
     V, S, E_ = g.vector, g.scalar, g.tensor
 
@@ -137,8 +142,8 @@ def rank_program(g, core, T, topo):
     def cp(o, i, reads, writes):
         op("v", lambda: V.tensor_copy(o, i), reads, writes)
 
-    def fill(o, c, w):
-        op("v", lambda: V.memset(o, c), [], [w])
+    def fill(o, c, *w):
+        op("v", lambda: V.memset(o, c), [], list(w))
 
     def act(o, i, reads, writes, func=AF.Copy, **kw):
         op("s", lambda: S.activation(o, i, func, **kw), reads, writes)
@@ -149,309 +154,409 @@ def rank_program(g, core, T, topo):
     def scan(o, d0, d1, a, b, reads, writes):
         op("v", lambda: V.tensor_tensor_scan(o, d0, d1, 0.0, a, b), reads, writes)
 
-    def iota(n, pat, base=0, cm=0, keys=None):
+    def iota(n, pat, base=0, cm=0):
         o = T[n]
-        if o.dtype == T.iA.dtype:
-            op("g", lambda: g.iota(o[:], pat, base, cm), [], keys or [n])
+        if n == "iA":
+            op("g", lambda: g.iota(o[:], pat, base, cm), [], [n])
         else:
-            op("g", lambda: g.iota(o[:], pat, base, cm, allow_small_or_imprecise_dtypes=True), [], keys or [n])
+            op("g", lambda: g.iota(o[:], pat, base, cm, allow_small_or_imprecise_dtypes=True), [], [n])
 
-    PKb = [T["PK%d" % r] for r in range(N)]
-    own = PKb[q]
-    pk = ["PK%d" % r for r in range(N)]
-    ul = ["UL%d" % r for r in range(N)]
-    for r in others:
-        arrive(pk[r], "set%d" % r, len(plans[r][q]))
+    def pick(o, i, pat, base, reads, writes):
+        op("g", lambda: g.affine_select(o, i, pat, A.is_equal, 0.0, base, -1), reads, writes)
 
-    def UL(r, a):
-        return T.UL[:, 112 * r + a:112 * r + a + 16]
+    TAT, CAT = {1: 0, 2: 176, 3: 304, 0: 480}, {1: 128, 2: 128, 3: 432, 0: 128}
 
-    def set_list(r):
-        cp(T.UL[:, 112 * r:112 * r + 80], PKb[r][:, PCF:PW], [pk[r]] if r != q else ["OC", "OS", "OL1", "OL2", "OL3"], [ul[r]])
+    def first(r, part, a, b):
+        d = (q - r) % N
+        at = (TAT, CAT)[part][d]
+        if d == 0:
+            return T.TS[:, at + a:at + b], ["TS0", "TC"][part]
+        at += W1 * r - min(TAT[d], CAT[d])
+        return T.X1[:, at + a:at + b], "X1"
 
-    rbuf = {0: "RB0", 1: "RB1", 2: "RB1", 3: "RB1", 4: "RB0"}
+    def second(r, a, b):
+        return T.X2[:, W2 * r + a:W2 * r + b], "XR" if r == q else "X2"
 
-    def expand(t, *parts):
-        r = (q - t) % N
-        for i in parts:
-            act(T[rbuf[t]][:, 1024 * i:1024 * i + 1024], PKb[r][:, PR:PR + 256].indirect(T.OFFS[:, 64 * i:64 * i + 64]),
-                ["OR" if r == q else pk[r], "OFFS"], ["%s%d" % (rbuf[t], i)])
+    def ul(t, order):
+        a = 32 * t + 16 * order
+        return T.UL[:, a:a + 16], "UL%d" % (t > 0)
 
-    def blist(t):
-        if t == 0:
-            return UL(q, 80), "ULa"
-        if t == 4:
-            return UL(q, 96), "ULb"
-        r = (q - t) % N
-        return UL(r, 16 + 16 * t), ul[r]
+    for d in (1, 2, 3):
+        r = (q + d) % N
+        dma("ysy"[d - 1], T.TI[:, TAT[d]:TAT[d] + 128], T.trunk[32 * r:32 * r + 32, :], [], ["TI%d" % d])
+    dma("s", T.IN[:, 336:352], T.calls[:], [], ["IC"])
+    for t in range(RO):
+        a = 256 + 16 * ((t - 1) % RO)
+        dma("sysys"[t], T.IN[:, a:a + 16], T.routes[t::16, :], [], ["IL%d" % t])
+    dma("y", T.IN[:, 0:256], T.routes[:], [], ["IR"])
+    INK = ["IR"] + ["IL%d" % n for n in range(1, RO)]
+    dma("s", T.TI[:, TAT[0]:TAT[0] + 128], T.trunk[32 * q:32 * q + 32, :], [], ["TI0"])
+    for x in range(N):
+        dma("y", T.FB[:, 128 * x:128 * x + 128], T.paths[32 * q:32 * q + 32, G * x:G * x + G], [], ["FB%d" % x])
+    FK = ["F%d" % n for n in range(N)]
+    WK = ["W%d" % x for x in range(N)]
 
-    def hold_v(t):
-        L, lk = blist(t)
-        cp(T.H16[:], T.TR[:].indirect(L), ["TR", lk], ["H16"])
+    iota("iA", [[0, 1]], 0, 1)
+    iota("iB", [[16, 4]], 256)
+    iota("iX", [[1, 144]])
+    iota("iC", [[1, 16], [0, 16]])
+    iota("CKf", [[0, 16], [-1, 16]], -17)
+    iota("ONE", [[0, 192]], 1)
+    for y in range(4):
+        pick(T.SelF[:, 128 * y:128 * y + 128], T.ONE[:, 0:128], [[64, 2], [0, 4], [4, 16]], y, ["ONE"], ["SelF%d" % y])
+    bits = [(0, 15), (0, 3), (2, 3), (0, 127), (5, 3), (6, 1), (4, 3), (4, 7)]
+    names = "k y z pc o n6 hh gg".split()
+    col = {n: T.CF[:, i:i + 1] for i, n in enumerate(names + "sw k16 o512 gp tZ eb m17 u v".split())}
 
-    def hold_s(t):
-        L, lk = blist(t)
-        act(T.Hf[:], T.TR[:].indirect(L), ["TR", lk], ["Hf"])
-        act(T.KH[:], T.TR[:].indirect(L), ["TR", lk, "BP"], ["KH"], func=AF.Identity, bias=T.BP[:], scale=-32.0)
+    def parts(a, b):
+        for i in range(a, b):
+            ts(T.CC[:, i:i + 1], T.iA[:], bits[i][0], bits[i][1], A.logical_shift_right, A.bitwise_and, ["iA"], ["CC%d" % i])
+        cp(T.CF[:, a:b], T.CC[:, a:b], ["CC%d" % i for i in range(a, b)], ["c_" + n for n in names[a:b]])
 
-    def hold_d(t):
-        for h in range(2):
-            mm(T.pR[:, 256 * h:256 * h + 256], T.Idm[:], T.Hf[:], False, h == 1, ["Idm", "Hf"], ["pR"])
-        act(T.ELIG[:], T.pR[:, 256:512], ["pR", "MB1"], ["ELIG"], func=AF.Sign, bias=T.MB[:, 1:2])
+    def num(o, i, s1, s2, a, b):
+        rd = ["c_" + x for x in (i, s1, s2) if isinstance(x, str)]
+        ts(col[o], col[i], col.get(s1, s1), col.get(s2, s2), a, b, rd, ["c_" + o])
+
+    parts(0, 4)
+    num("sw", "y", 4.0, "z", A.mult, A.add)
+    num("k16", "k", 16.0, None, A.mult, None)
+    ts(T.OFS[:, 0:1], col["k"], 16.0, None, A.add, None, ["c_k"], ["OFc"])
+    cp(T.OFS[:, 1:2], col["sw"], ["c_sw"], ["OFd"])
+    cp(T.OFS[:, 2:3], col["k"], ["c_k"], ["OFe"])
+    ts(T.OFS[:, 12:28], T.iX[:, 0:16], col["k16"], None, A.add, None, ["iX", "c_k16"], ["OFR"])
+    ts(T.OFS[:, 4:12:2], T.iB[:], col["sw"], None, A.add, None, ["iB", "c_sw"], ["OFa"])
+    ts(T.OFS[:, 5:12:2], T.iB[:], col["k"], None, A.add, None, ["iB", "c_k"], ["OFb"])
+    ts(T.Id16[:], T.iX[:, 0:128], col["pc"], None, A.is_equal, None, ["iX", "c_pc"], ["Id16"])
+
+    def turn_table(t):
+        for r in range(N):
+            o = (r + t) % N
+            act(T.OT[:, 128 * t + r:128 * t + 128:4], T.Id16[:, 32 * o:32 * o + 32], ["Id16"], ["OT%d_%d" % (t, r)])
+
+    turn_table(0)
+    act(T.Idb[:], T.Id16[:], ["Id16"], ["Idb"])
+    act(T.NK[:], T.Id16[:], ["Id16"], ["NK"], scale=-32.0)
+    parts(4, 8)
+    num("o512", "o", 512.0, None, A.mult, None)
+    num("gp", "hh", 2.0, "n6", A.mult, A.add)
+    num("tZ", "n6", 16.0, "y", A.mult, A.add)
+    fill(T.W[:, 0:1024], 0.0, "Wa")
+    cp(T.TS[:, 0:128], T.TI[:, 0:128], ["TI1"], ["TS1"])
+    for d in (1, 3):
+        cp(T.TS[:, CAT[d]:CAT[d] + 48], T.IN[:, 320:352].indirect(T.OFS[:, 0:3]), ["IC", "IL0", "OFc", "OFd", "OFe"], ["TC" if d == 1 else "TC3"])
+    cp(T.TS[:, 176:432], T.TI[:, 176:432], ["TI2", "TI3"], ["TS2"])
+    send(lambda r: T.TS[:, min(TAT[(r - q) % N], CAT[(r - q) % N]):min(TAT[(r - q) % N], CAT[(r - q) % N]) + W1],
+         lambda r: T.X1[:, W1 * q:W1 * q + W1], ["TS1", "TS2", "TC", "TC3"], "X1", "ra", "la")
+    act(second(q, 0, W2)[0], T.IN[:, 0:320].indirect(T.OFS[:, 4:28]), INK + ["OFR", "OFa", "OFb"], ["XR"])
+    send(lambda r: second(q, 0, W2)[0], lambda r: second(q, 0, W2)[0], ["XR"], "X2", "rb", "lb")
+    iota("iCa", [[1, 4], [4, 4], [0, 16]])
+    pick(T.SelR[:], T.ONE[:], [[16, 3], [-200, 4], [1, 16]], 32 * q + 600, ["ONE"], ["SelR"])
+    iota("DS", [[0, 2048]])
+    iota("BIG", [[0, 128]], 4096)
+    for x in range(N):
+        pick(T.ZD[0:32, 128 * x:128 * x + 128], T.BIG[0:32, :], [[16, 2], [0, 16], [1, 4]], 4 * x, ["BIG"], ["ZD%d" % x])
+    for o in range(N):
+        pick(T.ST[32 * o:32 * o + 32, :], T.ONE[32 * o:32 * o + 32, 0:144], [[1, 36], [100, 4]], -300, ["ONE"], ["ST%d" % o])
+
+    fill(T.W[:, 1024:2048], 0.0, *WK)
+    cp(T.TS[:, 480:608], T.TI[:, 480:608], ["TI0"], ["TS0"])
+    act(T.Idm[:], T.Id16[:], ["Id16"], ["Idm"], scale=-1.0)
+    act(T.Idn[:], T.Id16[:], ["Id16"], ["Idn"], scale=9.0 * LK)
+    fill(col["m17"], -17.0, "c_m17")
+    act(T.SM0[:], T.CKf[:], ["CKf", "c_m17"], ["SM0"], func=AF.Sign, scale=-1.0, bias=col["m17"])
+    for h in range(2):
+        act(T.SMb[:, 256 * h:256 * h + 256], T.SM0[:], ["SM0"], ["SMb%d" % h])
+    act(T.ZER[:], T.CKf[:], ["CKf"], ["ZER"], scale=0.0)
+    act(T.BN0[:], T.CKf[:], ["CKf"], ["BN0"], scale=0.0)
+    ts(T.Zq[:], T.iX[:, 0:48], -12.0, col["tZ"], A.add, A.is_equal, ["iX", "c_tZ"], ["Zq"])
+    ts(T.IND[:], T.iX[:, 0:8], col["gg"], None, A.is_equal, None, ["iX", "c_gg"], ["IND"])
+    ts(T.GM[:], T.iX[:, 0:8], col["gp"], None, A.is_equal, None, ["iX", "c_gp"], ["GM"])
+    ts(T.Ta[:], T.iX[:, 0:32], 15.0, -32.0 + 1.0 / 128, A.is_gt, A.mult, ["iX"], ["Ta"])
+    ts(T.Tb[:], T.iX[:, 0:32], 15.0, 0.5 + 1.0 / 128, A.is_equal, A.mult, ["iX"], ["Tb"])
+    ts(T.REP[:], T.iX[:, 0:16], 0.0, col["k"], A.mult, A.add, ["iX", "c_k"], ["REP"])
+    tt(T.Ta[:], T.Ta[:], T.Tb[:], A.add, ["Ta", "Tb"], ["Ta"])
+    ts(T.MKb[:], T.iC[:], col["k"], None, A.is_equal, None, ["iC", "c_k"], ["MKb"])
+    ts(T.Ta[:], T.Ta[:], -1.0 / 128, None, A.add, None, ["Ta"], ["Ta"])
+    for n in range(8):
+        act(T.TT[:, n, :], T.Ta[:], ["Ta", "GM"], ["TT%d" % n], scale=T.GM[:, n:n + 1])
+    TTK = ["TT%d" % n for n in range(8)]
+    act(T.BL[:], T.GM[:], ["GM"], ["BL"], scale=LK)
+    fill(T.CF[:, 30:31], -15.0, "c_m15")
+    cp(T.FB16[:], T.FB[:], ["FB%d" % x for x in range(N)], ["FB16"])
+    ts(T.NI[:], T.FB16[:], float(NONE), None, A.is_equal, None, ["FB16"], ["NI"])
+
+    def none_sums(last):
+        for x in range(N):
+            mm(T.pY[0:32, 0:128], T.Zq[:, 12 - 4 * x:44 - 4 * x], T.NI[:, 128 * x:128 * x + 128], x == 0, last and x == N - 1, ["Zq", "NI"], ["pY"])
+
+    def spread_flags():
+        for x in range(N):
+            dma("y", T.W[16 * x::64, :], T.Yf[0:32, :], ["Yf", "Wa"], [WK[x]])
+
+    for x, bank in enumerate(["pK", "pV", "pX", "pM"]):
+        for y in range(4):
+            mm(T[bank][:, 128 * y:128 * y + 128], T.SelF[:, 128 * y:128 * y + 128], T.FB16[:, 128 * x:128 * x + 128], True, True,
+               ["SelF%d" % y, "FB16"], [bank])
+        if x == 0:
+            none_sums(True)
+        if x == 1:
+            act(T.Yf[0:32, :], T.pY[0:32, 0:128], ["pY", "c_m15"], ["Yf"], func=AF.Relu, bias=T.CF[0:32, 30:31])
+            spread_flags()
+        (act if x < FS else cp)(T.F[:, G * x:G * x + G], T[bank][:], [bank], [FK[x]])
+    ts(T.MKa[:], T.iCa[:], col["k"], None, A.is_equal, None, ["iCa", "c_k"], ["MKa"])
+    ts(T.BOw[:, 0:128], T.iC[:, 0:128], col["gg"], None, A.is_equal, None, ["iC", "c_gg"], ["BOw0"])
+    act(T.BOw[:, 128:256], T.BOw[:, 0:128], ["BOw0"], ["BOw1"])
+    ts(T.TO[:], T.iC[:, 0:128], col["gp"], -64.0, A.is_equal, A.mult, ["iC", "c_gp"], ["TO"])
+    fill(T.LOD[:], -1.0, "LOD")
+    fill(T.SH[:, 16:32], 15.0, "SH1")
+    fill(T.SH[:, 32:48], 127.0, "SH2")
+    fill(col["eb"], 9 * LK - 16384 - 16, "c_eb")
+    num("u", "n6", 16.0, "k", A.mult, A.add)
+    num("v", "k", float(RO), None, A.is_lt, None)
+    num("u", "u", 4.0, 4.0, A.mult, A.add)
+    num("u", "u", "v", -1.0, A.mult, A.add)
+    ts(T.SD[:], T.iX[:], col["u"], None, A.is_equal, None, ["iX", "c_u"], ["SD"])
+
+    mine = T.Id16[:, 32 * q:32 * q + 32]
+    for r in [q] + others:
+        src, key = first(r, 1, 0, 48)
+        mm(T.pO[32 * r:32 * r + 32, 0:48], mine, src, True, True, ["Id16", key], ["pO"])
+    for o in [q] + others:
+        src, key = first(o, 0, 0, 128)
+        for x in range(4):
+            mm(T.pT[32 * o:32 * o + 32, 128 * x:128 * x + 128], T.Id16[:, x::4], src, True, True, ["Id16", key], ["pT"])
+    ts(T.UL[:, 0:32], T.pO[:, 16:48], col["o512"], None, A.subtract, None, ["pO", "c_o512"], ["UL0"])
+    cp(T.CQ[:], T.pO[:, 0:16], ["pO"], ["CQ"])
+
+    def routes():
+        for r in [q] + others:
+            for h in range(4):
+                src, key = second(r, 128 + 64 * h, 192 + 64 * h)
+                mm(T.pR[:, 64 * r:64 * r + 64], T.SelR[:, 48 - 16 * h:176 - 16 * h], src, h == 0, h == 3, ["SelR", key], ["pR"])
+        for n in range(4):
+            act(T.R[:, 256 * n:256 * n + 256], T.pR[:, 0:256], ["pR"], ["R%d" % n])
+
+    def hold_a(t):
+        L, lk = ul(t, 0)
+        (cp if HAV else act)(T.Ha[:], T.TR[:].indirect(L), ["TR", lk], ["Ha"])
+        for n in range(2):
+            for jb in range(4):
+                a = 128 * (t % N) + 64 * n
+                mm(T.pO[64 * n:64 * n + 64, jb:256:4], T.Ha[:, 64 * jb:64 * jb + 64], T.OT[:, a:a + 64], True, True,
+                   ["Ha"] + ["OT%d_%d" % (t % N, r) for r in range(N)], ["pO"])
+
+    def lists():
+        cp(T.O16[:, 0:256], T.pO[:, 0:256], ["pO"], ["O16"])
+
+    def hold_b(t):
+        L, lk = ul(t, 1)
+        act(T.Hb[:], T.TR[:].indirect(L), ["TR", lk], ["Hb"])
+        act(T.Hc[:], T.Hb[:], ["Hb"], ["Hc"])
+
+    def pieces(t):
+        for r in range(N):
+            o = (r + t) % N
+            for h in range(4):
+                yield 64 * (r % 2), 128 * (r // 2) + 32 * h, 32 * o, 64 * h
+
+    def keys(t):
+        mm(T.pR[:, 256:512], T.Idb[:], T.BND[:], True, False, ["Idb", "BND"], ["pR"])
+        for n, (a, b, c, d) in enumerate(pieces(t)):
+            mm(T.pR[a:a + 64, 256 + b:288 + b], T.Hc[:, d:d + 64], T.NK[:, c:c + 32], False, n in (11, 15), ["Hc", "NK"], ["pR"])
+        a = 32 * (N - t % N)
+        mm(T.pR[:, 0:256], T.BOw[:, a:a + 128], T.CMb[:], True, False, ["BOw0", "BOw1", "CMb"], ["pR"])
+        mm(T.pR[:, 0:256], T.Idm[:], T.Hc[:], False, True, ["Idm", "Hc"], ["pR"])
+        mm(T.pK[:, 0:256], T.Idb[:], T.BND[:], True, False, ["Idb", "BND"], ["pK"])
+        mm(T.pK[:, 0:256], T.Idb[:], T.CKf[:], False, False, ["Idb", "CKf"], ["pK"])
+        for a, b, c, d in pieces(t):
+            mm(T.pK[a:a + 64, b:b + 32], T.Hc[:, d:d + 64], T.NK[:, c:c + 32], False, False, ["Hc", "NK"], ["pK"])
+        mm(T.pV[:, 0:256], T.Idb[:], T.ZER[:], True, False, ["Idb", "ZER"], ["pV"])
+
+    def keys_s():
+        act(T.ELIG[:], T.pR[:, 256:512], ["pR", "c_eb"], ["ELIG"], func=AF.Sign, bias=col["eb"])
         act(T.DIFF[:], T.pR[:, 0:256], ["pR"], ["DIFF"])
 
-    def like(t, parts):
-        for i in parts:
-            b, j0, j1, first, last = LIKE[i]
-            u, w = 2048 * b + 16 * j0, 2048 * b + 16 * j1
-            tt(T.E[:, u:w], T.F[:].indirect(T.H16[:, 128 * b + j0:128 * b + j1]), T[rbuf[t]][:, u:w], A.is_equal,
-               FK + ["H16"] + ["%s%d" % (rbuf[t], n) for n in range((128 * b + j0) // 64, (128 * b + j1 + 63) // 64)], ["E%d" % i])
-            full = T.pK[:, 128 * b:128 * b + 128]
-            if first:
-                mm(full, T.KH[:, 128 * b:128 * b + 128], T.Idf[:], True, False, ["KH", "Idf"], ["pK"])
-            for p in range(16):
-                mm(T.pK[j0:j1, 128 * b + p:128 * b + 128:16], T.E[:, u + p:w:16], T.BL[:], False, False, ["E%d" % i, "BL"], ["pK"])
-            if last:
-                mm(full, T.ELIG[:, 128 * b:128 * b + 128], T.Idn[:], False, True, ["ELIG", "Idn"], ["pK"])
+    def like_v(a, b):
+        tt(T.E[:, 256 * a:256 * b], T.F[:].indirect(T.O16[:, 16 * a:16 * b]), T.R[:, 0:256 * (b - a)], A.is_equal,
+           FK + ["O16"] + ["R%d" % n for n in range(b - a)], ["E%d" % p for p in range(a, b)])
 
-    WK = ["W%d" % l for l in range(16)]
+    def like_t(p):
+        for b in range(2):
+            mm(T.pK[:, 128 * b + p:128 * b + 128:16], T.E[:, 256 * p + 128 * b:256 * p + 128 * b + 128], T.BL[:], False, p == 15 and b == 1,
+               ["E%d" % p, "BL"], ["pK"])
 
-    def build_w():
-        for l in range(16):
-            o, m = T.W[:, 128 * l:128 * l + 128], T.MK[:, 15 - l:16 - l]
-            if l < WS:
-                act(o, T.Yf[:], ["Yf", "MK"], [WK[l]], scale=m)
-            else:
-                ts(o, T.Yf[:], m, None, A.mult, None, ["Yf", "MK"], [WK[l]])
+    def chunks(sizes, end):
+        res, p = [], 0
+        for n in sizes:
+            e = min(p + n, end)
+            if e > p:
+                res.append((p, e))
+            p = e
+        return res
 
-    def kills_t(t):
-        mm(T.pY[:, 0:128], T.Idb[:], T.Yf[:], True, False, ["Idb", "Yf"], ["pY"])
-        for n, r in enumerate([q] + others):
-            c = ((t - 1) * N + r) * 128
-            mm(T.pY[:, 0:128], T.KS[:, c:c + 128], T.Idb[:], False, n == N - 1, ["KS%d_%d" % (t - 1, r), "Idb"], ["pY"])
+    def dead(qn, a, b):
+        win = T.W[:].indirect(T.O16[:, 16 * a:16 * b])
+        rd, wr = WK + ["O16", "SL"], ["Gd%d" % p for p in range(a, b)]
+        (act if qn == "s" else cp)(T.Gd[:, 256 * a:256 * b], win, rd, wr)
 
-    def kills_v():
-        ts(T.Yf[:], T.pY[:, 0:128], 1.0, None, A.min, None, ["pY"], ["Yf"])
+    def dead_t(p, last):
+        for b in range(2):
+            w = T.TT[:, :, 15 - p:31 - p] if p < 16 else T.TO[:]
+            mm(T.pV[:, 128 * b:128 * b + 128], T.Gd[:, 256 * p + 128 * b:256 * p + 128 * b + 128], w, False, b == 1 and last,
+               ["Gd%d" % p, "TO"] + TTK, ["pV"])
 
-    def dead_pass(t, qn):
-        if t > 0 and qn == "v":
-            r = (q - t) % N
-            cp(T.Gs[:], T.W[:].indirect(UL(r, 16)), WK + [ul[r]], ["Gs"])
-        for i, (b, j0, j1, e) in enumerate(PIECES):
-            if e != qn:
-                continue
-            win = T.W[:].indirect(T.H16[:, 128 * b + j0:128 * b + j1])
-            o = T.Gd[:, 2048 * b + 16 * j0:2048 * b + 16 * j1]
-            if e == "s":
-                act(o, win, WK + ["H16"], ["Gd%d" % i])
-            else:
-                cp(o, win, WK + ["H16"], ["Gd%d" % i])
+    def look_up(t):
+        lc, dc = chunks(LCH if t else LCH0, 16), chunks(DCH, 17 if t else 16)
+        ds, dv = dc[:len(dc) - VD], dc[len(dc) - VD:]
+        for n, c in enumerate(ds):
+            if n == KAT:
+                keys_s()
+            dead("s", *c)
+        for n, c in enumerate(lc):
+            like_v(*c)
+            if t == 0 and n == 2:
+                other_lists_v()
+            if t == 0 and n == HAT:
+                hops_v()
+        for c in dv:
+            dead("v", *c)
+        turns = [(b, 0, a, b) for a, b in lc] + [(b + DOFF, 1, a, b) for a, b in ds] + [(99 + b, 1, a, b) for a, b in dv]
+        turns.sort()
+        end = [x for x in turns if x[1]][-1]
+        for x in turns:
+            if x[2] == EAT and not x[1]:
+                mm(T.pK[:, 0:256], T.Idn[:], T.ELIG[:], False, False, ["Idn", "ELIG"], ["pK"])
+            for p in range(x[2], x[3]):
+                if x[1]:
+                    dead_t(p, x == end and p == x[3] - 1)
+                else:
+                    like_t(p)
 
-    def dead_t(t):
-        for i in DORD:
-            b, j0, j1, e = PIECES[i]
-            for p in range(16):
-                o = T.pD[j0:j1, 128 * b + p:128 * b + 128:16]
-                last = p == 15 and t > 0
-                mm(o, T.Gd[:, 2048 * b + 16 * j0 + p:2048 * b + 16 * j1:16], T.BW[:, 8 * p:8 * p + 8], True, not last, ["Gd%d" % i, "BW"], ["pD"])
-                if last:
-                    mm(o, T.Gs[:, 128 * b + j0:128 * b + j1], T.BD[:], False, True, ["Gs", "BD"], ["pD"])
-
-    def candidates(t):
-        r = (q - t) % N
-        scan(T.SC1[:], T.SM0[:], T.pK[:, 0:256], A.mult, A.max, ["SM0", "pK"], ["SC1"])
-        tt(T.BI[:], T.SC1[:, 15::16], PKb[r][:, PSK:PSK + 16], A.max, ["SC1", pk[r]], ["BI"])
-        ts(T.HI[:], T.BI[:], 5, 127, A.logical_shift_right, A.bitwise_and, ["BI"], ["HI"])
-        ts(T.LOI[:], T.BI[:], 12, 15, A.logical_shift_right, A.bitwise_and, ["BI"], ["LOI"])
-        ts(T.PPI[:], T.BI[:], 31, None, A.bitwise_and, None, ["BI"], ["PPI"])
-        cp(T.HIF[:], T.HI[:], ["HI"], ["HIF"])
-        for c in range(16):
-            ts(T.OH[:, 128 * c:128 * c + 128], T.IREV[:], T.HIF[:, c:c + 1], None, A.is_equal, None, ["IREV", "HIF"], ["OH%d" % c])
+    def onehot(a, b):
+        for c in range(a, b):
+            ts(T.OH[:, 128 * c:128 * c + 128], T.iX[:, 0:128], T.LOD[:, 512 + 16 * c:513 + 16 * c], None, A.is_equal, None, ["iX", "LOD"], ["OH%d" % c])
 
     def decide(t):
-        scan(T.SD[:], T.SM0[:], T.pD[:, 0:256], A.mult, A.max, ["SM0", "pD"], ["SD"])
-        d = T.SD[:, 15::16]
-        tt(T.LOD[:, 0::16], d, T.LOI[:], A.add, ["SD", "LOI"], ["LOD"])
-        scan(T.LOS[:], T.SMb[:], T.LOD[:], A.mult, A.add, ["SMb", "LOD"], ["LOS"])
-        ts(T.LOO[:], T.LOS[:], 0.0, None, A.is_equal, None, ["LOS"], ["LOO"])
-        for gg in range(8):
-            for b in range(2):
-                c = 8 * b + gg
-                mm(T.pX[:, 16 * gg:16 * gg + 16], T.OH[:, 128 * c:128 * c + 128], T.LOO[:, 16 * c:16 * c + 16], b == 0, b == 1, ["OH%d" % c, "LOO"], ["pX"])
-        c = (t * N + q) * 128
-        if t < 3:
-            expand(t + 1, 0)
-        act(T.KS[:, c:c + 128], T.pX[:, 0:128], ["pX"], ["KS%d_%d" % (t, q)])
-        if t < 3:
-            expand(t + 1, 1)
-        send(T.KS[:, c:c + 128], ["KS%d_%d" % (t, q)], "kill%d" % t, "lk%d" % t)
-        n = sum(len(plans[r][q]) for r in others)
-        for r in others:
-            arrive("KS%d_%d" % (t, r), "kill%d" % t, n)
-        ts(T.T1[:], d, 0.0, None, A.is_equal, None, ["SD"], ["T1"])
-        ts(T.T2[:], d, 1.0 / 64, None, A.mult, None, ["SD"], ["T2"])
-        tt(T.T1[:], T.T1[:], T.PPI[:], A.mult, ["T1", "PPI"], ["T1"])
-        tt(T.SED[:, 0::16], T.T1[:], T.T2[:], A.add, ["T1", "T2"], ["SED"])
-        scan(T.SES[:], T.SMb[:], T.SED[:], A.mult, A.add, ["SMb", "SED"], ["SES"])
-        ts(T.SEO[:], T.SES[:], 15.0, None, A.is_equal, None, ["SES"], ["SEO"])
-        for b in range(2):
-            mm(T.pT[:, 128 * b:128 * b + 128], T.SEO[:, 128 * b:128 * b + 128], T.Idb[:], True, True, ["SEO", "Idb"], ["pT"])
+        scan(T.SC1[:], T.SM0[:], T.pK[:, 0:256], A.mult, A.max, ["SM0", "pK"], ["SC1"])
+        tt(T.BI[:], T.SC1[:, 15::16], T.SK[:], A.max, ["SC1", "SK"], ["BI"])
+        for n, (sh, m) in enumerate([(12, 15), (0, 31), (5, 127)]):
+            ts(T.XI[:, 16 * n:16 * n + 16], T.BI[:], sh, m, A.logical_shift_right, A.bitwise_and, ["BI"], ["XI%d" % n])
+        tt(T.LOD[:, 0::16], T.SH[:], T.XI[:], A.subtract, ["SH0", "SH1", "SH2", "XI0", "XI1", "XI2"], ["LOD"])
+        scan(T.LOS[:], T.SMb[:], T.LOD[:, 0:512], A.mult, A.add, ["SMb0", "SMb1", "LOD"], ["LOS"])
+        onehot(0, 1)
+        ts(T.LO[:], T.LOS[:, 256:512], 0.0, 0.25, A.not_equal, A.mult, ["LOS"], ["LO"])
+        onehot(1, OH0)
+        tt(T.SEO[:], T.pV[:, 0:256], T.LO[:], A.is_ge, ["pV", "LO"], ["SEO"])
+        for a, b, c, d in pieces(t):
+            mm(T.pT[c:c + 32, d:d + 64], T.SEO[a:a + 64, b:b + 32], T.Idb[a:a + 64, a:a + 64], True, True, ["SEO", "Idb"], ["pT"])
+        tt(T.LOO[:], T.pV[:, 0:256], T.LOS[:, 0:256], A.is_equal, ["pV", "LOS"], ["LOO"])
+        if OH0 == 16:
+            kills(t)
         tt(T.DM[:], T.pT[:, 0:256], T.DIFF[:], A.mult, ["pT", "DIFF"], ["DM"])
-        L, lk = blist(t)
-        tt(T.TR[:].indirect(L), T.Hf[:], T.DM[:], A.add, ["Hf", "DM", lk], ["TR"])
+        L, lk = ul(t, 1)
+        tt(T.TR[:].indirect(L), T.Hb[:], T.DM[:], A.add, ["Hb", "DM", lk], ["TR"])
 
-    dma("y", T.CI[:], T.calls[:], [], ["CI"])
-    dma("s", T.RI[:], T.routes[:], [], ["RI"])
-    dma("y", T.LI[:, 0:16], T.routes[0::16, :], [], ["LI0"])
-    dma("s", T.TI[:], T.trunk[:], [], ["TI"])
-    for h in range(2):
-        dma("y", T.F[:, 1024 * h:1024 * h + 1024], T.paths[:, 1024 * h:1024 * h + 1024], [], [FK[h]])
-    for t in range(1, RO):
-        dma("s", T.LI[:, 16 * t:16 * t + 16], T.routes[t::16, :], [], ["LI%d" % t])
-    iota("iOF", [[1, 16], [16, 16]])
-    iota("iA", [[0, 1]], 0, 1)
-    iota("iG16", [[1, 8], [0, 16]])
-    iota("iX", [[1, 144]])
-    iota("iG8", [[0, 16], [1, 8]])
-    iota("i16t", [[1, 16]])
-    iota("iS", [[0, 16], [1, 16]])
-    iota("iWT", [[-64, 16], [0, 8]], 976)
-    iota("iFI", [[16, 64]])
-    iota("IREV", [[-1, 128]], 127)
-    iota("FS", [[0, 2048]], 0, 0, FSK)
-    fill(T.S0[:], 0.0, "S0")
-    cp(T.OFFS[:], T.iOF[:], ["iOF"], ["OFFS"])
-    ts(T.CC[:, 0:1], T.iA[:], 15, None, A.bitwise_and, None, ["iA"], ["CC0"])
-    ts(T.CC[:, 1:2], T.iA[:], 4, None, A.logical_shift_right, None, ["iA"], ["CC1"])
-    ts(T.CC[:, 2:3], T.iA[:], 4, 1, A.logical_shift_right, A.bitwise_and, ["iA"], ["CC2"])
-    cp(T.CC[:, 3:4], T.iA[:], ["iA"], ["CC3"])
-    ts(T.CC[:, 4:5], T.iA[:], 112, None, A.bitwise_and, None, ["iA"], ["CC4"])
-    cp(T.CCf[:, 0:5], T.CC[:, 0:5], ["CC%d" % i for i in range(5)], ["CCf"])
-    kc, gc, par, pc, g16 = [T.CCf[:, i:i + 1] for i in range(5)]
-    ts(T.BP[:], kc, -1.0, -8 * LK + 2047 * 32 + 15, A.mult, A.add, ["CCf"], ["BP"])
-    ts(T.BO[:], T.iG16[:], gc, None, A.is_equal, None, ["iG16", "CCf"], ["BO"])
-    cp(own[:, PCF:PCF + 16], T.CI[:], ["CI"], ["OC"])
-    ts(T.TH[:], T.CI[:], 3584, None, A.bitwise_and, None, ["CI"], ["TH"])
-    cp(own[:, PTF:PTF + 16], T.TH[:], ["TH"], ["OT"])
+    def kills(t):
+        for n in range(2):
+            for s in range(n, 16, 2):
+                mm(T.pX[:, 16 * n:16 * n + 16], T.OH[:, 128 * s:128 * s + 128], T.LOO[:, 16 * s:16 * s + 16], s == n, s == 14 + n,
+                   ["LOO", "OH%d" % s], ["pX"])
+        y = "Yf" if t else "YfB"
+        mm(T.pY[0:32, 0:128], T.Idb[0:32, 0:32], T[y][0:32, :], True, False, ["Idb", y], ["pY"])
+        act(T.KS[:], T.pX[:, 0:32], ["pX"], ["KS"])
+        mm(T.pY[0:32, 0:128], T.KS[:], T.Idb[:], False, True, ["Idb", "KS"], ["pY"])
+        act(T.Yf[0:32, :], T.pY[0:32, 0:128], ["pY"], ["Yf"], func=AF.Sign)
+        if t < RO - 1:
+            spread_flags()
 
-    def load_s0(r):
-        dma("y", T.S0[0::16, 0:256], PKb[r][:, PCF:PCF + 16], ["OC" if r == q else pk[r]], ["S0"])
-        dma("y", T.S0[0::16, 256:512], PKb[r][:, PTF:PTF + 16], ["OT" if r == q else pk[r]], ["S0"])
+    def seeker_names():
+        tt(T.CMb[:], T.CQ[:].indirect(T.REP[:]), T.MKb[:], A.mult, ["CQ", "REP", "MKb"], ["CMb"])
+        for r in range(N):
+            for h in range(4):
+                a, s = 64 * (r % 2), 8 * (r // 2) + 2 * h
+                mm(T.pX[a:a + 64, s:s + 2], T.CMb[:, 64 * h:64 * h + 64], T.IND[:, 2 * r:2 * r + 2], True, True, ["CMb", "IND"], ["pX"])
+        cp(T.TR[:], T.pT[:], ["pT"], ["TR"])
+        tt(T.CMa[:], T.CQ[:].indirect(T.REP[:]), T.MKa[:], A.mult, ["CQ", "REP", "MKa"], ["CMa"])
+        for n in range(2):
+            for jb in range(4):
+                mm(T.pM[64 * n:64 * n + 64, jb:16:4], T.CMa[:, 64 * jb:64 * jb + 64], T.IND[:, n::2], True, True, ["CMa", "IND"], ["pM"])
 
-    def load_sr():
-        mm(T.pR[:, 0:512], T.BO[:], T.S0[:], True, False, ["BO", "S0"], ["pR"])
+    def seeker_keys():
+        cp(T.NI32[:], T.pX[:, 0:16], ["pX"], ["NI32"])
+        ts(T.BD[:], T.NI32[:], 1536, None, A.bitwise_and, None, ["NI32"], ["BD"])
+        cp(T.O16[:, 256:272], T.pM[:, 0:16], ["pM"], ["SL"])
+        ts(T.BN0[:, 0::16], T.BD[:], 32.0, 16384 - 9 * LK, A.mult, A.add, ["BD"], ["BN0"])
+        tt(T.NF[:], T.BD[:], T.NI32[:], A.subtract, ["BD", "NI32"], ["NF"])
+        scan(T.BND[:], T.SMb[:, 0:256], T.BN0[:], A.mult, A.add, ["SMb0", "BN0"], ["BND"])
+        ts(T.SK[:], T.NF[:], 32.0, 16368.0, A.mult, A.add, ["NF"], ["SK"])
+        ts(T.SH[:, 0:16], T.BD[:], 1.0 / 128, 3.0, A.mult, A.add, ["BD"], ["SH0"])
 
-    def none_s(tab, keys):
-        act(T.NI[:, 1024:2048], tab[:, 1024:2048].indirect(T.OFI[:]), keys + ["OFI", "MB"], ["NI1"], func=AF.Relu, bias=T.MB[:, 0:1])
+    def other_lists():
+        for r in range(N):
+            for t in range(1, RO):
+                src, key = second(r, 32 * t - 32, 32 * t)
+                o = (r + t) % N
+                mm(T.pT[32 * o:32 * o + 32, 32 * t:32 + 32 * t], mine, src, True, True, ["Id16", key], ["pT"])
 
-    def none_v(tab, keys):
-        ts(T.NI[:, 0:1024], tab[:, 0:1024], float(NONE), None, A.is_equal, None, keys, ["NI0"])
+    def other_lists_v():
+        ts(T.UL[:, 32:160], T.pT[:, 32:160], col["o512"], None, A.subtract, None, ["pT", "c_o512"], ["UL1"])
 
-    load_s0(q)
+    def hops_v():
+        op("v", lambda: V.tensor_scalar(T.DS[:].indirect(T.O16[:, 256:272]), T.R[:, 0:256], 1.0, -float(NONE), A.mult, A.add), ["R0", "SL"], ["DS"])
+
+    def seekers():
+        for x in range(N):
+            act(T.D16[:, G * x:G * x + G], T.DS[:, G * x:G * x + G], ["DS"], ["D16%d" % x])
+            for y in range(4):
+                mm(T.pM[:, 128 * x:128 * x + 128], T.SD[:, 3 - y:131 - y], T.D16[:, G * x + 128 * y:G * x + 128 * y + 128], y == 0, y == 3,
+                   ["SD", "D16%d" % x], ["pM"])
+        act(T.YD[:], T.pM[:], ["pM"], ["YD"])
+        none_sums(False)
+        for x in range(N):
+            mm(T.pY[0:32, 0:128], T.Zq[:, 12 - 4 * x:44 - 4 * x], T.YD[:, 128 * x:128 * x + 128], False, x == N - 1, ["Zq", "YD"], ["pY"])
+        act(T.YfB[0:32, :], T.pY[0:32, 0:128], ["pY", "c_m15"], ["YfB"], func=AF.Relu, bias=T.CF[0:32, 30:31])
+
+    seeker_names()
+    hold_a(0)
+    routes()
+    lists()
+    seeker_keys()
+    hold_b(0)
+    other_lists()
     for t in range(RO):
-        dma("y", T.FS[t::16, :], T.paths[t::16, :], [], ["FS%d" % t])
-    cp(own[:, PR:PR + 256], T.RI[:], ["RI"], ["OR"])
-    expand(0, 0, 1)
-    ts(UL(q, 80), T.LI[:, 0:16], -q * G, None, A.add, None, ["LI0"], ["ULa"])
-    cp(T.TR[:], T.TI[:], ["TI"], ["TR"])
-    hold_v(0)
-    hold_s(0)
-    expand(0, 3)
-    ts(T.IND[:], T.iG8[:], gc, None, A.is_equal, None, ["iG8", "CCf"], ["IND"])
-    ts(T.XB[:, 16:32], T.CI[:], par, None, A.mult, None, ["CI", "CCf"], ["XBo"])
-    tt(T.XB[:, 0:16], own[:, PCF:PCF + 16], T.XB[:, 16:32], A.subtract, ["OC", "XBo"], ["XBe"])
-    op("v", lambda: V.transpose(T.XT[:], T.XB[:]), ["XBo", "XBe"], ["XT"])
-    for t in (1, 2, 3):
-        ts(own[:, PL + 16 * t - 16:PL + 16 * t], T.LI[:, 16 * t:16 * t + 16], -((q + t) % N * G), None, A.add, None, ["LI%d" % t], ["OL%d" % t])
-    tt(own[:, PSL:PSL + 16], T.XT[:, 0:16], T.XT[:, 16:32], A.add, ["XT"], ["OS"])
-    for b in range(2):
-        mm(T.pM[:, 8 * b:8 * b + 8], T.S0[:, 128 * b:128 * b + 128], T.IND[:, 0:8], True, True, ["S0", "IND"], ["pM"])
-    load_sr()
-    ts(T.Idf[:], T.iX[:, 0:128], pc, None, A.is_equal, None, ["iX", "CCf"], ["Idf"])
-    ts(T.Idb[:], T.iX[:, 0:128], pc, None, A.is_equal, None, ["iX", "CCf"], ["Idb"])
-    ts(T.Idm[:], T.Idf[:], -1.0, None, A.mult, None, ["Idf"], ["Idm"])
-    fill(T.MB[:, 1:2], -0.5, "MB1")
-    ts(own[:, PSK:PSK + 16], T.pM[:, 0:16], -32.0, 2047.0 * 32 + 16, A.mult, A.add, ["pM"], [pk[q]])
-    send(own[:], [pk[q], "OC", "OT", "OR", "OS", "OL1", "OL2", "OL3"], "set%d" % q, "lset")
-    ts(T.CCf[:, 5:6], g16, 15.0, None, A.add, None, ["CCf"], ["CCf5"])
-    ts(T.Z[:], T.iX[:], T.CCf[:, 5:6], None, A.is_equal, None, ["iX", "CCf5"], ["Z"])
-    ts(T.MK[:], T.i16t[:], kc, None, A.is_equal, None, ["i16t", "CCf"], ["MK"])
-    ts(T.Idn[:], T.Idb[:], 9.0 * LK, None, A.mult, None, ["Idb"], ["Idn"])
-    tt(T.BW[:], T.IND[:], T.iWT[:], A.mult, ["IND", "iWT"], ["BW"])
-    ts(T.BL[:], T.IND[:, 0:8], LK, None, A.mult, None, ["IND"], ["BL"])
-    ts(T.BD[:], T.IND[:, 0:8], OUT, None, A.mult, None, ["IND"], ["BD"])
-    ts(T.SM0[:], T.iS[:], 1.0, None, A.min, None, ["iS"], ["SM0"])
-    ts(T.SMb[:], T.iS[:], 1.0, None, A.min, None, ["iS"], ["SMb"])
-    fill(T.LOD[:], -1.0, "LOD")
-    fill(T.SED[:], 1.0, "SED")
-    fill(T.MB[:, 0:1], -2047.0, "MB")
-    ts(T.OFI[:], T.iFI[:], kc, None, A.add, None, ["iFI", "CCf"], ["OFI"])
-    none_s(T.F, ["Fb"])
-    hold_d(0)
-    expand(0, 2)
-    ts(UL(q, 96), T.LI[:, 64:80], -q * G, None, A.add, None, ["LI4"], ["ULb"])
-    set_list(q)
-    ts(T.Z0[:], T.Z[:], T.MK[:, 0:1], None, A.mult, None, ["Z", "MK"], ["Z0"])
-
-    none_v(T.F, ["Fa"])
-    for l in range(16):
-        mm(T.pY[:, 0:128], T.Z[:, l:l + 128], T.NI[:, 128 * l:128 * l + 128], l == 0, l == 15, ["Z", "NI%d" % (l // 8)], ["pY"])
-    like(0, range(PRE))
-    ts(T.Yf[:], T.pY[:, 0:128], 16.0, None, A.is_ge, None, ["pY"], ["Yf"])
-    build_w()
-    dead_pass(0, "s")
-    like(0, range(PRE, 3))
-    dead_pass(0, "v")
-    for t in range(RO):
-        if t < 4:
-            load_s0((q - t - 1) % N)
-        dead_t(t)
-        candidates(t)
-        if t > 0:
-            dma("y", T.F[t::16, :], T.FS[t::16, :], ["FS%d" % t], FK)
+        keys(t)
+        look_up(t)
+        if t == 0:
+            seekers()
+        if t < N - 1:
+            turn_table(t + 1)
+        if t == RO - 1:
+            mm(T.pM[:], T.Id16[:], T.YD[:], True, False, ["Id16", "YD"], ["pM"])
+            mm(T.pM[:], T.Id16[:], T.FB16[:], False, False, ["Id16", "FB16"], ["pM"])
         decide(t)
-        if t == 4:
-            break
-        load_sr()
-        if t == 0:
-            set_list(others[2])
-        hold_v(t + 1)
-        hold_s(t + 1)
-        if t < 3:
-            expand(t + 1, 3)
-        hold_d(t + 1)
-        if t < 3:
-            expand(t + 1, 2)
-        if t == 0:
-            cp(T.FS[:].indirect(UL(q, 0)), own[:, PR:PR + 256], [ul[q], "OR"], FSK)
-            for r in [others[2], others[1], others[0]]:
-                if r != others[2]:
-                    set_list(r)
-                cp(T.FS[:].indirect(UL(r, 0)), PKb[r][:, PR:PR + 256], [ul[r], pk[r]], FSK)
-            dma("y", T.F[0::16, :], T.FS[0::16, :], ["FS0"], FK)
-            none_s(T.FS, FSK)
-            none_v(T.FS, FSK)
-            mm(T.pY[:, 0:128], T.Idb[:], T.Yf[:], True, False, ["Idb", "Yf"], ["pY"])
-            for l in range(16):
-                mm(T.pY[:, 0:128], T.Z0[:, l:l + 128], T.NI[:, 128 * l:128 * l + 128], False, l == 15, ["Z0", "NI%d" % (l // 8)], ["pY"])
-            ts(T.Yf[:], T.pY[:, 0:128], 2.0, None, A.is_ge, None, ["pY"], ["Yf"])
-            kills_t(1)
-        else:
-            kills_t(t + 1)
-            like(t + 1, range(PRE))
-        kills_v()
-        build_w()
-        dead_pass(t + 1, "s")
-        like(t + 1, range(3) if t == 0 else range(PRE, 3))
-        dead_pass(t + 1, "v")
-    dma("y", T.yt[:], T.TR[:], ["TR"], ["yt"])
-    for l in range(4):
-        m = 15 - 4 * q - l
-        ts(T.BS[:, 128 * l:128 * l + 128], T.BO[:], T.MK[:, m:m + 1], float(NONE), A.mult, A.mult, ["BO", "MK"], ["BS"])
-    kills_t(RO)
-    kills_v()
-    for l in range(4):
-        mm(T.pM[:, 128 * l:128 * l + 128], T.BS[:, 128 * l:128 * l + 128], T.Yf[:], True, True, ["BS", "Yf"], ["pM"])
-    tt(T.YO[:], T.pM[:, 0:512], T.F[:, G * q:G * q + G], A.max, ["pM"] + FK, ["YO"])
-    dma("y", T.yp[:], T.YO[:], ["YO"], ["yp"])
+        if t < RO - 1:
+            hold_a(t + 1)
+        if OH0 < 16:
+            onehot(OH0, 16)
+            kills(t)
+        if t < RO - 1:
+            lists()
+            hold_b(t + 1)
+    for x in range(N):
+        mm(T.pM[:, 128 * x:128 * x + 128], T.ZD[0:32, 128 * x:128 * x + 128], T.Yf[0:32, :], False, x == N - 1, ["ZD%d" % x, "Yf"], ["pM"])
+    ts(T.OP[:], T.pM[:], float(NONE), None, A.min, None, ["pM"], ["OP"])
+    send(lambda r: T.OP[:, 128 * r:128 * r + 128], lambda r: T.RP[:, 128 * q:128 * q + 128], ["OP"], "RP", "rp", "lp")
+    banks = list(zip(others + [q], ["pK", "pT", "pR", "pO"]))
+    for y in range(4):
+        act(T.TR16[:, 128 * y:128 * y + 128], T.TR[:, 128 * y:128 * y + 128], ["TR"], ["TR16%d" % y])
+        for o, bank in banks:
+            mm(T[bank][:, 0:128], T.ST[32 * o:32 * o + 32, 3 - y:131 - y], T.TR16[32 * o:32 * o + 32, 128 * y:128 * y + 128], y == 0, y == 3,
+               ["ST%d" % o, "TR16%d" % y], [bank])
+    for n, (o, bank) in enumerate(banks):
+        (act if n % 2 else cp)(T.OY[:, 128 * o:128 * o + 128], T[bank][:, 0:128], [bank], ["OY%d" % o])
+    send(lambda r: T.OY[:, 128 * r:128 * r + 128], lambda r: T.RY[:, 128 * q:128 * q + 128], ["OY%d" % r for r in others], "RY", "ry", "ly")
+    for out, own, far, qn in ((T.yp, "OP", "RP", "s"), (T.yt, "OY", "RY", "y")):
+        for r in [q] + others:
+            k = own if r == q else far
+            dma(qn, out[32 * r:32 * r + 32, :], T[k][:, 128 * r:128 * r + 128], ["OY%d" % q if k == "OY" else k], ["out%s%d" % (own, r)])
     need("g", [(s, v) for s, v in total.items()])

@@ -5,15 +5,15 @@ N, G, C, K, RO = 4, 512, 2048, 256, 5
 NONE = N * G
 f32, f16, b16, i32, u16 = "float32", "float16", "bfloat16", "int32", "uint16"
 LK = 65536.0
-W1, W2 = 176, 384
-LCH = [4, 4, 4, 2, 1, 1]
+W1, W2 = 176, 128
+LCH = [4, 4, 4, 3, 1]
 DCH = [4, 4, 4, 2, 2, 1]
-LCH0 = [1, 1, 2, 4, 4, 2, 1, 1]
-DOFF = 5.0
-KAT = 1
+LCH0 = [1, 1, 2, 4, 4, 3, 1]
+DOFF = 6.0
+KAT = 0
 EAT = 12
-HAT = 4
-OH0 = 16
+OHV = 10
+OH3 = 3
 VD = 0
 FS = 4
 HAV = False
@@ -25,12 +25,12 @@ def sb(names, cols, dtype):
 
 SCRATCH = {
     **sb("iA", 1, i32), **sb("CC", 12, i32), **sb("CF", 32, f32), **sb("iB", 4, f32), **sb("OFS", 28, u16),
-    **sb("iX", 144, b16), **sb("SelR ONE", 192, f16), **sb("Zq", 48, f16), **sb("ST SD", 144, f16),
-    **sb("Id16 Idm NK", 128, f16), **sb("Idb Idn TO Yf YfB BIG", 128, b16), **sb("KS", 32, b16), **sb("ZD", 512, b16),
+    **sb("iX", 176, b16), **sb("SelR", 176, f16), **sb("ONE", 256, b16), **sb("Zq", 48, f16), **sb("Zs", 48, b16), **sb("ST SD", 144, f16),
+    **sb("Id16 Idm NK Dm", 128, f16), **sb("Idb Idn TO Yf YfB BIG", 128, b16), **sb("KS", 64, f16), **sb("ZD", 512, b16),
     **sb("SM0 Hb DIFF DM SC1", 256, f32), **sb("iC iCa MKa MKb", 256, b16), **sb("BOw CMa CMb Ha Hc", 256, f16),
     **sb("ZER CKf BND BN0 ELIG LO SEO LOO", 256, b16), **sb("SMb LOS", 512, b16), **sb("LOD", 768, b16), **sb("OT", 512, f16),
     **sb("CQ SK NF", 16, f32), **sb("SH", 48, f32), **sb("NI32 BD BI", 16, i32), **sb("XI", 48, i32), **sb("REP", 16, u16),
-    **sb("BL", 8, b16), **sb("IND", 8, f16), **sb("R", 1024, f32),
+    **sb("BL", 8, b16), **sb("IND", 8, f16), **sb("R", 1024, f16), **sb("RQ RS", 256, f16), **sb("RF", 256, f32),
     **sb("IN", 352, i32), **sb("TI", 608, i32), **sb("TS", 608, f16), **sb("FB", 512, i32), **sb("FB16 NI YD TR16", 512, f16),
     **sb("X1", N * W1, f16), **sb("X2", N * W2, f16),
     **sb("UL", 160, u16), **sb("O16", 272, u16), **sb("TR OY OP RY RP", 512, f32),
@@ -38,7 +38,7 @@ SCRATCH = {
     **sb("Ta Tb", 32, f32), **sb("GM", 8, f32), **sb("D16", 2048, f16), "TT": ("sbuf", [128, 8, 32], b16),
     **{n: ("psum", [128, 512], f32) for n in "pK pV pX pY pO pT pR pM".split()},
 }
-SEMAPHORES = ["cv", "cs", "ct", "cg", "ra", "rb", "ry", "rp", "la", "lb", "ly", "lp"] + ["d%d" % i for i in range(56)]
+SEMAPHORES = ["cv", "cs", "ct", "cg", "ra", "rb", "rc", "ry", "rp", "la", "lb", "lc", "ly", "lp"] + ["d%d" % i for i in range(56)]
 
 
 def rank_program(g, core, T, topo):
@@ -85,7 +85,7 @@ def rank_program(g, core, T, topo):
                     toks.append((s, v))
             if ps or k in writes:
                 for (oq, s, v, far) in readers.get(k, []):
-                    if far or oq != qn:
+                    if far or oq != qn or k[:2] == "c_":
                         toks.append((s, v))
         return toks
 
@@ -189,7 +189,7 @@ def rank_program(g, core, T, topo):
         a = 256 + 16 * ((t - 1) % RO)
         dma("sysys"[t], T.IN[:, a:a + 16], T.routes[t::16, :], [], ["IL%d" % t])
     dma("y", T.IN[:, 0:256], T.routes[:], [], ["IR"])
-    INK = ["IR"] + ["IL%d" % n for n in range(1, RO)]
+    INK = ["IL%d" % n for n in range(1, RO)]
     dma("s", T.TI[:, TAT[0]:TAT[0] + 128], T.trunk[32 * q:32 * q + 32, :], [], ["TI0"])
     for x in range(N):
         dma("y", T.FB[:, 128 * x:128 * x + 128], T.paths[32 * q:32 * q + 32, G * x:G * x + G], [], ["FB%d" % x])
@@ -197,16 +197,14 @@ def rank_program(g, core, T, topo):
     WK = ["W%d" % x for x in range(N)]
 
     iota("iA", [[0, 1]], 0, 1)
-    iota("iB", [[16, 4]], 256)
-    iota("iX", [[1, 144]])
+    iota("iB", [[16, 4]])
+    iota("iX", [[1, 176]])
     iota("iC", [[1, 16], [0, 16]])
     iota("CKf", [[0, 16], [-1, 16]], -17)
-    iota("ONE", [[0, 192]], 1)
-    for y in range(4):
-        pick(T.SelF[:, 128 * y:128 * y + 128], T.ONE[:, 0:128], [[64, 2], [0, 4], [4, 16]], y, ["ONE"], ["SelF%d" % y])
-    bits = [(0, 15), (0, 3), (2, 3), (0, 127), (5, 3), (6, 1), (4, 3), (4, 7)]
-    names = "k y z pc o n6 hh gg".split()
-    col = {n: T.CF[:, i:i + 1] for i, n in enumerate(names + "sw k16 o512 gp tZ eb m17 u v".split())}
+    iota("ONE", [[0, 256]], 1)
+    bits = [(0, 15), (0, 3), (2, 3), (0, 127), (5, 3), (6, 1), (4, 3), (4, 7), (4, 1)]
+    names = "k y z pc o n6 hh gg n4".split()
+    col = {n: T.CF[:, i:i + 1] for i, n in enumerate(names + "sw k16 o512 gp tZ eb m17 k0 u v".split())}
 
     def parts(a, b):
         for i in range(a, b):
@@ -236,7 +234,19 @@ def rank_program(g, core, T, topo):
     turn_table(0)
     act(T.Idb[:], T.Id16[:], ["Id16"], ["Idb"])
     act(T.NK[:], T.Id16[:], ["Id16"], ["NK"], scale=-32.0)
-    parts(4, 8)
+    act(T.Idm[:], T.Id16[:], ["Id16"], ["Idm"], scale=-1.0)
+    act(T.Idn[:], T.Id16[:], ["Id16"], ["Idn"], scale=9.0 * LK)
+    fill(col["m17"], -17.0, "c_m17")
+    act(T.SM0[:], T.CKf[:], ["CKf", "c_m17"], ["SM0"], func=AF.Sign, scale=-1.0, bias=col["m17"])
+    iota("iCa", [[1, 4], [4, 4], [0, 16]])
+
+    def spread_table(y):
+        pick(T.SelF[:, 128 * y:128 * y + 128], T.ONE[:, 0:128], [[64, 2], [0, 4], [4, 16]], y, ["ONE"], ["SelF%d" % y])
+
+    spread_table(0)
+    parts(4, 9)
+    num("u", "n4", 64.0, "k", A.mult, A.add)
+    ts(T.SelR[:], T.iX[:], -48.0, col["u"], A.add, A.is_equal, ["iX", "c_u"], ["SelR"])
     num("o512", "o", 512.0, None, A.mult, None)
     num("gp", "hh", 2.0, "n6", A.mult, A.add)
     num("tZ", "n6", 16.0, "y", A.mult, A.add)
@@ -247,10 +257,25 @@ def rank_program(g, core, T, topo):
     cp(T.TS[:, 176:432], T.TI[:, 176:432], ["TI2", "TI3"], ["TS2"])
     send(lambda r: T.TS[:, min(TAT[(r - q) % N], CAT[(r - q) % N]):min(TAT[(r - q) % N], CAT[(r - q) % N]) + W1],
          lambda r: T.X1[:, W1 * q:W1 * q + W1], ["TS1", "TS2", "TC", "TC3"], "X1", "ra", "la")
-    act(second(q, 0, W2)[0], T.IN[:, 0:320].indirect(T.OFS[:, 4:28]), INK + ["OFR", "OFa", "OFb"], ["XR"])
-    send(lambda r: second(q, 0, W2)[0], lambda r: second(q, 0, W2)[0], ["XR"], "X2", "rb", "lb")
-    iota("iCa", [[1, 4], [4, 4], [0, 16]])
-    pick(T.SelR[:], T.ONE[:], [[16, 3], [-200, 4], [1, 16]], 32 * q + 600, ["ONE"], ["SelR"])
+    spread_table(1)
+    spread_table(2)
+    act(T.RQ[:], T.IN[:, 0:256].indirect(T.OFS[:, 12:28]), ["IR", "OFR"], ["RQ"])
+    for r in others + [q]:
+        need("t", [("ct", cnt.get("ct", 0))])
+        for h in range(4):
+            mm(T.pR[:, 64 * r:64 * r + 64], T.SelR[32 * r:32 * r + 32, 48 - 16 * h:176 - 16 * h], T.RQ[32 * r:32 * r + 32, 64 * h:64 * h + 64],
+               h == 0, h == 3, ["SelR", "RQ"], ["pR"])
+    act(T.RS[:], T.pR[:, 0:256], ["pR"], ["RS"])
+    send(lambda r: T.RS[:, 64 * r:64 * r + 64], lambda r: T.R[:, 64 * q:64 * q + 64], ["RS"], "RX", "rb", "lb")
+    act(T.R[:, 64 * q:64 * q + 64], T.RS[:, 64 * q:64 * q + 64], ["RS"], ["RO"])
+    act(second(q, 0, W2)[0], T.IN[:, 256:320].indirect(T.OFS[:, 4:12]), INK + ["OFa", "OFb"], ["XR"])
+    send(lambda r: second(q, 0, W2)[0], lambda r: second(q, 0, W2)[0], ["XR"], "X2", "rc", "lc")
+    spread_table(3)
+    iota("BN0", [[0, 256]])
+    iota("ZER", [[0, 256]])
+    iota("LOD", [[0, 768]], -1)
+    op("g", lambda: g.affine_select(T.Dm[:], T.Idm[:], [[1, 128]], A.not_equal, 1.0, -1, -1), ["Idm"], ["Dm"])
+    op("g", lambda: g.affine_select(T.Dm[:], T.Dm[:], [[200, 128]], A.not_equal, -1.0, -127, 1), ["Dm"], ["Dm"])
     iota("DS", [[0, 2048]])
     iota("BIG", [[0, 128]], 4096)
     for x in range(N):
@@ -260,14 +285,8 @@ def rank_program(g, core, T, topo):
 
     fill(T.W[:, 1024:2048], 0.0, *WK)
     cp(T.TS[:, 480:608], T.TI[:, 480:608], ["TI0"], ["TS0"])
-    act(T.Idm[:], T.Id16[:], ["Id16"], ["Idm"], scale=-1.0)
-    act(T.Idn[:], T.Id16[:], ["Id16"], ["Idn"], scale=9.0 * LK)
-    fill(col["m17"], -17.0, "c_m17")
-    act(T.SM0[:], T.CKf[:], ["CKf", "c_m17"], ["SM0"], func=AF.Sign, scale=-1.0, bias=col["m17"])
     for h in range(2):
         act(T.SMb[:, 256 * h:256 * h + 256], T.SM0[:], ["SM0"], ["SMb%d" % h])
-    act(T.ZER[:], T.CKf[:], ["CKf"], ["ZER"], scale=0.0)
-    act(T.BN0[:], T.CKf[:], ["CKf"], ["BN0"], scale=0.0)
     ts(T.Zq[:], T.iX[:, 0:48], -12.0, col["tZ"], A.add, A.is_equal, ["iX", "c_tZ"], ["Zq"])
     ts(T.IND[:], T.iX[:, 0:8], col["gg"], None, A.is_equal, None, ["iX", "c_gg"], ["IND"])
     ts(T.GM[:], T.iX[:, 0:8], col["gp"], None, A.is_equal, None, ["iX", "c_gp"], ["GM"])
@@ -277,8 +296,10 @@ def rank_program(g, core, T, topo):
     tt(T.Ta[:], T.Ta[:], T.Tb[:], A.add, ["Ta", "Tb"], ["Ta"])
     ts(T.MKb[:], T.iC[:], col["k"], None, A.is_equal, None, ["iC", "c_k"], ["MKb"])
     ts(T.Ta[:], T.Ta[:], -1.0 / 128, None, A.add, None, ["Ta"], ["Ta"])
+    num("k0", "k", 0.0, None, A.is_equal, None)
+    ts(T.Tb[:], T.Ta[:], col["k0"], None, A.mult, None, ["Ta", "c_k0"], ["Tb"])
     for n in range(8):
-        act(T.TT[:, n, :], T.Ta[:], ["Ta", "GM"], ["TT%d" % n], scale=T.GM[:, n:n + 1])
+        act(T.TT[:, n, :], T.Tb[:], ["Tb", "GM"], ["TT%d" % n], scale=T.GM[:, n:n + 1])
     TTK = ["TT%d" % n for n in range(8)]
     act(T.BL[:], T.GM[:], ["GM"], ["BL"], scale=LK)
     fill(T.CF[:, 30:31], -15.0, "c_m15")
@@ -301,57 +322,61 @@ def rank_program(g, core, T, topo):
             none_sums(True)
         if x == 1:
             act(T.Yf[0:32, :], T.pY[0:32, 0:128], ["pY", "c_m15"], ["Yf"], func=AF.Relu, bias=T.CF[0:32, 30:31])
-            spread_flags()
         (act if x < FS else cp)(T.F[:, G * x:G * x + G], T[bank][:], [bank], [FK[x]])
     ts(T.MKa[:], T.iCa[:], col["k"], None, A.is_equal, None, ["iCa", "c_k"], ["MKa"])
     ts(T.BOw[:, 0:128], T.iC[:, 0:128], col["gg"], None, A.is_equal, None, ["iC", "c_gg"], ["BOw0"])
     act(T.BOw[:, 128:256], T.BOw[:, 0:128], ["BOw0"], ["BOw1"])
-    ts(T.TO[:], T.iC[:, 0:128], col["gp"], -64.0, A.is_equal, A.mult, ["iC", "c_gp"], ["TO"])
-    fill(T.LOD[:], -1.0, "LOD")
+    num("u", "k0", -64.0, None, A.mult, None)
+    ts(T.TO[:], T.iC[:, 0:128], col["gp"], col["u"], A.is_equal, A.mult, ["iC", "c_gp", "c_u"], ["TO"])
+    num("u", "n6", 16.0, 15.0, A.mult, A.add)
+    num("v", "k", 1.0, -1.0, A.is_equal, A.mult)
+    ts(T.Zs[:], T.iX[:, 0:48], col["u"], col["v"], A.is_equal, A.mult, ["iX", "c_u", "c_v"], ["Zs"])
     fill(T.SH[:, 16:32], 15.0, "SH1")
-    fill(T.SH[:, 32:48], 127.0, "SH2")
+    fill(T.SH[:, 32:32 + OHV], 127.0, "SH2")
+    if OHV < 16:
+        fill(T.SH[:, 32 + OHV:48], 127.5, "SH3")
     fill(col["eb"], 9 * LK - 16384 - 16, "c_eb")
-    num("u", "n6", 16.0, "k", A.mult, A.add)
-    num("v", "k", float(RO), None, A.is_lt, None)
-    num("u", "u", 4.0, 4.0, A.mult, A.add)
-    num("u", "u", "v", -1.0, A.mult, A.add)
-    ts(T.SD[:], T.iX[:], col["u"], None, A.is_equal, None, ["iX", "c_u"], ["SD"])
+
+    def hops_table():
+        num("u", "n6", 64.0, 3.0, A.mult, A.add)
+        num("v", "k", float(RO), None, A.is_lt, None)
+        num("u", "k", 4.0, "u", A.mult, A.add)
+        ts(T.SD[:], T.iX[:, 0:144], col["u"], col["v"], A.is_equal, A.mult, ["iX", "c_u", "c_v"], ["SD"])
 
     mine = T.Id16[:, 32 * q:32 * q + 32]
-    for r in [q] + others:
-        src, key = first(r, 1, 0, 48)
-        mm(T.pO[32 * r:32 * r + 32, 0:48], mine, src, True, True, ["Id16", key], ["pO"])
-    for o in [q] + others:
+
+    def trunks(o):
         src, key = first(o, 0, 0, 128)
         for x in range(4):
             mm(T.pT[32 * o:32 * o + 32, 128 * x:128 * x + 128], T.Id16[:, x::4], src, True, True, ["Id16", key], ["pT"])
-    ts(T.UL[:, 0:32], T.pO[:, 16:48], col["o512"], None, A.subtract, None, ["pO", "c_o512"], ["UL0"])
+
+    trunks(q)
+    for r in [q] + others:
+        src, key = first(r, 1, 0, 48)
+        mm(T.pO[32 * r:32 * r + 32, 0:48], mine, src, True, True, ["Id16", key], ["pO"])
     cp(T.CQ[:], T.pO[:, 0:16], ["pO"], ["CQ"])
+    ts(T.UL[:, 0:32], T.pO[:, 16:48], col["o512"], None, A.subtract, None, ["pO", "c_o512"], ["UL0"])
 
     def routes():
-        for r in [q] + others:
-            for h in range(4):
-                src, key = second(r, 128 + 64 * h, 192 + 64 * h)
-                mm(T.pR[:, 64 * r:64 * r + 64], T.SelR[:, 48 - 16 * h:176 - 16 * h], src, h == 0, h == 3, ["SelR", key], ["pR"])
-        for n in range(4):
-            act(T.R[:, 256 * n:256 * n + 256], T.pR[:, 0:256], ["pR"], ["R%d" % n])
+        act(T.R[:, 256:512], T.R[:, 0:256], ["RX", "RO"], ["R1"])
+        act(T.R[:, 512:1024], T.R[:, 0:512], ["RX", "RO", "R1"], ["R2", "R3"])
 
     def hold_a(t):
         L, lk = ul(t, 0)
-        (cp if HAV else act)(T.Ha[:], T.TR[:].indirect(L), ["TR", lk], ["Ha"])
-        for n in range(2):
-            for jb in range(4):
+        for h, way in enumerate([cp, act]):
+            way(T.Ha[:, 128 * h:128 * h + 128], T.TR[:].indirect(T.UL[:, 32 * t + 8 * h:32 * t + 8 * h + 8]), ["TR", lk], ["Ha%d" % h])
+        for jb in range(4):
+            for n in range(2):
                 a = 128 * (t % N) + 64 * n
                 mm(T.pO[64 * n:64 * n + 64, jb:256:4], T.Ha[:, 64 * jb:64 * jb + 64], T.OT[:, a:a + 64], True, True,
-                   ["Ha"] + ["OT%d_%d" % (t % N, r) for r in range(N)], ["pO"])
+                   ["Ha%d" % (jb // 2)] + ["OT%d_%d" % (t % N, r) for r in range(N)], ["pO"])
 
     def lists():
         cp(T.O16[:, 0:256], T.pO[:, 0:256], ["pO"], ["O16"])
 
-    def hold_b(t):
+    def hold(t, name):
         L, lk = ul(t, 1)
-        act(T.Hb[:], T.TR[:].indirect(L), ["TR", lk], ["Hb"])
-        act(T.Hc[:], T.Hb[:], ["Hb"], ["Hc"])
+        act(T[name][:], T.TR[:].indirect(L), ["TR", lk], [name])
 
     def pieces(t):
         for r in range(N):
@@ -378,7 +403,7 @@ def rank_program(g, core, T, topo):
 
     def like_v(a, b):
         tt(T.E[:, 256 * a:256 * b], T.F[:].indirect(T.O16[:, 16 * a:16 * b]), T.R[:, 0:256 * (b - a)], A.is_equal,
-           FK + ["O16"] + ["R%d" % n for n in range(b - a)], ["E%d" % p for p in range(a, b)])
+           FK + ["O16", "RX", "RO"] + ["R%d" % n for n in range(1, b - a)], ["E%d" % p for p in range(a, b)])
 
     def like_t(p):
         for b in range(2):
@@ -409,21 +434,24 @@ def rank_program(g, core, T, topo):
         lc, dc = chunks(LCH if t else LCH0, 16), chunks(DCH, 17 if t else 16)
         ds, dv = dc[:len(dc) - VD], dc[len(dc) - VD:]
         for n, c in enumerate(ds):
-            if n == KAT:
+            if n == (KAT if t else 1):
                 keys_s()
+            if t == 0 and n == 2:
+                seekers()
             dead("s", *c)
         for n, c in enumerate(lc):
-            like_v(*c)
+            if t or n:
+                like_v(*c)
             if t == 0 and n == 2:
                 other_lists_v()
-            if t == 0 and n == HAT:
-                hops_v()
         for c in dv:
             dead("v", *c)
         turns = [(b, 0, a, b) for a, b in lc] + [(b + DOFF, 1, a, b) for a, b in ds] + [(99 + b, 1, a, b) for a, b in dv]
         turns.sort()
         end = [x for x in turns if x[1]][-1]
         for x in turns:
+            if x[2] == 4 and not x[1] and t == RO - 1:
+                hops_t()
             if x[2] == EAT and not x[1]:
                 mm(T.pK[:, 0:256], T.Idn[:], T.ELIG[:], False, False, ["Idn", "ELIG"], ["pK"])
             for p in range(x[2], x[3]):
@@ -434,57 +462,77 @@ def rank_program(g, core, T, topo):
 
     def onehot(a, b):
         for c in range(a, b):
-            ts(T.OH[:, 128 * c:128 * c + 128], T.iX[:, 0:128], T.LOD[:, 512 + 16 * c:513 + 16 * c], None, A.is_equal, None, ["iX", "LOD"], ["OH%d" % c])
+            o, low = T.OH[:, 128 * c:128 * c + 128], T.LOD[:, 512 + 16 * c:513 + 16 * c]
+            if c < OHV:
+                ts(o, T.iX[:, 0:128], low, None, A.is_equal, None, ["iX", "LOD"], ["OH%d" % c])
+            else:
+                act(o, T.iX[:, 1:129], ["iX", "LOD"], ["OH%d" % c], func=AF.Sign, scale=-1.0, bias=low)
 
     def decide(t):
         scan(T.SC1[:], T.SM0[:], T.pK[:, 0:256], A.mult, A.max, ["SM0", "pK"], ["SC1"])
         tt(T.BI[:], T.SC1[:, 15::16], T.SK[:], A.max, ["SC1", "SK"], ["BI"])
         for n, (sh, m) in enumerate([(12, 15), (0, 31), (5, 127)]):
             ts(T.XI[:, 16 * n:16 * n + 16], T.BI[:], sh, m, A.logical_shift_right, A.bitwise_and, ["BI"], ["XI%d" % n])
-        tt(T.LOD[:, 0::16], T.SH[:], T.XI[:], A.subtract, ["SH0", "SH1", "SH2", "XI0", "XI1", "XI2"], ["LOD"])
+        tt(T.LOD[:, 0::16], T.SH[:], T.XI[:], A.subtract, ["SH0", "SH1", "SH2", "SH3", "XI0", "XI1", "XI2"], ["LOD"])
         scan(T.LOS[:], T.SMb[:], T.LOD[:, 0:512], A.mult, A.add, ["SMb0", "SMb1", "LOD"], ["LOS"])
+        onehot(OHV, 16)
+        hold(t, "Hb")
+        if t < N - 1:
+            turn_table(t + 1)
         onehot(0, 1)
         ts(T.LO[:], T.LOS[:, 256:512], 0.0, 0.25, A.not_equal, A.mult, ["LOS"], ["LO"])
-        onehot(1, OH0)
+        onehot(1, OHV - OH3)
         tt(T.SEO[:], T.pV[:, 0:256], T.LO[:], A.is_ge, ["pV", "LO"], ["SEO"])
         for a, b, c, d in pieces(t):
             mm(T.pT[c:c + 32, d:d + 64], T.SEO[a:a + 64, b:b + 32], T.Idb[a:a + 64, a:a + 64], True, True, ["SEO", "Idb"], ["pT"])
         tt(T.LOO[:], T.pV[:, 0:256], T.LOS[:, 0:256], A.is_equal, ["pV", "LOS"], ["LOO"])
-        if OH0 == 16:
-            kills(t)
+        onehot(OHV - OH3, OHV)
+        kills(t)
         tt(T.DM[:], T.pT[:, 0:256], T.DIFF[:], A.mult, ["pT", "DIFF"], ["DM"])
         L, lk = ul(t, 1)
         tt(T.TR[:].indirect(L), T.Hb[:], T.DM[:], A.add, ["Hb", "DM", lk], ["TR"])
 
     def kills(t):
-        for n in range(2):
-            for s in range(n, 16, 2):
-                mm(T.pX[:, 16 * n:16 * n + 16], T.OH[:, 128 * s:128 * s + 128], T.LOO[:, 16 * s:16 * s + 16], s == n, s == 14 + n,
-                   ["LOO", "OH%d" % s], ["pX"])
+        kinds = [x for x in (range(OHV, 16), range(OHV)) if len(x)]
+        for kind in kinds:
+            for n in range(2):
+                col0, ss = 16 * n + (32 if kind[0] else 0), [s for s in kind if s % 2 == n]
+                for s in ss:
+                    mm(T.pX[:, col0:col0 + 16], T.OH[:, 128 * s:128 * s + 128], T.LOO[:, 16 * s:16 * s + 16], s == ss[0], s == ss[-1],
+                       ["LOO", "OH%d" % s], ["pX"])
         y = "Yf" if t else "YfB"
         mm(T.pY[0:32, 0:128], T.Idb[0:32, 0:32], T[y][0:32, :], True, False, ["Idb", y], ["pY"])
-        act(T.KS[:], T.pX[:, 0:32], ["pX"], ["KS"])
-        mm(T.pY[0:32, 0:128], T.KS[:], T.Idb[:], False, True, ["Idb", "KS"], ["pY"])
+        act(T.KS[:, 0:32 * len(kinds)], T.pX[:, 0:32 * len(kinds)], ["pX"], ["KS"])
+        if len(kinds) > 1:
+            mm(T.pY[0:32, 0:128], T.KS[:, 32:64], T.Dm[:], False, False, ["Dm", "KS"], ["pY"])
+        mm(T.pY[0:32, 0:128], T.KS[:, 0:32], T.Id16[:], False, True, ["Id16", "KS"], ["pY"])
         act(T.Yf[0:32, :], T.pY[0:32, 0:128], ["pY"], ["Yf"], func=AF.Sign)
         if t < RO - 1:
             spread_flags()
 
     def seeker_names():
+        tt(T.CMa[:], T.CQ[:].indirect(T.REP[:]), T.MKa[:], A.mult, ["CQ", "REP", "MKa"], ["CMa"])
+        trunks(others[0])
+        trunks(others[1])
+        for n in range(2):
+            for jb in range(4):
+                mm(T.pY[64 * n:64 * n + 64, jb:16:4], T.CMa[:, 64 * jb:64 * jb + 64], T.IND[:, n::2], True, True, ["CMa", "IND"], ["pY"])
+        trunks(others[2])
+        act(T.TR[:], T.pT[:], ["pT"], ["TR"])
         tt(T.CMb[:], T.CQ[:].indirect(T.REP[:]), T.MKb[:], A.mult, ["CQ", "REP", "MKb"], ["CMb"])
+        cp(T.O16[:, 256:272], T.pY[:, 0:16], ["pY"], ["SL"])
+        cp(T.W[:].indirect(T.O16[:, 256:272]), T.ONE[:], ["SL", "ONE"], WK + ["Wa"])
+        spread_flags()
+
+    def seeker_turn():
         for r in range(N):
             for h in range(4):
                 a, s = 64 * (r % 2), 8 * (r // 2) + 2 * h
                 mm(T.pX[a:a + 64, s:s + 2], T.CMb[:, 64 * h:64 * h + 64], T.IND[:, 2 * r:2 * r + 2], True, True, ["CMb", "IND"], ["pX"])
-        cp(T.TR[:], T.pT[:], ["pT"], ["TR"])
-        tt(T.CMa[:], T.CQ[:].indirect(T.REP[:]), T.MKa[:], A.mult, ["CQ", "REP", "MKa"], ["CMa"])
-        for n in range(2):
-            for jb in range(4):
-                mm(T.pM[64 * n:64 * n + 64, jb:16:4], T.CMa[:, 64 * jb:64 * jb + 64], T.IND[:, n::2], True, True, ["CMa", "IND"], ["pM"])
 
     def seeker_keys():
         cp(T.NI32[:], T.pX[:, 0:16], ["pX"], ["NI32"])
         ts(T.BD[:], T.NI32[:], 1536, None, A.bitwise_and, None, ["NI32"], ["BD"])
-        cp(T.O16[:, 256:272], T.pM[:, 0:16], ["pM"], ["SL"])
         ts(T.BN0[:, 0::16], T.BD[:], 32.0, 16384 - 9 * LK, A.mult, A.add, ["BD"], ["BN0"])
         tt(T.NF[:], T.BD[:], T.NI32[:], A.subtract, ["BD", "NI32"], ["NF"])
         scan(T.BND[:], T.SMb[:, 0:256], T.BN0[:], A.mult, A.add, ["SMb0", "BN0"], ["BND"])
@@ -502,60 +550,64 @@ def rank_program(g, core, T, topo):
         ts(T.UL[:, 32:160], T.pT[:, 32:160], col["o512"], None, A.subtract, None, ["pT", "c_o512"], ["UL1"])
 
     def hops_v():
-        op("v", lambda: V.tensor_scalar(T.DS[:].indirect(T.O16[:, 256:272]), T.R[:, 0:256], 1.0, -float(NONE), A.mult, A.add), ["R0", "SL"], ["DS"])
+        op("v", lambda: V.tensor_scalar(T.DS[:].indirect(T.O16[:, 256:272]), T.RF[:], 1.0, -float(NONE), A.mult, A.add), ["RF", "SL"], ["DS"])
+
+    def hops_s(x):
+        act(T.D16[:, G * x:G * x + G], T.DS[:, G * x:G * x + G], ["DS"], ["D16%d" % x])
+
+    def hops_t():
+        mm(T.pM[:], T.Id16[:], T.FB16[:], True, False, ["Id16", "FB16"], ["pM"])
+        for x in range(N):
+            for y in range(4):
+                mm(T.pM[:, 128 * x:128 * x + 128], T.SD[:, 3 - y:131 - y], T.D16[:, G * x + 128 * y:G * x + 128 * y + 128], False, False,
+                   ["SD", "D16%d" % x], ["pM"])
 
     def seekers():
-        for x in range(N):
-            act(T.D16[:, G * x:G * x + G], T.DS[:, G * x:G * x + G], ["DS"], ["D16%d" % x])
-            for y in range(4):
-                mm(T.pM[:, 128 * x:128 * x + 128], T.SD[:, 3 - y:131 - y], T.D16[:, G * x + 128 * y:G * x + 128 * y + 128], y == 0, y == 3,
-                   ["SD", "D16%d" % x], ["pM"])
-        act(T.YD[:], T.pM[:], ["pM"], ["YD"])
-        none_sums(False)
-        for x in range(N):
-            mm(T.pY[0:32, 0:128], T.Zq[:, 12 - 4 * x:44 - 4 * x], T.YD[:, 128 * x:128 * x + 128], False, x == N - 1, ["Zq", "YD"], ["pY"])
-        act(T.YfB[0:32, :], T.pY[0:32, 0:128], ["pY", "c_m15"], ["YfB"], func=AF.Relu, bias=T.CF[0:32, 30:31])
+        mm(T.pY[0:32, 0:128], T.Idb[0:32, 0:32], T.Yf[0:32, :], True, False, ["Idb", "Yf"], ["pY"])
+        for l in range(16):
+            mm(T.pY[0:32, 0:128], T.Zs[:, 15 - l:47 - l], T.W[:, 128 * l:128 * l + 128], False, l == 15, ["Zs"] + WK, ["pY"])
+        act(T.YfB[0:32, :], T.pY[0:32, 0:128], ["pY"], ["YfB"])
 
     seeker_names()
     hold_a(0)
+    seeker_turn()
     routes()
     lists()
+    like_v(0, 1)
     seeker_keys()
-    hold_b(0)
+    hold(0, "Hc")
     other_lists()
     for t in range(RO):
         keys(t)
         look_up(t)
-        if t == 0:
-            seekers()
-        if t < N - 1:
-            turn_table(t + 1)
-        if t == RO - 1:
-            mm(T.pM[:], T.Id16[:], T.YD[:], True, False, ["Id16", "YD"], ["pM"])
-            mm(T.pM[:], T.Id16[:], T.FB16[:], False, False, ["Id16", "FB16"], ["pM"])
         decide(t)
         if t < RO - 1:
             hold_a(t + 1)
-        if OH0 < 16:
-            onehot(OH0, 16)
-            kills(t)
-        if t < RO - 1:
+            if t == 1:
+                hops_v()
+            if t == 0:
+                hops_table()
             lists()
-            hold_b(t + 1)
+            hold(t + 1, "Hc")
+            if t == 0:
+                act(T.RF[:], T.R[:, 0:256], ["RX", "RO"], ["RF"])
+            for x in [[], [0], [1, 2], [3]][t]:
+                hops_s(x)
     for x in range(N):
         mm(T.pM[:, 128 * x:128 * x + 128], T.ZD[0:32, 128 * x:128 * x + 128], T.Yf[0:32, :], False, x == N - 1, ["ZD%d" % x, "Yf"], ["pM"])
-    ts(T.OP[:], T.pM[:], float(NONE), None, A.min, None, ["pM"], ["OP"])
-    send(lambda r: T.OP[:, 128 * r:128 * r + 128], lambda r: T.RP[:, 128 * q:128 * q + 128], ["OP"], "RP", "rp", "lp")
     banks = list(zip(others + [q], ["pK", "pT", "pR", "pO"]))
     for y in range(4):
-        act(T.TR16[:, 128 * y:128 * y + 128], T.TR[:, 128 * y:128 * y + 128], ["TR"], ["TR16%d" % y])
+        (act if y else cp)(T.TR16[:, 128 * y:128 * y + 128], T.TR[:, 128 * y:128 * y + 128], ["TR"], ["TR16%d" % y])
+    ts(T.OP[:], T.pM[:], float(NONE), None, A.min, None, ["pM"], ["OP"])
+    send(lambda r: T.OP[:, 128 * r:128 * r + 128], lambda r: T.RP[:, 128 * q:128 * q + 128], ["OP"], "RP", "rp", "lp")
+    for y in range(4):
         for o, bank in banks:
             mm(T[bank][:, 0:128], T.ST[32 * o:32 * o + 32, 3 - y:131 - y], T.TR16[32 * o:32 * o + 32, 128 * y:128 * y + 128], y == 0, y == 3,
                ["ST%d" % o, "TR16%d" % y], [bank])
     for n, (o, bank) in enumerate(banks):
         (act if n % 2 else cp)(T.OY[:, 128 * o:128 * o + 128], T[bank][:, 0:128], [bank], ["OY%d" % o])
     send(lambda r: T.OY[:, 128 * r:128 * r + 128], lambda r: T.RY[:, 128 * q:128 * q + 128], ["OY%d" % r for r in others], "RY", "ry", "ly")
-    for out, own, far, qn in ((T.yp, "OP", "RP", "s"), (T.yt, "OY", "RY", "y")):
+    for out, own, far, qn in ((T.yp, "OP", "RP", "y"), (T.yt, "OY", "RY", "s")):
         for r in [q] + others:
             k = own if r == q else far
             dma(qn, out[32 * r:32 * r + 32, :], T[k][:, 128 * r:128 * r + 128], ["OY%d" % q if k == "OY" else k], ["out%s%d" % (own, r)])

@@ -6,17 +6,17 @@ NONE = N * G
 f32, f16, b16, i32, u16 = "float32", "float16", "bfloat16", "int32", "uint16"
 LK = 65536.0
 W1, W2 = 176, 128
-LCH = [4, 4, 4, 3, 1]
+NB = 2
+GAT = 0
+LCH = [4, 4, 4, 2, 2]
 DCH = [4, 4, 4, 2, 2, 1]
-LCH0 = [1, 1, 2, 4, 4, 3, 1]
-DOFF = 6.0
+LCH0 = [2, 2, 4, 4, 2, 2]
+DOFF = 4.0
 KAT = 0
 EAT = 12
-OHV = 10
-OH3 = 3
-VD = 0
-FS = 4
-HAV = False
+HAT = 4
+OHV = [8, 8, 8, 8, 8]
+OH3 = 7
 
 
 def sb(names, cols, dtype):
@@ -25,20 +25,21 @@ def sb(names, cols, dtype):
 
 SCRATCH = {
     **sb("iA", 1, i32), **sb("CC", 12, i32), **sb("CF", 32, f32), **sb("iB", 4, f32), **sb("OFS", 28, u16),
-    **sb("iX", 176, b16), **sb("SelR", 176, f16), **sb("ONE", 256, b16), **sb("Zq", 48, f16), **sb("Zs", 48, b16), **sb("ST SD", 144, f16),
-    **sb("Id16 Idm NK Dm", 128, f16), **sb("Idb Idn TO Yf YfB BIG", 128, b16), **sb("KS", 64, f16), **sb("ZD", 512, b16),
+    **sb("iX", 176, b16), **sb("SelR", 176, f16), **sb("ONE", 256, b16), **sb("Zq", 48, f16), **sb("Zs", 32, f32), **sb("FX", 128, f32), **sb("ST", 144, f16), **sb("SD", 144, f32),
+    **sb("Id16 Idm Id3 NK Dm", 128, f16), **sb("Idb Idn TO Yf YfB BIG", 128, b16), **sb("KS", 64, f16), **sb("ZD", 512, b16),
     **sb("SM0 Hb DIFF DM SC1", 256, f32), **sb("iC iCa MKa MKb", 256, b16), **sb("BOw CMa CMb Ha Hc", 256, f16),
-    **sb("ZER CKf BND BN0 ELIG LO SEO LOO", 256, b16), **sb("SMb LOS", 512, b16), **sb("LOD", 768, b16), **sb("OT", 512, f16),
+    **sb("ZER CKf BND BN0 ELIG LO SEO LOO", 256, b16), **sb("SMb LOS", 512, b16), **sb("LOD", 768, b16), "OT": ("sbuf", [128, 32, 8], f16),
     **sb("CQ SK NF", 16, f32), **sb("SH", 48, f32), **sb("NI32 BD BI", 16, i32), **sb("XI", 48, i32), **sb("REP", 16, u16),
     **sb("BL", 8, b16), **sb("IND", 8, f16), **sb("R", 1024, f16), **sb("RQ RS", 256, f16), **sb("RF", 256, f32),
     **sb("IN", 352, i32), **sb("TI", 608, i32), **sb("TS", 608, f16), **sb("FB", 512, i32), **sb("FB16 NI YD TR16", 512, f16),
     **sb("X1", N * W1, f16), **sb("X2", N * W2, f16),
-    **sb("UL", 160, u16), **sb("O16", 272, u16), **sb("TR OY OP RY RP", 512, f32),
+    **sb("UL", 160, u16), **sb("O16", 272, u16), **sb("TR", 512, f32),
+    "OS": ("sbuf", [128, N, 256], f16), "OL": ("sbuf", [128, N, 256], f16), "OF": ("sbuf", [128, N, 256], f32),
     **sb("F DS", 2048, f32), **sb("SelF", 512, f16), **sb("W OH", 2048, b16), **sb("E", 4096, b16), **sb("Gd", 4352, b16),
-    **sb("Ta Tb", 32, f32), **sb("GM", 8, f32), **sb("D16", 2048, f16), "TT": ("sbuf", [128, 8, 32], b16),
-    **{n: ("psum", [128, 512], f32) for n in "pK pV pX pY pO pT pR pM".split()},
+    **sb("M32", 256, b16), **sb("GH", 512, f16), **sb("SN", 1024, f32), "TT": ("sbuf", [128, 8, 32], b16),
+    **{n: ("psum", [128, 512], f32) for n in "pK pV pQ pY pO pT pR pM".split()},
 }
-SEMAPHORES = ["cv", "cs", "ct", "cg", "ra", "rb", "rc", "ry", "rp", "la", "lb", "lc", "ly", "lp"] + ["d%d" % i for i in range(56)]
+SEMAPHORES = ["cv", "cs", "ct", "cg", "ra", "rb", "rc", "la", "lb", "lc", "lf"] + ["rf%d" % r for r in range(N)] + ["d%d" % i for i in range(56)]
 
 
 def rank_program(g, core, T, topo):
@@ -58,7 +59,7 @@ def rank_program(g, core, T, topo):
             res[r] = out[n * k:(n + 1) * k]
         for n, r in enumerate(near):
             rest = [e for e in topo.engines(T.cores[a], T.cores[r]) if e not in out]
-            k = len(rest) // len(near)
+            k = len(out) // len(away)
             res[r] = rest[n * k:(n + 1) * k]
         return res
     plans = [plan(r) for r in range(N)]
@@ -161,6 +162,9 @@ def rank_program(g, core, T, topo):
         else:
             op("g", lambda: g.iota(o[:], pat, base, cm, allow_small_or_imprecise_dtypes=True), [], [n])
 
+    def number(o, c, key):
+        op("g", lambda: g.iota(o, [[0, o.shape[1]]], c, 0, allow_small_or_imprecise_dtypes=True), [], [key])
+
     def pick(o, i, pat, base, reads, writes):
         op("g", lambda: g.affine_select(o, i, pat, A.is_equal, 0.0, base, -1), reads, writes)
 
@@ -195,16 +199,15 @@ def rank_program(g, core, T, topo):
         dma("y", T.FB[:, 128 * x:128 * x + 128], T.paths[32 * q:32 * q + 32, G * x:G * x + G], [], ["FB%d" % x])
     FK = ["F%d" % n for n in range(N)]
     WK = ["W%d" % x for x in range(N)]
+    DK = ["DS%d" % x for x in range(N)]
 
     iota("iA", [[0, 1]], 0, 1)
     iota("iB", [[16, 4]])
     iota("iX", [[1, 176]])
-    iota("iC", [[1, 16], [0, 16]])
-    iota("CKf", [[0, 16], [-1, 16]], -17)
     iota("ONE", [[0, 256]], 1)
-    bits = [(0, 15), (0, 3), (2, 3), (0, 127), (5, 3), (6, 1), (4, 3), (4, 7), (4, 1)]
-    names = "k y z pc o n6 hh gg n4".split()
-    col = {n: T.CF[:, i:i + 1] for i, n in enumerate(names + "sw k16 o512 gp tZ eb m17 k0 u v".split())}
+    bits = [(0, 15), (0, 3), (2, 3), (0, 127), (4, 1), (5, 3), (6, 1), (4, 3), (4, 7)]
+    names = "k y z pc n4 o n6 hh gg".split()
+    col = {n: T.CF[:, i:i + 1] for i, n in enumerate(names + "sw k16 o512 gp tZ eb early late tS u".split())}
 
     def parts(a, b):
         for i in range(a, b):
@@ -215,41 +218,30 @@ def rank_program(g, core, T, topo):
         rd = ["c_" + x for x in (i, s1, s2) if isinstance(x, str)]
         ts(col[o], col[i], col.get(s1, s1), col.get(s2, s2), a, b, rd, ["c_" + o])
 
-    parts(0, 4)
+    parts(0, 5)
     num("sw", "y", 4.0, "z", A.mult, A.add)
     num("k16", "k", 16.0, None, A.mult, None)
     ts(T.OFS[:, 0:1], col["k"], 16.0, None, A.add, None, ["c_k"], ["OFc"])
     cp(T.OFS[:, 1:2], col["sw"], ["c_sw"], ["OFd"])
     cp(T.OFS[:, 2:3], col["k"], ["c_k"], ["OFe"])
     ts(T.OFS[:, 12:28], T.iX[:, 0:16], col["k16"], None, A.add, None, ["iX", "c_k16"], ["OFR"])
-    ts(T.OFS[:, 4:12:2], T.iB[:], col["sw"], None, A.add, None, ["iB", "c_sw"], ["OFa"])
-    ts(T.OFS[:, 5:12:2], T.iB[:], col["k"], None, A.add, None, ["iB", "c_k"], ["OFb"])
     ts(T.Id16[:], T.iX[:, 0:128], col["pc"], None, A.is_equal, None, ["iX", "c_pc"], ["Id16"])
 
-    def turn_table(t):
-        for r in range(N):
-            o = (r + t) % N
-            act(T.OT[:, 128 * t + r:128 * t + 128:4], T.Id16[:, 32 * o:32 * o + 32], ["Id16"], ["OT%d_%d" % (t, r)])
-
-    turn_table(0)
     act(T.Idb[:], T.Id16[:], ["Id16"], ["Idb"])
     act(T.NK[:], T.Id16[:], ["Id16"], ["NK"], scale=-32.0)
     act(T.Idm[:], T.Id16[:], ["Id16"], ["Idm"], scale=-1.0)
     act(T.Idn[:], T.Id16[:], ["Id16"], ["Idn"], scale=9.0 * LK)
-    fill(col["m17"], -17.0, "c_m17")
-    act(T.SM0[:], T.CKf[:], ["CKf", "c_m17"], ["SM0"], func=AF.Sign, scale=-1.0, bias=col["m17"])
-    iota("iCa", [[1, 4], [4, 4], [0, 16]])
+    act(T.Id3[:], T.Id16[:], ["Id16"], ["Id3"], scale=-3.0)
 
     def spread_table(y):
         pick(T.SelF[:, 128 * y:128 * y + 128], T.ONE[:, 0:128], [[64, 2], [0, 4], [4, 16]], y, ["ONE"], ["SelF%d" % y])
 
     spread_table(0)
-    parts(4, 9)
+    spread_table(1)
     num("u", "n4", 64.0, "k", A.mult, A.add)
+    ts(T.OFS[:, 4:12:2], T.iB[:], col["sw"], None, A.add, None, ["iB", "c_sw"], ["OFa"])
     ts(T.SelR[:], T.iX[:], -48.0, col["u"], A.add, A.is_equal, ["iX", "c_u"], ["SelR"])
-    num("o512", "o", 512.0, None, A.mult, None)
-    num("gp", "hh", 2.0, "n6", A.mult, A.add)
-    num("tZ", "n6", 16.0, "y", A.mult, A.add)
+    ts(T.OFS[:, 5:12:2], T.iB[:], col["k"], None, A.add, None, ["iB", "c_k"], ["OFb"])
     fill(T.W[:, 0:1024], 0.0, "Wa")
     cp(T.TS[:, 0:128], T.TI[:, 0:128], ["TI1"], ["TS1"])
     for d in (1, 3):
@@ -257,8 +249,9 @@ def rank_program(g, core, T, topo):
     cp(T.TS[:, 176:432], T.TI[:, 176:432], ["TI2", "TI3"], ["TS2"])
     send(lambda r: T.TS[:, min(TAT[(r - q) % N], CAT[(r - q) % N]):min(TAT[(r - q) % N], CAT[(r - q) % N]) + W1],
          lambda r: T.X1[:, W1 * q:W1 * q + W1], ["TS1", "TS2", "TC", "TC3"], "X1", "ra", "la")
-    spread_table(1)
     spread_table(2)
+    spread_table(3)
+    number(T.CF[:, 30:31], 1 - 16 * NONE, "c_all")
     act(T.RQ[:], T.IN[:, 0:256].indirect(T.OFS[:, 12:28]), ["IR", "OFR"], ["RQ"])
     for r in others + [q]:
         need("t", [("ct", cnt.get("ct", 0))])
@@ -270,87 +263,96 @@ def rank_program(g, core, T, topo):
     act(T.R[:, 64 * q:64 * q + 64], T.RS[:, 64 * q:64 * q + 64], ["RS"], ["RO"])
     act(second(q, 0, W2)[0], T.IN[:, 256:320].indirect(T.OFS[:, 4:12]), INK + ["OFa", "OFb"], ["XR"])
     send(lambda r: second(q, 0, W2)[0], lambda r: second(q, 0, W2)[0], ["XR"], "X2", "rc", "lc")
-    spread_table(3)
+    iota("iCa", [[1, 4], [4, 4], [0, 16]])
+    iota("iC", [[1, 16], [0, 16]])
+    pick(T.OT[:], T.ONE[:], [[1, 32], [0, 2], [32, 4]], 0, ["ONE"], ["OT"])
+
+    def scan_mask(h):
+        op("g", lambda: g.affine_select(T.SMb[:, 256 * h:256 * h + 256], T.ONE[:], [[0, 16], [1, 16]], A.not_equal, 0.0, 0, 0), ["ONE"], ["SMb%d" % h])
+
+    scan_mask(0)
     iota("BN0", [[0, 256]])
+    iota("CKf", [[0, 16], [-1, 16]], -17)
+    iota("M32", [[0, 256]], -32)
+    number(col["eb"], int(9 * LK) - 16384 - 16, "c_eb")
     iota("ZER", [[0, 256]])
+    number(T.CF[:, 29:30], -N * NONE, "c_four")
+    for n, (cmp, c) in enumerate([(A.is_gt, -1.0 / 128), (A.not_equal, 0.5)]):
+        op("g", lambda: g.affine_select(T.TT[:], T.TT[:] if n else T.M32[:], [[0, 8], [1, 32]], cmp, c, -15, 0), ["M32", "TT"], ["TT"])
+    pick(T.TT[:], T.TT[:], [[16, 4], [64, 2], [0, 32]], 0, ["TT"], ["TT"])
+    number(T.SH[:, 16:32], 15, "SH1")
     iota("LOD", [[0, 768]], -1)
+    scan_mask(1)
     op("g", lambda: g.affine_select(T.Dm[:], T.Idm[:], [[1, 128]], A.not_equal, 1.0, -1, -1), ["Idm"], ["Dm"])
     op("g", lambda: g.affine_select(T.Dm[:], T.Dm[:], [[200, 128]], A.not_equal, -1.0, -127, 1), ["Dm"], ["Dm"])
-    iota("DS", [[0, 2048]])
+    iota("TO", [[0, 128]], -64)
+    pick(T.TO[:], T.TO[:], [[16, 4], [64, 2], [0, 16]], 0, ["TO"], ["TO"])
+    number(T.CF[:, 28:29], NONE, "c_none")
     iota("BIG", [[0, 128]], 4096)
     for x in range(N):
         pick(T.ZD[0:32, 128 * x:128 * x + 128], T.BIG[0:32, :], [[16, 2], [0, 16], [1, 4]], 4 * x, ["BIG"], ["ZD%d" % x])
     for o in range(N):
         pick(T.ST[32 * o:32 * o + 32, :], T.ONE[32 * o:32 * o + 32, 0:144], [[1, 36], [100, 4]], -300, ["ONE"], ["ST%d" % o])
 
+    parts(5, 9)
+    num("o512", "o", 512.0, None, A.mult, None)
+    num("gp", "hh", 2.0, "n6", A.mult, A.add)
+    num("tZ", "n6", 16.0, "y", A.mult, A.add)
     fill(T.W[:, 1024:2048], 0.0, *WK)
     cp(T.TS[:, 480:608], T.TI[:, 480:608], ["TI0"], ["TS0"])
-    for h in range(2):
-        act(T.SMb[:, 256 * h:256 * h + 256], T.SM0[:], ["SM0"], ["SMb%d" % h])
     ts(T.Zq[:], T.iX[:, 0:48], -12.0, col["tZ"], A.add, A.is_equal, ["iX", "c_tZ"], ["Zq"])
     ts(T.IND[:], T.iX[:, 0:8], col["gg"], None, A.is_equal, None, ["iX", "c_gg"], ["IND"])
-    ts(T.GM[:], T.iX[:, 0:8], col["gp"], None, A.is_equal, None, ["iX", "c_gp"], ["GM"])
-    ts(T.Ta[:], T.iX[:, 0:32], 15.0, -32.0 + 1.0 / 128, A.is_gt, A.mult, ["iX"], ["Ta"])
-    ts(T.Tb[:], T.iX[:, 0:32], 15.0, 0.5 + 1.0 / 128, A.is_equal, A.mult, ["iX"], ["Tb"])
+    ts(T.BL[:], T.iX[:, 0:8], col["gp"], LK, A.is_equal, A.mult, ["iX", "c_gp"], ["BL"])
     ts(T.REP[:], T.iX[:, 0:16], 0.0, col["k"], A.mult, A.add, ["iX", "c_k"], ["REP"])
-    tt(T.Ta[:], T.Ta[:], T.Tb[:], A.add, ["Ta", "Tb"], ["Ta"])
-    ts(T.MKb[:], T.iC[:], col["k"], None, A.is_equal, None, ["iC", "c_k"], ["MKb"])
-    ts(T.Ta[:], T.Ta[:], -1.0 / 128, None, A.add, None, ["Ta"], ["Ta"])
-    num("k0", "k", 0.0, None, A.is_equal, None)
-    ts(T.Tb[:], T.Ta[:], col["k0"], None, A.mult, None, ["Ta", "c_k0"], ["Tb"])
-    for n in range(8):
-        act(T.TT[:, n, :], T.Tb[:], ["Tb", "GM"], ["TT%d" % n], scale=T.GM[:, n:n + 1])
-    TTK = ["TT%d" % n for n in range(8)]
-    act(T.BL[:], T.GM[:], ["GM"], ["BL"], scale=LK)
-    fill(T.CF[:, 30:31], -15.0, "c_m15")
     cp(T.FB16[:], T.FB[:], ["FB%d" % x for x in range(N)], ["FB16"])
-    ts(T.NI[:], T.FB16[:], float(NONE), None, A.is_equal, None, ["FB16"], ["NI"])
 
-    def none_sums(last):
+    def all_none(paths):
         for x in range(N):
-            mm(T.pY[0:32, 0:128], T.Zq[:, 12 - 4 * x:44 - 4 * x], T.NI[:, 128 * x:128 * x + 128], x == 0, last and x == N - 1, ["Zq", "NI"], ["pY"])
+            mm(T.pY[0:32, 0:128], T.Zq[:, 12 - 4 * x:44 - 4 * x], T[paths][:, 128 * x:128 * x + 128], x == 0, x == N - 1, ["Zq", paths], ["pY"])
+
+    def dead_flags(flags):
+        act(T[flags][0:32, :], T.pY[0:32, 0:128], ["pY", "c_all"], [flags], func=AF.Relu, bias=T.CF[0:32, 30:31])
 
     def spread_flags():
         for x in range(N):
             dma("y", T.W[16 * x::64, :], T.Yf[0:32, :], ["Yf", "Wa"], [WK[x]])
 
-    for x, bank in enumerate(["pK", "pV", "pX", "pM"]):
+    def trunks(o, h):
+        src, key = first(o, 0, 0, 128)
+        bank = ["pT", "pR"][h]
+        for x in range(2):
+            mm(T[bank][32 * o:32 * o + 32, 128 * x:128 * x + 128], T.Id16[:, 2 * h + x::4], src, True, True, ["Id16", key], [bank])
+
+    trunks(q, 0)
+    trunks(q, 1)
+    all_none("FB16")
+    dead_flags("Yf")
+    spread_flags()
+    for x, bank in enumerate(["pQ", "pV", "pK", "pM"]):
         for y in range(4):
             mm(T[bank][:, 128 * y:128 * y + 128], T.SelF[:, 128 * y:128 * y + 128], T.FB16[:, 128 * x:128 * x + 128], True, True,
                ["SelF%d" % y, "FB16"], [bank])
-        if x == 0:
-            none_sums(True)
-        if x == 1:
-            act(T.Yf[0:32, :], T.pY[0:32, 0:128], ["pY", "c_m15"], ["Yf"], func=AF.Relu, bias=T.CF[0:32, 30:31])
-        (act if x < FS else cp)(T.F[:, G * x:G * x + G], T[bank][:], [bank], [FK[x]])
-    ts(T.MKa[:], T.iCa[:], col["k"], None, A.is_equal, None, ["iCa", "c_k"], ["MKa"])
-    ts(T.BOw[:, 0:128], T.iC[:, 0:128], col["gg"], None, A.is_equal, None, ["iC", "c_gg"], ["BOw0"])
-    act(T.BOw[:, 128:256], T.BOw[:, 0:128], ["BOw0"], ["BOw1"])
-    num("u", "k0", -64.0, None, A.mult, None)
-    ts(T.TO[:], T.iC[:, 0:128], col["gp"], col["u"], A.is_equal, A.mult, ["iC", "c_gp", "c_u"], ["TO"])
-    num("u", "n6", 16.0, 15.0, A.mult, A.add)
-    num("v", "k", 1.0, -1.0, A.is_equal, A.mult)
-    ts(T.Zs[:], T.iX[:, 0:48], col["u"], col["v"], A.is_equal, A.mult, ["iX", "c_u", "c_v"], ["Zs"])
-    fill(T.SH[:, 16:32], 15.0, "SH1")
-    fill(T.SH[:, 32:32 + OHV], 127.0, "SH2")
-    if OHV < 16:
-        fill(T.SH[:, 32 + OHV:48], 127.5, "SH3")
-    fill(col["eb"], 9 * LK - 16384 - 16, "c_eb")
+        act(T.F[:, G * x:G * x + G], T[bank][:], [bank], [FK[x]])
+    fill(T.SH[:, 32:48], 127.5, "SH2")
+
+    def name_masks():
+        ts(T.MKa[:], T.iCa[:], col["k"], None, A.is_equal, None, ["iCa", "c_k"], ["MKa"])
+        ts(T.MKb[:], T.iC[:], col["k"], None, A.is_equal, None, ["iC", "c_k"], ["MKb"])
+        for h in range(2):
+            ts(T.BOw[:, 128 * h:128 * h + 128], T.iC[:, 0:128], col["gg"], None, A.is_equal, None, ["iC", "c_gg"], ["BOw%d" % h])
 
     def hops_table():
         num("u", "n6", 64.0, 3.0, A.mult, A.add)
-        num("v", "k", float(RO), None, A.is_lt, None)
+        num("early", "k", float(RO), None, A.is_lt, None)
         num("u", "k", 4.0, "u", A.mult, A.add)
-        ts(T.SD[:], T.iX[:, 0:144], col["u"], col["v"], A.is_equal, A.mult, ["iX", "c_u", "c_v"], ["SD"])
+        num("late", "k", float(RO), float(NONE), A.is_ge, A.mult)
+        num("tS", "n6", 16.0, "k", A.mult, A.add)
+        ts(T.SD[:], T.iX[:, 0:144], col["u"], None, A.is_equal, None, ["iX", "c_u"], ["SD"])
+        ts(T.Zs[:], T.iX[:, 0:32], col["tS"], None, A.is_equal, None, ["iX", "c_tS"], ["Zs"])
 
+    hops_table()
+    name_masks()
     mine = T.Id16[:, 32 * q:32 * q + 32]
-
-    def trunks(o):
-        src, key = first(o, 0, 0, 128)
-        for x in range(4):
-            mm(T.pT[32 * o:32 * o + 32, 128 * x:128 * x + 128], T.Id16[:, x::4], src, True, True, ["Id16", key], ["pT"])
-
-    trunks(q)
     for r in [q] + others:
         src, key = first(r, 1, 0, 48)
         mm(T.pO[32 * r:32 * r + 32, 0:48], mine, src, True, True, ["Id16", key], ["pO"])
@@ -360,16 +362,17 @@ def rank_program(g, core, T, topo):
     def routes():
         act(T.R[:, 256:512], T.R[:, 0:256], ["RX", "RO"], ["R1"])
         act(T.R[:, 512:1024], T.R[:, 0:512], ["RX", "RO", "R1"], ["R2", "R3"])
+        if NB:
+            mm(T.pQ[:, 0:256 * NB], T.Id16[:], T.R[:, 0:256 * NB], True, True, ["Id16", "RX", "RO", "R1"], ["pQ"])
 
     def hold_a(t):
         L, lk = ul(t, 0)
         for h, way in enumerate([cp, act]):
-            way(T.Ha[:, 128 * h:128 * h + 128], T.TR[:].indirect(T.UL[:, 32 * t + 8 * h:32 * t + 8 * h + 8]), ["TR", lk], ["Ha%d" % h])
+            way(T.Ha[:, 128 * h:128 * h + 128], T.TR[:].indirect(T.UL[:, 32 * t + 8 * h:32 * t + 8 * h + 8]), ["TR", "TRa", lk], ["Ha%d" % h])
         for jb in range(4):
             for n in range(2):
-                a = 128 * (t % N) + 64 * n
-                mm(T.pO[64 * n:64 * n + 64, jb:256:4], T.Ha[:, 64 * jb:64 * jb + 64], T.OT[:, a:a + 64], True, True,
-                   ["Ha%d" % (jb // 2)] + ["OT%d_%d" % (t % N, r) for r in range(N)], ["pO"])
+                mm(T.pO[64 * n:64 * n + 64, jb:256:4], T.Ha[:, 64 * jb:64 * jb + 64], T.OT[:, 16 * n:16 * n + 16, t % N:t % N + N], True, True,
+                   ["Ha%d" % (jb // 2), "OT"], ["pO"])
 
     def lists():
         cp(T.O16[:, 0:256], T.pO[:, 0:256], ["pO"], ["O16"])
@@ -399,9 +402,11 @@ def rank_program(g, core, T, topo):
 
     def keys_s():
         act(T.ELIG[:], T.pR[:, 256:512], ["pR", "c_eb"], ["ELIG"], func=AF.Sign, bias=col["eb"])
-        act(T.DIFF[:], T.pR[:, 0:256], ["pR"], ["DIFF"])
 
     def like_v(a, b):
+        if a >= 16 - NB:
+            u, w = 256 * (a - 16 + NB), 256 * (b - 16 + NB)
+            return tt(T.E[:, 256 * a:256 * b], T.GH[:, u:w], T.pQ[:, u:w], A.is_equal, ["GH", "pQ"], ["E%d" % p for p in range(a, b)])
         tt(T.E[:, 256 * a:256 * b], T.F[:].indirect(T.O16[:, 16 * a:16 * b]), T.R[:, 0:256 * (b - a)], A.is_equal,
            FK + ["O16", "RX", "RO"] + ["R%d" % n for n in range(1, b - a)], ["E%d" % p for p in range(a, b)])
 
@@ -419,90 +424,84 @@ def rank_program(g, core, T, topo):
             p = e
         return res
 
-    def dead(qn, a, b):
-        win = T.W[:].indirect(T.O16[:, 16 * a:16 * b])
-        rd, wr = WK + ["O16", "SL"], ["Gd%d" % p for p in range(a, b)]
-        (act if qn == "s" else cp)(T.Gd[:, 256 * a:256 * b], win, rd, wr)
+    def dead(way, a, b, keys_):
+        way(T.Gd[:, 16 * a:16 * b], T.W[:].indirect(T.O16[:, a:b]), WK + ["O16", "SL"], keys_)
 
-    def dead_t(p, last):
+    def dead_t(p, keys_, last):
         for b in range(2):
             w = T.TT[:, :, 15 - p:31 - p] if p < 16 else T.TO[:]
             mm(T.pV[:, 128 * b:128 * b + 128], T.Gd[:, 256 * p + 128 * b:256 * p + 128 * b + 128], w, False, b == 1 and last,
-               ["Gd%d" % p, "TO"] + TTK, ["pV"])
+               keys_ + ["TT" if p < 16 else "TO"], ["pV"])
 
     def look_up(t):
-        lc, dc = chunks(LCH if t else LCH0, 16), chunks(DCH, 17 if t else 16)
-        ds, dv = dc[:len(dc) - VD], dc[len(dc) - VD:]
+        lc, ds = chunks(LCH if t else LCH0, 16), chunks(DCH, 17 if t else 16)
         for n, c in enumerate(ds):
-            if n == (KAT if t else 1):
+            if NB and n == (GAT if t else 1):
+                act(T.GH[:, 0:256 * NB], T.F[:].indirect(T.O16[:, 256 - 16 * NB:256]), FK + ["O16"], ["GH"])
+            if n == (KAT if t else 2):
                 keys_s()
-            if t == 0 and n == 2:
-                seekers()
-            dead("s", *c)
+            dead(act, 16 * c[0], 16 * c[1], ["Gd%d" % p for p in range(*c)])
         for n, c in enumerate(lc):
             if t or n:
                 like_v(*c)
             if t == 0 and n == 2:
                 other_lists_v()
-        for c in dv:
-            dead("v", *c)
-        turns = [(b, 0, a, b) for a, b in lc] + [(b + DOFF, 1, a, b) for a, b in ds] + [(99 + b, 1, a, b) for a, b in dv]
-        turns.sort()
-        end = [x for x in turns if x[1]][-1]
-        for x in turns:
-            if x[2] == 4 and not x[1] and t == RO - 1:
-                hops_t()
+        for x in sorted([(b, 0, a, b) for a, b in lc] + [(b + DOFF, 1, a, b) for a, b in ds]):
+            if t and not x[1] and x[2] == HAT:
+                hops_t(t - 1)
+            if t == 0 and x[2] == 8 and not x[1]:
+                seekers()
             if x[2] == EAT and not x[1]:
                 mm(T.pK[:, 0:256], T.Idn[:], T.ELIG[:], False, False, ["Idn", "ELIG"], ["pK"])
             for p in range(x[2], x[3]):
                 if x[1]:
-                    dead_t(p, x == end and p == x[3] - 1)
+                    dead_t(p, ["Gd%d" % p], p == ds[-1][1] - 1)
                 else:
                     like_t(p)
 
-    def onehot(a, b):
+    def onehot(way, a, b):
         for c in range(a, b):
             o, low = T.OH[:, 128 * c:128 * c + 128], T.LOD[:, 512 + 16 * c:513 + 16 * c]
-            if c < OHV:
-                ts(o, T.iX[:, 0:128], low, None, A.is_equal, None, ["iX", "LOD"], ["OH%d" % c])
+            if way is ts:
+                ts(o, T.iX[:, 0:128], 0.5, low, A.add, A.is_equal, ["iX", "LOD"], ["OH%d" % c])
             else:
                 act(o, T.iX[:, 1:129], ["iX", "LOD"], ["OH%d" % c], func=AF.Sign, scale=-1.0, bias=low)
 
     def decide(t):
-        scan(T.SC1[:], T.SM0[:], T.pK[:, 0:256], A.mult, A.max, ["SM0", "pK"], ["SC1"])
+        scan(T.SC1[:], T.SMb[:, 0:256], T.pK[:, 0:256], A.mult, A.max, ["SMb0", "pK"], ["SC1"])
         tt(T.BI[:], T.SC1[:, 15::16], T.SK[:], A.max, ["SC1", "SK"], ["BI"])
         for n, (sh, m) in enumerate([(12, 15), (0, 31), (5, 127)]):
             ts(T.XI[:, 16 * n:16 * n + 16], T.BI[:], sh, m, A.logical_shift_right, A.bitwise_and, ["BI"], ["XI%d" % n])
-        tt(T.LOD[:, 0::16], T.SH[:], T.XI[:], A.subtract, ["SH0", "SH1", "SH2", "SH3", "XI0", "XI1", "XI2"], ["LOD"])
+        tt(T.LOD[:, 0::16], T.SH[:], T.XI[:], A.subtract, ["SH0", "SH1", "SH2", "XI0", "XI1", "XI2"], ["LOD"])
         scan(T.LOS[:], T.SMb[:], T.LOD[:, 0:512], A.mult, A.add, ["SMb0", "SMb1", "LOD"], ["LOS"])
-        onehot(OHV, 16)
-        hold(t, "Hb")
-        if t < N - 1:
-            turn_table(t + 1)
-        onehot(0, 1)
+        act(T.DIFF[:], T.pR[:, 0:256], ["pR"], ["DIFF"])
+        nv = OHV[t]
+        onehot(act, nv, 16)
+        onehot(ts, 0, 1)
         ts(T.LO[:], T.LOS[:, 256:512], 0.0, 0.25, A.not_equal, A.mult, ["LOS"], ["LO"])
-        onehot(1, OHV - OH3)
-        tt(T.SEO[:], T.pV[:, 0:256], T.LO[:], A.is_ge, ["pV", "LO"], ["SEO"])
+        onehot(ts, 1, nv - OH3)
+        tt(T.SEO[:], T.pV[:, 0:256], T.LO[:], A.is_lt, ["pV", "LO"], ["SEO"])
         for a, b, c, d in pieces(t):
             mm(T.pT[c:c + 32, d:d + 64], T.SEO[a:a + 64, b:b + 32], T.Idb[a:a + 64, a:a + 64], True, True, ["SEO", "Idb"], ["pT"])
         tt(T.LOO[:], T.pV[:, 0:256], T.LOS[:, 0:256], A.is_equal, ["pV", "LOS"], ["LOO"])
-        onehot(OHV - OH3, OHV)
+        onehot(ts, nv - OH3, nv)
         kills(t)
         tt(T.DM[:], T.pT[:, 0:256], T.DIFF[:], A.mult, ["pT", "DIFF"], ["DM"])
         L, lk = ul(t, 1)
-        tt(T.TR[:].indirect(L), T.Hb[:], T.DM[:], A.add, ["Hb", "DM", lk], ["TR"])
+        u = t % N
+        tt(T.TR[:].indirect(L), T.SN[:, 256 * u:256 * u + 256], T.DM[:], A.subtract, ["SN%da" % u, "SN%db" % u, "DM", lk], ["TR"])
 
     def kills(t):
-        kinds = [x for x in (range(OHV, 16), range(OHV)) if len(x)]
+        kinds = [x for x in (range(OHV[t], 16), range(OHV[t])) if len(x)]
         for kind in kinds:
             for n in range(2):
                 col0, ss = 16 * n + (32 if kind[0] else 0), [s for s in kind if s % 2 == n]
                 for s in ss:
-                    mm(T.pX[:, col0:col0 + 16], T.OH[:, 128 * s:128 * s + 128], T.LOO[:, 16 * s:16 * s + 16], s == ss[0], s == ss[-1],
-                       ["LOO", "OH%d" % s], ["pX"])
+                    mm(T.pO[:, 256 + col0:272 + col0], T.OH[:, 128 * s:128 * s + 128], T.LOO[:, 16 * s:16 * s + 16], s == ss[0], s == ss[-1],
+                       ["LOO", "OH%d" % s], ["pO"])
         y = "Yf" if t else "YfB"
         mm(T.pY[0:32, 0:128], T.Idb[0:32, 0:32], T[y][0:32, :], True, False, ["Idb", y], ["pY"])
-        act(T.KS[:, 0:32 * len(kinds)], T.pX[:, 0:32 * len(kinds)], ["pX"], ["KS"])
+        act(T.KS[:, 0:32 * len(kinds)], T.pO[:, 256:256 + 32 * len(kinds)], ["pO"], ["KS"])
         if len(kinds) > 1:
             mm(T.pY[0:32, 0:128], T.KS[:, 32:64], T.Dm[:], False, False, ["Dm", "KS"], ["pY"])
         mm(T.pY[0:32, 0:128], T.KS[:, 0:32], T.Id16[:], False, True, ["Id16", "KS"], ["pY"])
@@ -512,27 +511,27 @@ def rank_program(g, core, T, topo):
 
     def seeker_names():
         tt(T.CMa[:], T.CQ[:].indirect(T.REP[:]), T.MKa[:], A.mult, ["CQ", "REP", "MKa"], ["CMa"])
-        trunks(others[0])
-        trunks(others[1])
+        for h in range(2):
+            for o in others:
+                trunks(o, h)
+        act(T.TR[:, 0:256], T.pT[:, 0:256], ["pT"], ["TRa"])
+        cp(T.TR[:, 256:512], T.pR[:, 0:256], ["pR"], ["TR"])
         for n in range(2):
             for jb in range(4):
                 mm(T.pY[64 * n:64 * n + 64, jb:16:4], T.CMa[:, 64 * jb:64 * jb + 64], T.IND[:, n::2], True, True, ["CMa", "IND"], ["pY"])
-        trunks(others[2])
-        act(T.TR[:], T.pT[:], ["pT"], ["TR"])
+        hold_a(0)
         tt(T.CMb[:], T.CQ[:].indirect(T.REP[:]), T.MKb[:], A.mult, ["CQ", "REP", "MKb"], ["CMb"])
-        cp(T.O16[:, 256:272], T.pY[:, 0:16], ["pY"], ["SL"])
-        cp(T.W[:].indirect(T.O16[:, 256:272]), T.ONE[:], ["SL", "ONE"], WK + ["Wa"])
-        spread_flags()
-
-    def seeker_turn():
+        lists()
         for r in range(N):
             for h in range(4):
                 a, s = 64 * (r % 2), 8 * (r // 2) + 2 * h
-                mm(T.pX[a:a + 64, s:s + 2], T.CMb[:, 64 * h:64 * h + 64], T.IND[:, 2 * r:2 * r + 2], True, True, ["CMb", "IND"], ["pX"])
+                mm(T.pT[a:a + 64, s:s + 2], T.CMb[:, 64 * h:64 * h + 64], T.IND[:, 2 * r:2 * r + 2], True, True, ["CMb", "IND"], ["pT"])
 
     def seeker_keys():
-        cp(T.NI32[:], T.pX[:, 0:16], ["pX"], ["NI32"])
+        cp(T.NI32[:], T.pT[:, 0:16], ["pT"], ["NI32"])
+        cp(T.O16[:, 256:272], T.pY[:, 0:16], ["pY"], ["SL"])
         ts(T.BD[:], T.NI32[:], 1536, None, A.bitwise_and, None, ["NI32"], ["BD"])
+        hops_v()
         ts(T.BN0[:, 0::16], T.BD[:], 32.0, 16384 - 9 * LK, A.mult, A.add, ["BD"], ["BN0"])
         tt(T.NF[:], T.BD[:], T.NI32[:], A.subtract, ["BD", "NI32"], ["NF"])
         scan(T.BND[:], T.SMb[:, 0:256], T.BN0[:], A.mult, A.add, ["SMb0", "BN0"], ["BND"])
@@ -550,32 +549,35 @@ def rank_program(g, core, T, topo):
         ts(T.UL[:, 32:160], T.pT[:, 32:160], col["o512"], None, A.subtract, None, ["pT", "c_o512"], ["UL1"])
 
     def hops_v():
-        op("v", lambda: V.tensor_scalar(T.DS[:].indirect(T.O16[:, 256:272]), T.RF[:], 1.0, -float(NONE), A.mult, A.add), ["RF", "SL"], ["DS"])
+        cp(T.F[:].indirect(T.O16[:, 256:272]), T.RF[:], ["RF", "SL"], FK)
+        dma("y", T.FX[:], T.F[0::16, :], FK, ["FX"])
 
-    def hops_s(x):
-        act(T.D16[:, G * x:G * x + G], T.DS[:, G * x:G * x + G], ["DS"], ["D16%d" % x])
+    def hops_t(x):
+        if x == 0:
+            mm(T.pM[:], T.Id3[:], T.FB16[:], True, False, ["Id3", "FB16"], ["pM"])
+        for y in range(4):
+            mm(T.pM[:, 128 * x:128 * x + 128], T.SD[:, 3 - y:131 - y], T.F[:, G * x + 128 * y:G * x + 128 * y + 128], False, False,
+               ["SD"] + FK, ["pM"])
 
-    def hops_t():
-        mm(T.pM[:], T.Id16[:], T.FB16[:], True, False, ["Id16", "FB16"], ["pM"])
-        for x in range(N):
-            for y in range(4):
-                mm(T.pM[:, 128 * x:128 * x + 128], T.SD[:, 3 - y:131 - y], T.D16[:, G * x + 128 * y:G * x + 128 * y + 128], False, False,
-                   ["SD", "D16%d" % x], ["pM"])
+    def names_h():
+        mm(T.pR[:, 0:256], T.BOw[:, 0:128], T.CMb[:], True, True, ["BOw0", "CMb"], ["pR"])
+        act(T.SN[:, 0:256], T.pR[:, 0:256], ["pR"], ["SN0a", "SN0b"])
+        for t in range(1, N):
+            dma("y", T.SN[32 * t:128, 256 * t:256 * t + 256], T.SN[0:128 - 32 * t, 0:256], ["SN0a"], ["SN%da" % t])
+            dma("y", T.SN[0:32 * t, 256 * t:256 * t + 256], T.SN[128 - 32 * t:128, 0:256], ["SN0a"], ["SN%db" % t])
 
     def seekers():
-        mm(T.pY[0:32, 0:128], T.Idb[0:32, 0:32], T.Yf[0:32, :], True, False, ["Idb", "Yf"], ["pY"])
-        for l in range(16):
-            mm(T.pY[0:32, 0:128], T.Zs[:, 15 - l:47 - l], T.W[:, 128 * l:128 * l + 128], False, l == 15, ["Zs"] + WK, ["pY"])
-        act(T.YfB[0:32, :], T.pY[0:32, 0:128], ["pY"], ["YfB"])
+        mm(T.pY[0:32, 0:128], T.Zs[:], T.FX[:], True, False, ["Zs", "FX"], ["pY"])
+        mm(T.pY[0:32, 0:128], T.Idb[0:32, 0:32], T.Yf[0:32, :], False, True, ["Idb", "Yf"], ["pY"])
+        act(T.YfB[0:32, :], T.pY[0:32, 0:128], ["pY", "c_four"], ["YfB"], func=AF.Relu, bias=T.CF[0:32, 29:30])
 
     seeker_names()
-    hold_a(0)
-    seeker_turn()
     routes()
-    lists()
-    like_v(0, 1)
-    seeker_keys()
+    like_v(0, 2)
+    act(T.RF[:], T.R[:, 0:256], ["RX", "RO", "c_early", "c_late"], ["RF"], func=AF.Identity, scale=col["early"], bias=col["late"])
     hold(0, "Hc")
+    seeker_keys()
+    names_h()
     other_lists()
     for t in range(RO):
         keys(t)
@@ -583,32 +585,30 @@ def rank_program(g, core, T, topo):
         decide(t)
         if t < RO - 1:
             hold_a(t + 1)
-            if t == 1:
-                hops_v()
-            if t == 0:
-                hops_table()
             lists()
             hold(t + 1, "Hc")
-            if t == 0:
-                act(T.RF[:], T.R[:, 0:256], ["RX", "RO"], ["RF"])
-            for x in [[], [0], [1, 2], [3]][t]:
-                hops_s(x)
     for x in range(N):
         mm(T.pM[:, 128 * x:128 * x + 128], T.ZD[0:32, 128 * x:128 * x + 128], T.Yf[0:32, :], False, x == N - 1, ["ZD%d" % x, "Yf"], ["pM"])
     banks = list(zip(others + [q], ["pK", "pT", "pR", "pO"]))
     for y in range(4):
-        (act if y else cp)(T.TR16[:, 128 * y:128 * y + 128], T.TR[:, 128 * y:128 * y + 128], ["TR"], ["TR16%d" % y])
-    ts(T.OP[:], T.pM[:], float(NONE), None, A.min, None, ["pM"], ["OP"])
-    send(lambda r: T.OP[:, 128 * r:128 * r + 128], lambda r: T.RP[:, 128 * q:128 * q + 128], ["OP"], "RP", "rp", "lp")
+        cp(T.TR16[:, 128 * y:128 * y + 128], T.TR[:, 128 * y:128 * y + 128], ["TR"], ["TR16%d" % y])
+    act(T.OS[:, :, 128:256], T.pM[:], ["pM", "c_none"], ["OP"], func=AF.Relu, scale=-1.0, bias=T.CF[:, 28:29])
     for y in range(4):
         for o, bank in banks:
             mm(T[bank][:, 0:128], T.ST[32 * o:32 * o + 32, 3 - y:131 - y], T.TR16[32 * o:32 * o + 32, 128 * y:128 * y + 128], y == 0, y == 3,
                ["ST%d" % o, "TR16%d" % y], [bank])
     for n, (o, bank) in enumerate(banks):
-        (act if n % 2 else cp)(T.OY[:, 128 * o:128 * o + 128], T[bank][:, 0:128], [bank], ["OY%d" % o])
-    send(lambda r: T.OY[:, 128 * r:128 * r + 128], lambda r: T.RY[:, 128 * q:128 * q + 128], ["OY%d" % r for r in others], "RY", "ry", "ly")
-    for out, own, far, qn in ((T.yp, "OP", "RP", "y"), (T.yt, "OY", "RY", "s")):
-        for r in [q] + others:
-            k = own if r == q else far
-            dma(qn, out[32 * r:32 * r + 32, :], T[k][:, 128 * r:128 * r + 128], ["OY%d" % q if k == "OY" else k], ["out%s%d" % (own, r)])
+        (act if n == 1 else cp)(T.OS[:, o, 0:128], T[bank][:, 0:128], [bank], ["OY%d" % o])
+    send(lambda r: T.OS[:, r, :], lambda r: T.OL[:, q, :], ["OP"] + ["OY%d" % r for r in others], "OL", "rf%d" % q, "lf")
+    del total["rf%d" % q]
+    near = [r for r in others if T.cores[r] in topo.cores_of(core)]
+    for n, r in enumerate([q] + near + [r for r in others if r not in near]):
+        if r != q:
+            total["rf%d" % r] = len(plans[r][q])
+            lastw["OL"] = [("remote", "rf%d" % r, total["rf%d" % r], True)]
+        src, keys_ = (T.OS, ["OP", "OY%d" % q]) if r == q else (T.OL, ["OL"])
+        cp(T.OF[:, r, 0:128], src[:, r, 0:128], keys_, ["OFy%d" % r])
+        act(T.OF[:, r, 128:256], src[:, r, 128:256], keys_ + ["c_none"], ["OFp%d" % r], func=AF.Identity, scale=-1.0, bias=T.CF[:, 28:29])
+        dma("y", T.yt[32 * r:32 * r + 32, :], T.OF[:, r, 0:128], ["OFy%d" % r], ["yt%d" % r])
+        dma("s", T.yp[32 * r:32 * r + 32, :], T.OF[:, r, 128:256], ["OFp%d" % r], ["yp%d" % r])
     need("g", [(s, v) for s, v in total.items()])

@@ -6,17 +6,19 @@ NONE = N * G
 f32, f16, b16, i32, u16 = "float32", "float16", "bfloat16", "int32", "uint16"
 LK = 65536.0
 W1, W2 = 176, 128
-NB = 2
-GAT = 0
-LCH = [4, 4, 4, 2, 2]
-DCH = [4, 4, 4, 2, 2, 1]
-LCH0 = [2, 2, 4, 4, 2, 2]
-DOFF = 4.0
-KAT = 0
-EAT = 12
-HAT = 4
+DEAD = 32768.0
+PLAN = [(0, 0, 4, 0)] + [(4, 2, 3, 1)] * 4
+CUTS = [0, 8, 10, 12, 14, 16]
+MQ = "yyyy"
+FV = (1,)
+SB = 2
+SHARES = [[], [0], [1], [2, 3], []]
+DOFF = 1.0
+SAT = 1
+HAV = 0
+GC, CC = 1.56, 1.0
 OHV = [8, 8, 8, 8, 8]
-OH3 = 7
+OH3 = 6
 
 
 def sb(names, cols, dtype):
@@ -25,21 +27,22 @@ def sb(names, cols, dtype):
 
 SCRATCH = {
     **sb("iA", 1, i32), **sb("CC", 12, i32), **sb("CF", 32, f32), **sb("iB", 4, f32), **sb("OFS", 28, u16),
-    **sb("iX", 176, b16), **sb("SelR", 176, f16), **sb("ONE", 256, b16), **sb("Zq", 48, f16), **sb("Zs", 32, f32), **sb("FX", 128, f32), **sb("ST", 144, f16), **sb("SD", 144, f32),
-    **sb("Id16 Idm Id3 NK Dm", 128, f16), **sb("Idb Idn TO Yf YfB BIG", 128, b16), **sb("KS", 64, f16), **sb("ZD", 512, b16),
+    **sb("iX", 176, b16), **sb("SelR", 176, f16), **sb("ONE", 256, b16), **sb("Zq Z15", 48, f16), **sb("Zs Id32", 32, f32),
+    **sb("FX NA NB", 128, f32), **sb("ST SD", 144, f16), **sb("F16", 2048, f16),
+    **sb("Id16 Idm Id3 IdS Idk NK Dm TO Yf YfB", 128, f16), **sb("Idb Idn Yz BIG", 128, b16), **sb("KS", 64, f16), **sb("ZD", 512, b16),
     **sb("SM0 Hb DIFF DM SC1", 256, f32), **sb("iC iCa MKa MKb", 256, b16), **sb("BOw CMa CMb Ha Hc", 256, f16),
-    **sb("ZER CKf BND BN0 ELIG LO SEO LOO", 256, b16), **sb("SMb LOS", 512, b16), **sb("LOD", 768, b16), "OT": ("sbuf", [128, 32, 8], f16),
+    **sb("ZER", 128, b16), **sb("SIX CKf BND BN0 ELIG LO SEO LOO", 256, b16), **sb("SMb LOS", 512, b16), **sb("LOD", 768, b16), "OT": ("sbuf", [128, 32, 8], f16),
     **sb("CQ SK NF", 16, f32), **sb("SH", 48, f32), **sb("NI32 BD BI", 16, i32), **sb("XI", 48, i32), **sb("REP", 16, u16),
     **sb("BL", 8, b16), **sb("IND", 8, f16), **sb("R", 1024, f16), **sb("RQ RS", 256, f16), **sb("RF", 256, f32),
     **sb("IN", 352, i32), **sb("TI", 608, i32), **sb("TS", 608, f16), **sb("FB", 512, i32), **sb("FB16 NI YD TR16", 512, f16),
     **sb("X1", N * W1, f16), **sb("X2", N * W2, f16),
-    **sb("UL", 160, u16), **sb("O16", 272, u16), **sb("TR", 512, f32),
+    **sb("UL", 160, u16), **sb("O16", 272, u16), **sb("TR RN", 512, f32),
     "OS": ("sbuf", [128, N, 256], f16), "OL": ("sbuf", [128, N, 256], f16), "OF": ("sbuf", [128, N, 256], f32),
-    **sb("F DS", 2048, f32), **sb("SelF", 512, f16), **sb("W OH", 2048, b16), **sb("E", 4096, b16), **sb("Gd", 4352, b16),
-    **sb("M32", 256, b16), **sb("GH", 512, f16), **sb("SN", 1024, f32), "TT": ("sbuf", [128, 8, 32], b16),
+    **sb("F FO", 2048, f32), **sb("SelF", 512, f16), **sb("OH", 2048, b16), **sb("E", 4096, b16), **sb("GH GO", 4352, f16),
+    **sb("SN", 1024, f32), "TT": ("sbuf", [128, 8, 32], f16),
     **{n: ("psum", [128, 512], f32) for n in "pK pV pQ pY pO pT pR pM".split()},
 }
-SEMAPHORES = ["cv", "cs", "ct", "cg", "ra", "rb", "rc", "la", "lb", "lc", "lf"] + ["rf%d" % r for r in range(N)] + ["d%d" % i for i in range(56)]
+SEMAPHORES = ["cv", "cs", "ct", "cg", "ra", "rb", "rc", "la", "lb", "lc", "lf"] + ["rf%d" % r for r in range(N)] + ["d%d" % i for i in range(60)]
 
 
 def rank_program(g, core, T, topo):
@@ -199,15 +202,14 @@ def rank_program(g, core, T, topo):
         dma("y", T.FB[:, 128 * x:128 * x + 128], T.paths[32 * q:32 * q + 32, G * x:G * x + G], [], ["FB%d" % x])
     FK = ["F%d" % n for n in range(N)]
     WK = ["W%d" % x for x in range(N)]
-    DK = ["DS%d" % x for x in range(N)]
 
     iota("iA", [[0, 1]], 0, 1)
     iota("iB", [[16, 4]])
     iota("iX", [[1, 176]])
     iota("ONE", [[0, 256]], 1)
-    bits = [(0, 15), (0, 3), (2, 3), (0, 127), (4, 1), (5, 3), (6, 1), (4, 3), (4, 7)]
-    names = "k y z pc n4 o n6 hh gg".split()
-    col = {n: T.CF[:, i:i + 1] for i, n in enumerate(names + "sw k16 o512 gp tZ eb early late tS u".split())}
+    bits = [(0, 15), (0, 3), (2, 3), (0, 127), (4, 1), (5, 3), (6, 1), (4, 3), (4, 7), (2, 15)]
+    names = "k y z pc n4 o n6 hh gg kk".split()
+    col = {n: T.CF[:, i:i + 1] for i, n in enumerate(names + "sw k16 o512 gp tZ eb early late tS u v gs gb rs m3 up dn".split())}
 
     def parts(a, b):
         for i in range(a, b):
@@ -231,7 +233,8 @@ def rank_program(g, core, T, topo):
     act(T.NK[:], T.Id16[:], ["Id16"], ["NK"], scale=-32.0)
     act(T.Idm[:], T.Id16[:], ["Id16"], ["Idm"], scale=-1.0)
     act(T.Idn[:], T.Id16[:], ["Id16"], ["Idn"], scale=9.0 * LK)
-    act(T.Id3[:], T.Id16[:], ["Id16"], ["Id3"], scale=-3.0)
+    act(T.Idk[:], T.Id16[:], ["Id16"], ["Idk"], scale=-DEAD)
+    act(T.Id32[:], T.Id16[:, 0:32], ["Id16"], ["Id32"])
 
     def spread_table(y):
         pick(T.SelF[:, 128 * y:128 * y + 128], T.ONE[:, 0:128], [[64, 2], [0, 4], [4, 16]], y, ["ONE"], ["SelF%d" % y])
@@ -242,7 +245,6 @@ def rank_program(g, core, T, topo):
     ts(T.OFS[:, 4:12:2], T.iB[:], col["sw"], None, A.add, None, ["iB", "c_sw"], ["OFa"])
     ts(T.SelR[:], T.iX[:], -48.0, col["u"], A.add, A.is_equal, ["iX", "c_u"], ["SelR"])
     ts(T.OFS[:, 5:12:2], T.iB[:], col["k"], None, A.add, None, ["iB", "c_k"], ["OFb"])
-    fill(T.W[:, 0:1024], 0.0, "Wa")
     cp(T.TS[:, 0:128], T.TI[:, 0:128], ["TI1"], ["TS1"])
     for d in (1, 3):
         cp(T.TS[:, CAT[d]:CAT[d] + 48], T.IN[:, 320:352].indirect(T.OFS[:, 0:3]), ["IC", "IL0", "OFc", "OFd", "OFe"], ["TC" if d == 1 else "TC3"])
@@ -252,6 +254,8 @@ def rank_program(g, core, T, topo):
     spread_table(2)
     spread_table(3)
     number(T.CF[:, 30:31], 1 - 16 * NONE, "c_all")
+    number(T.CF[:, 31:32], int(DEAD), "c_dead")
+    iota("iC", [[1, 16], [0, 16]])
     act(T.RQ[:], T.IN[:, 0:256].indirect(T.OFS[:, 12:28]), ["IR", "OFR"], ["RQ"])
     for r in others + [q]:
         need("t", [("ct", cnt.get("ct", 0))])
@@ -264,7 +268,6 @@ def rank_program(g, core, T, topo):
     act(second(q, 0, W2)[0], T.IN[:, 256:320].indirect(T.OFS[:, 4:12]), INK + ["OFa", "OFb"], ["XR"])
     send(lambda r: second(q, 0, W2)[0], lambda r: second(q, 0, W2)[0], ["XR"], "X2", "rc", "lc")
     iota("iCa", [[1, 4], [4, 4], [0, 16]])
-    iota("iC", [[1, 16], [0, 16]])
     pick(T.OT[:], T.ONE[:], [[1, 32], [0, 2], [32, 4]], 0, ["ONE"], ["OT"])
 
     def scan_mask(h):
@@ -273,20 +276,21 @@ def rank_program(g, core, T, topo):
     scan_mask(0)
     iota("BN0", [[0, 256]])
     iota("CKf", [[0, 16], [-1, 16]], -17)
-    iota("M32", [[0, 256]], -32)
     number(col["eb"], int(9 * LK) - 16384 - 16, "c_eb")
-    iota("ZER", [[0, 256]])
+    iota("SIX", [[0, 256]], 6)
     number(T.CF[:, 29:30], -N * NONE, "c_four")
-    for n, (cmp, c) in enumerate([(A.is_gt, -1.0 / 128), (A.not_equal, 0.5)]):
-        op("g", lambda: g.affine_select(T.TT[:], T.TT[:] if n else T.M32[:], [[0, 8], [1, 32]], cmp, c, -15, 0), ["M32", "TT"], ["TT"])
-    pick(T.TT[:], T.TT[:], [[16, 4], [64, 2], [0, 32]], 0, ["TT"], ["TT"])
+    for n, (step, cmp, c) in enumerate([(-1, A.is_ge, -17.0), (1, A.is_ge, -1.0), (1, A.not_equal, 16.0)]):
+        op("g", lambda: g.affine_select(T.TT[:], T.TT[:] if n else T.ONE[:], [[0, 8], [step, 32]], cmp, c / 2048, -15 * step, 0), ["ONE", "TT"], ["TT"])
+    pick(T.TT[:], T.TT[:], [[16, 4], [64, 2], [0, 32]], 15, ["TT"], ["TT"])
     number(T.SH[:, 16:32], 15, "SH1")
     iota("LOD", [[0, 768]], -1)
     scan_mask(1)
-    op("g", lambda: g.affine_select(T.Dm[:], T.Idm[:], [[1, 128]], A.not_equal, 1.0, -1, -1), ["Idm"], ["Dm"])
-    op("g", lambda: g.affine_select(T.Dm[:], T.Dm[:], [[200, 128]], A.not_equal, -1.0, -127, 1), ["Dm"], ["Dm"])
-    iota("TO", [[0, 128]], -64)
-    pick(T.TO[:], T.TO[:], [[16, 4], [64, 2], [0, 16]], 0, ["TO"], ["TO"])
+    iota("ZER", [[0, 128]])
+    op("g", lambda: g.affine_select(T.Dm[:], T.ZER[:, 0:128], [[1, 128]], A.not_equal, DEAD, 0, -1), ["ZER"], ["Dm"])
+    op("g", lambda: g.affine_select(T.Dm[:], T.Dm[:], [[1, 128]], A.not_equal, -DEAD, -1, -1), ["Dm"], ["Dm"])
+    op("g", lambda: g.affine_select(T.Dm[:], T.Dm[:], [[200, 128]], A.not_equal, DEAD, -127, 1), ["Dm"], ["Dm"])
+    op("g", lambda: g.affine_select(T.TO[:], T.ZER[:, 0:128], [[16, 4], [64, 2], [0, 16]], A.not_equal, -32.0 / 2048, 15, -1), ["ZER"], ["TO"])
+    number(T.CF[:, 27:28], 1, "c_one")
     number(T.CF[:, 28:29], NONE, "c_none")
     iota("BIG", [[0, 128]], 4096)
     for x in range(N):
@@ -294,13 +298,21 @@ def rank_program(g, core, T, topo):
     for o in range(N):
         pick(T.ST[32 * o:32 * o + 32, :], T.ONE[32 * o:32 * o + 32, 0:144], [[1, 36], [100, 4]], -300, ["ONE"], ["ST%d" % o])
 
-    parts(5, 9)
+    parts(5, 10)
     num("o512", "o", 512.0, None, A.mult, None)
     num("gp", "hh", 2.0, "n6", A.mult, A.add)
     num("tZ", "n6", 16.0, "y", A.mult, A.add)
-    fill(T.W[:, 1024:2048], 0.0, *WK)
+    num("v", "kk", 15.0, -1.0 / 64, A.is_equal, A.mult)
+    num("m3", "kk", 15.0, 4.0, A.is_equal, A.mult)
+    num("gb", "k", 15.0, DEAD, A.is_equal, A.mult)
+    num("gs", "k", 15.0, -2.0, A.is_equal, A.mult)
+    num("rs", "k", 15.0, 1.0 / 64 - 1, A.is_equal, A.mult)
+    num("m3", "m3", -3.0, None, A.add, None)
+    num("gs", "gs", 1.0, None, A.add, None)
+    num("rs", "rs", 1.0, None, A.add, None)
     cp(T.TS[:, 480:608], T.TI[:, 480:608], ["TI0"], ["TS0"])
     ts(T.Zq[:], T.iX[:, 0:48], -12.0, col["tZ"], A.add, A.is_equal, ["iX", "c_tZ"], ["Zq"])
+    ts(T.Z15[:], T.Zq[:], col["v"], None, A.mult, None, ["Zq", "c_v"], ["Z15"])
     ts(T.IND[:], T.iX[:, 0:8], col["gg"], None, A.is_equal, None, ["iX", "c_gg"], ["IND"])
     ts(T.BL[:], T.iX[:, 0:8], col["gp"], LK, A.is_equal, A.mult, ["iX", "c_gp"], ["BL"])
     ts(T.REP[:], T.iX[:, 0:16], 0.0, col["k"], A.mult, A.add, ["iX", "c_k"], ["REP"])
@@ -313,9 +325,15 @@ def rank_program(g, core, T, topo):
     def dead_flags(flags):
         act(T[flags][0:32, :], T.pY[0:32, 0:128], ["pY", "c_all"], [flags], func=AF.Relu, bias=T.CF[0:32, 30:31])
 
-    def spread_flags():
+    def marks(flags, out):
         for x in range(N):
-            dma("y", T.W[16 * x::64, :], T.Yf[0:32, :], ["Yf", "Wa"], [WK[x]])
+            mm(T.pY[0:32, 0:128], T.Z15[:, 12 - 4 * x:44 - 4 * x], T.FB16[:, 128 * x:128 * x + 128], x == 0, False, ["Z15", "FB16"], ["pY"])
+        mm(T.pY[0:32, 0:128], T.Idk[0:32, 0:32], T[flags][0:32, :], False, True, ["Idk", flags], ["pY"])
+        act(T[out][0:32, :], T.pY[0:32, 0:128], ["pY", "c_dead"], [out], func=AF.Relu, bias=T.CF[0:32, 31:32])
+
+    def spread_marks():
+        for x in range(N):
+            dma(MQ[x], T.F[16 * x + 15::64, :], T.NA[0:32, :], ["NA"] + FK, [WK[x]])
 
     def trunks(o, h):
         src, key = first(o, 0, 0, 128)
@@ -323,17 +341,30 @@ def rank_program(g, core, T, topo):
         for x in range(2):
             mm(T[bank][32 * o:32 * o + 32, 128 * x:128 * x + 128], T.Id16[:, 2 * h + x::4], src, True, True, ["Id16", key], [bank])
 
+    num("u", "n6", 64.0, 3.0, A.mult, A.add)
+    num("early", "k", float(RO), None, A.is_lt, None)
+    num("u", "k", 4.0, "u", A.mult, A.add)
+    num("late", "k", float(RO), float(NONE), A.is_ge, A.mult)
+    num("v", "k", 15.0, None, A.is_lt, None)
+    num("tS", "n6", 16.0, "k", A.mult, A.add)
+    num("late", "late", "v", None, A.mult, None)
+    ts(T.SD[:], T.iX[:, 0:144], col["u"], col["v"], A.is_equal, A.mult, ["iX", "c_u", "c_v"], ["SD"])
+    ts(T.Id3[:], T.Id16[:], col["m3"], None, A.mult, None, ["Id16", "c_m3"], ["Id3"])
+    ts(T.Zs[:], T.iX[:, 0:32], col["tS"], None, A.is_equal, None, ["iX", "c_tS"], ["Zs"])
+    ts(T.IdS[:], T.Id16[:], col["rs"], None, A.mult, None, ["Id16", "c_rs"], ["IdS"])
+    fill(T.SH[:, 32:48], 127.5, "SH2")
     trunks(q, 0)
     trunks(q, 1)
     all_none("FB16")
     dead_flags("Yf")
-    spread_flags()
     for x, bank in enumerate(["pQ", "pV", "pK", "pM"]):
         for y in range(4):
             mm(T[bank][:, 128 * y:128 * y + 128], T.SelF[:, 128 * y:128 * y + 128], T.FB16[:, 128 * x:128 * x + 128], True, True,
                ["SelF%d" % y, "FB16"], [bank])
-        act(T.F[:, G * x:G * x + G], T[bank][:], [bank], [FK[x]])
-    fill(T.SH[:, 32:48], 127.5, "SH2")
+        if x == 1:
+            marks("Yf", "NA")
+        (cp if x in FV else act)(T.F[:, G * x:G * x + G], T[bank][:], [bank], [FK[x]])
+    spread_marks()
 
     def name_masks():
         ts(T.MKa[:], T.iCa[:], col["k"], None, A.is_equal, None, ["iCa", "c_k"], ["MKa"])
@@ -341,16 +372,6 @@ def rank_program(g, core, T, topo):
         for h in range(2):
             ts(T.BOw[:, 128 * h:128 * h + 128], T.iC[:, 0:128], col["gg"], None, A.is_equal, None, ["iC", "c_gg"], ["BOw%d" % h])
 
-    def hops_table():
-        num("u", "n6", 64.0, 3.0, A.mult, A.add)
-        num("early", "k", float(RO), None, A.is_lt, None)
-        num("u", "k", 4.0, "u", A.mult, A.add)
-        num("late", "k", float(RO), float(NONE), A.is_ge, A.mult)
-        num("tS", "n6", 16.0, "k", A.mult, A.add)
-        ts(T.SD[:], T.iX[:, 0:144], col["u"], None, A.is_equal, None, ["iX", "c_u"], ["SD"])
-        ts(T.Zs[:], T.iX[:, 0:32], col["tS"], None, A.is_equal, None, ["iX", "c_tS"], ["Zs"])
-
-    hops_table()
     name_masks()
     mine = T.Id16[:, 32 * q:32 * q + 32]
     for r in [q] + others:
@@ -361,13 +382,11 @@ def rank_program(g, core, T, topo):
 
     def routes():
         act(T.R[:, 256:512], T.R[:, 0:256], ["RX", "RO"], ["R1"])
-        act(T.R[:, 512:1024], T.R[:, 0:512], ["RX", "RO", "R1"], ["R2", "R3"])
-        if NB:
-            mm(T.pQ[:, 0:256 * NB], T.Id16[:], T.R[:, 0:256 * NB], True, True, ["Id16", "RX", "RO", "R1"], ["pQ"])
+        mm(T.pQ[:], T.IdS[:], T.R[:, 0:512], True, True, ["IdS", "RX", "RO", "R1"], ["pQ"])
 
     def hold_a(t):
         L, lk = ul(t, 0)
-        for h, way in enumerate([cp, act]):
+        for h, way in enumerate([cp, cp if HAV and t else act]):
             way(T.Ha[:, 128 * h:128 * h + 128], T.TR[:].indirect(T.UL[:, 32 * t + 8 * h:32 * t + 8 * h + 8]), ["TR", "TRa", lk], ["Ha%d" % h])
         for jb in range(4):
             for n in range(2):
@@ -398,66 +417,111 @@ def rank_program(g, core, T, topo):
         mm(T.pK[:, 0:256], T.Idb[:], T.CKf[:], False, False, ["Idb", "CKf"], ["pK"])
         for a, b, c, d in pieces(t):
             mm(T.pK[a:a + 64, b:b + 32], T.Hc[:, d:d + 64], T.NK[:, c:c + 32], False, False, ["Hc", "NK"], ["pK"])
-        mm(T.pV[:, 0:256], T.Idb[:], T.ZER[:], True, False, ["Idb", "ZER"], ["pV"])
+        mm(T.pV[:, 0:256], T.Idb[:], T.SIX[:], True, False, ["Idb", "SIX"], ["pV"])
 
     def keys_s():
         act(T.ELIG[:], T.pR[:, 256:512], ["pR", "c_eb"], ["ELIG"], func=AF.Sign, bias=col["eb"])
 
-    def like_v(a, b):
-        if a >= 16 - NB:
-            u, w = 256 * (a - 16 + NB), 256 * (b - 16 + NB)
-            return tt(T.E[:, 256 * a:256 * b], T.GH[:, u:w], T.pQ[:, u:w], A.is_equal, ["GH", "pQ"], ["E%d" % p for p in range(a, b)])
-        tt(T.E[:, 256 * a:256 * b], T.F[:].indirect(T.O16[:, 16 * a:16 * b]), T.R[:, 0:256 * (b - a)], A.is_equal,
-           FK + ["O16", "RX", "RO"] + ["R%d" % n for n in range(1, b - a)], ["E%d" % p for p in range(a, b)])
+    def gather(way, a, b, old):
+        o, win = T[["GH", "GO"][old]][:, 256 * a:256 * b], T[["F", "FO"][old]][:].indirect(T.O16[:, 16 * a:16 * b])
+        rd = (["FO%d" % x for x in range(N)] if old else FK + WK) + ["O16", "SL", "c_gs", "c_gb"]
+        wr = ["G%s%d" % ("O" * old, p) for p in range(a, b)]
+        if way is act:
+            act(o, win, rd, wr, func=AF.Identity, scale=col["gs"], bias=col["gb"])
+        else:
+            ts(o, win, col["gs"], col["gb"], A.mult, A.add, rd, wr)
 
-    def like_t(p):
+    def like_v(a, b, old):
+        tt(T.E[:, 256 * a:256 * b], T[["GH", "GO"][old]][:, 256 * a:256 * b], T.pQ[:, 0:256 * (b - a)], A.is_equal,
+           ["pQ"] + ["G%s%d" % ("O" * old, p) for p in range(a, b)], ["E%d" % p for p in range(a, b)])
+
+    def like_t(p, last):
         for b in range(2):
-            mm(T.pK[:, 128 * b + p:128 * b + 128:16], T.E[:, 256 * p + 128 * b:256 * p + 128 * b + 128], T.BL[:], False, p == 15 and b == 1,
+            mm(T.pK[:, 128 * b + p:128 * b + 128:16], T.E[:, 256 * p + 128 * b:256 * p + 128 * b + 128], T.BL[:], False, last and b == 1,
                ["E%d" % p, "BL"], ["pK"])
 
-    def chunks(sizes, end):
-        res, p = [], 0
-        for n in sizes:
-            e = min(p + n, end)
-            if e > p:
-                res.append((p, e))
-            p = e
-        return res
-
-    def dead(way, a, b, keys_):
-        way(T.Gd[:, 16 * a:16 * b], T.W[:].indirect(T.O16[:, a:b]), WK + ["O16", "SL"], keys_)
-
-    def dead_t(p, keys_, last):
+    def dead_t(p, last):
         for b in range(2):
             w = T.TT[:, :, 15 - p:31 - p] if p < 16 else T.TO[:]
-            mm(T.pV[:, 128 * b:128 * b + 128], T.Gd[:, 256 * p + 128 * b:256 * p + 128 * b + 128], w, False, b == 1 and last,
-               keys_ + ["TT" if p < 16 else "TO"], ["pV"])
+            mm(T.pV[:, 128 * b:128 * b + 128], T.GH[:, 256 * p + 128 * b:256 * p + 128 * b + 128], w, False, b == 1 and last,
+               ["G%d" % p, "TT" if p < 16 else "TO"], ["pV"])
+
+    def pairs(a, b):
+        return [(c, min(c + 2, b)) for c in range(a, b, 2)]
 
     def look_up(t):
-        lc, ds = chunks(LCH if t else LCH0, 16), chunks(DCH, 17 if t else 16)
-        for n, c in enumerate(ds):
-            if NB and n == (GAT if t else 1):
-                act(T.GH[:, 0:256 * NB], T.F[:].indirect(T.O16[:, 256 - 16 * NB:256]), FK + ["O16"], ["GH"])
-            if n == (KAT if t else 2):
+        ev, es, nv, vd = PLAN[t]
+        early = ev + es
+        turns, ready, clock = [], {}, {act: 0.0, ts: 0.0}
+
+        def fetch(way, c, old):
+            gather(way, c[0], c[1], old)
+            clock[way] += GC * (c[1] - c[0])
+            ready[c] = clock[way]
+            if not old:
+                turns.append((clock[way] + DOFF, 1, c))
+
+        def compare(c, old):
+            like_v(c[0], c[1], old)
+            clock[ts] = max(clock[ts], ready[c]) + CC * (c[1] - c[0])
+            turns.append((clock[ts], 0, c))
+
+        for c in pairs(ev, early):
+            fetch(act, c, True)
+        if t:
+            keys_s()
+        for a, b in pairs(0, ev):
+            tt(T.E[:, 256 * a:256 * b], T.FO[:].indirect(T.O16[:, 16 * a:16 * b]), T.RN[:, 0:256 * (b - a)], A.is_equal,
+               ["FO%d" % x for x in range(N)] + ["O16", "RN"], ["E%d" % p for p in range(a, b)])
+            clock[ts] += 2 * CC * (b - a)
+            turns.append((clock[ts], 0, (a, b)))
+        for c in pairs(ev, early):
+            compare(c, True)
+        clock[act] = clock[ts] = max(clock[act], clock[ts])
+        mine_v, mine_s = pairs(early, early + nv), pairs(early + nv, 15) + [(15, 16)]
+        for n, c in enumerate(mine_s):
+            if n == 0:
+                for d in mine_v:
+                    fetch(ts, d, False)
+            if t == 0 and n == SB:
                 keys_s()
-            dead(act, 16 * c[0], 16 * c[1], ["Gd%d" % p for p in range(*c)])
-        for n, c in enumerate(lc):
-            if t or n:
-                like_v(*c)
+            fetch(act, c, False)
+        for c in pairs(vd, early) + [(16, 17)] * (t > 0):
+            fetch(act, c, False)
+        for n, c in enumerate(mine_v + mine_s):
+            compare(c, False)
             if t == 0 and n == 2:
                 other_lists_v()
-        for x in sorted([(b, 0, a, b) for a, b in lc] + [(b + DOFF, 1, a, b) for a, b in ds]):
-            if t and not x[1] and x[2] == HAT:
-                hops_t(t - 1)
-            if t == 0 and x[2] == 8 and not x[1]:
-                seekers()
-            if x[2] == EAT and not x[1]:
+        turns.sort()
+        ends = [[x for x in turns if x[1] == kind][-1] for kind in (0, 1)]
+        for n, x in enumerate(turns):
+            if n == 2:
+                for y in SHARES[t - 1]:
+                    hops_t(y)
+            if n == 8:
                 mm(T.pK[:, 0:256], T.Idn[:], T.ELIG[:], False, False, ["Idn", "ELIG"], ["pK"])
-            for p in range(x[2], x[3]):
-                if x[1]:
-                    dead_t(p, ["Gd%d" % p], p == ds[-1][1] - 1)
-                else:
-                    like_t(p)
+            if n == 12 and t == 0:
+                seekers()
+            if x == ends[1] and vd:
+                late.append(x[2])
+                continue
+            for p in range(*x[2]):
+                (dead_t if x[1] else like_t)(p, x in ends and p == x[2][1] - 1)
+
+    late = []
+
+    def piece(t, n):
+        if PLAN[t][3]:
+            a, b = CUTS[n:n + 2]
+            ts(T.GH[:, 16 * a:16 * b], T.F[:].indirect(T.O16[:, a:b]), col["gs"], col["gb"], A.mult, A.add,
+               FK + WK + ["O16", "c_gs", "c_gb"], ["G0" if b == 16 else "Gp%d" % n])
+            if b == 16:
+                need("t", [("cv", cnt["cv"])])
+                for p in [0] + list(range(*late[-1])):
+                    dead_t(p, p == late[-1][1] - 1)
+
+    def whole():
+        ts(T.pV[:, 0:256], T.pV[:, 0:256], 1.5 * 2 ** 27, -1.5 * 2 ** 27, A.add, A.add, ["pV"], ["pV"])
 
     def onehot(way, a, b):
         for c in range(a, b):
@@ -468,23 +532,33 @@ def rank_program(g, core, T, topo):
                 act(o, T.iX[:, 1:129], ["iX", "LOD"], ["OH%d" % c], func=AF.Sign, scale=-1.0, bias=low)
 
     def decide(t):
+        piece(t, 0)
         scan(T.SC1[:], T.SMb[:, 0:256], T.pK[:, 0:256], A.mult, A.max, ["SMb0", "pK"], ["SC1"])
+        piece(t, 1)
         tt(T.BI[:], T.SC1[:, 15::16], T.SK[:], A.max, ["SC1", "SK"], ["BI"])
+        piece(t, 2)
         for n, (sh, m) in enumerate([(12, 15), (0, 31), (5, 127)]):
             ts(T.XI[:, 16 * n:16 * n + 16], T.BI[:], sh, m, A.logical_shift_right, A.bitwise_and, ["BI"], ["XI%d" % n])
+        piece(t, 3)
         tt(T.LOD[:, 0::16], T.SH[:], T.XI[:], A.subtract, ["SH0", "SH1", "SH2", "XI0", "XI1", "XI2"], ["LOD"])
+        piece(t, 4)
         scan(T.LOS[:], T.SMb[:], T.LOD[:, 0:512], A.mult, A.add, ["SMb0", "SMb1", "LOD"], ["LOS"])
         act(T.DIFF[:], T.pR[:, 0:256], ["pR"], ["DIFF"])
         nv = OHV[t]
         onehot(act, nv, 16)
+        for x in SHARES[t][:SAT]:
+            hops_s(x)
         onehot(ts, 0, 1)
-        ts(T.LO[:], T.LOS[:, 256:512], 0.0, 0.25, A.not_equal, A.mult, ["LOS"], ["LO"])
+        ts(T.LO[:], T.LOS[:, 256:512], 0.0, 14.0, A.not_equal, A.mult, ["LOS"], ["LO"])
         onehot(ts, 1, nv - OH3)
         tt(T.SEO[:], T.pV[:, 0:256], T.LO[:], A.is_lt, ["pV", "LO"], ["SEO"])
         for a, b, c, d in pieces(t):
             mm(T.pT[c:c + 32, d:d + 64], T.SEO[a:a + 64, b:b + 32], T.Idb[a:a + 64, a:a + 64], True, True, ["SEO", "Idb"], ["pT"])
+        whole()
+        onehot(ts, nv - OH3, nv - OH3 + 2)
+        need("v", [("cv", cnt["cv"] - 2)])
         tt(T.LOO[:], T.pV[:, 0:256], T.LOS[:, 0:256], A.is_equal, ["pV", "LOS"], ["LOO"])
-        onehot(ts, nv - OH3, nv)
+        onehot(ts, nv - OH3 + 2, nv)
         kills(t)
         tt(T.DM[:], T.pT[:, 0:256], T.DIFF[:], A.mult, ["pT", "DIFF"], ["DM"])
         L, lk = ul(t, 1)
@@ -499,33 +573,35 @@ def rank_program(g, core, T, topo):
                 for s in ss:
                     mm(T.pO[:, 256 + col0:272 + col0], T.OH[:, 128 * s:128 * s + 128], T.LOO[:, 16 * s:16 * s + 16], s == ss[0], s == ss[-1],
                        ["LOO", "OH%d" % s], ["pO"])
-        y = "Yf" if t else "YfB"
-        mm(T.pY[0:32, 0:128], T.Idb[0:32, 0:32], T[y][0:32, :], True, False, ["Idb", y], ["pY"])
+        y = "NA" if t else "NB"
+        mm(T.pY[0:32, 0:128], T.Id32[0:32, :], T[y][0:32, :], True, False, ["Id32", y], ["pY"])
         act(T.KS[:, 0:32 * len(kinds)], T.pO[:, 256:256 + 32 * len(kinds)], ["pO"], ["KS"])
         if len(kinds) > 1:
             mm(T.pY[0:32, 0:128], T.KS[:, 32:64], T.Dm[:], False, False, ["Dm", "KS"], ["pY"])
-        mm(T.pY[0:32, 0:128], T.KS[:, 0:32], T.Id16[:], False, True, ["Id16", "KS"], ["pY"])
-        act(T.Yf[0:32, :], T.pY[0:32, 0:128], ["pY"], ["Yf"], func=AF.Sign)
+        mm(T.pY[0:32, 0:128], T.KS[:, 0:32], T.Idk[:], False, True, ["Idk", "KS"], ["pY"])
         if t < RO - 1:
-            spread_flags()
+            act(T.NA[0:32, :], T.pY[0:32, 0:128], ["pY"], ["NA"], func=AF.Relu)
+            spread_marks()
+        else:
+            act(T.Yz[0:32, :], T.pY[0:32, 0:128], ["pY", "c_one"], ["Yz"], func=AF.Relu, scale=-1.0, bias=T.CF[0:32, 27:28])
 
     def seeker_names():
-        tt(T.CMa[:], T.CQ[:].indirect(T.REP[:]), T.MKa[:], A.mult, ["CQ", "REP", "MKa"], ["CMa"])
+        tt(T.CMb[:], T.CQ[:].indirect(T.REP[:]), T.MKb[:], A.mult, ["CQ", "REP", "MKb"], ["CMb"])
         for h in range(2):
             for o in others:
                 trunks(o, h)
         act(T.TR[:, 0:256], T.pT[:, 0:256], ["pT"], ["TRa"])
         cp(T.TR[:, 256:512], T.pR[:, 0:256], ["pR"], ["TR"])
-        for n in range(2):
-            for jb in range(4):
-                mm(T.pY[64 * n:64 * n + 64, jb:16:4], T.CMa[:, 64 * jb:64 * jb + 64], T.IND[:, n::2], True, True, ["CMa", "IND"], ["pY"])
-        hold_a(0)
-        tt(T.CMb[:], T.CQ[:].indirect(T.REP[:]), T.MKb[:], A.mult, ["CQ", "REP", "MKb"], ["CMb"])
-        lists()
         for r in range(N):
             for h in range(4):
                 a, s = 64 * (r % 2), 8 * (r // 2) + 2 * h
                 mm(T.pT[a:a + 64, s:s + 2], T.CMb[:, 64 * h:64 * h + 64], T.IND[:, 2 * r:2 * r + 2], True, True, ["CMb", "IND"], ["pT"])
+        hold_a(0)
+        tt(T.CMa[:], T.CQ[:].indirect(T.REP[:]), T.MKa[:], A.mult, ["CQ", "REP", "MKa"], ["CMa"])
+        lists()
+        for n in range(2):
+            for jb in range(4):
+                mm(T.pY[64 * n:64 * n + 64, jb:16:4], T.CMa[:, 64 * jb:64 * jb + 64], T.IND[:, n::2], True, True, ["CMa", "IND"], ["pY"])
 
     def seeker_keys():
         cp(T.NI32[:], T.pT[:, 0:16], ["pT"], ["NI32"])
@@ -549,46 +625,64 @@ def rank_program(g, core, T, topo):
         ts(T.UL[:, 32:160], T.pT[:, 32:160], col["o512"], None, A.subtract, None, ["pT", "c_o512"], ["UL1"])
 
     def hops_v():
-        cp(T.F[:].indirect(T.O16[:, 256:272]), T.RF[:], ["RF", "SL"], FK)
+        cp(T.F[:].indirect(T.O16[:, 256:272]), T.RF[:], ["RF", "SL"], FK + WK)
         dma("y", T.FX[:], T.F[0::16, :], FK, ["FX"])
 
     def hops_t(x):
         if x == 0:
             mm(T.pM[:], T.Id3[:], T.FB16[:], True, False, ["Id3", "FB16"], ["pM"])
         for y in range(4):
-            mm(T.pM[:, 128 * x:128 * x + 128], T.SD[:, 3 - y:131 - y], T.F[:, G * x + 128 * y:G * x + 128 * y + 128], False, False,
-               ["SD"] + FK, ["pM"])
+            mm(T.pM[:, 128 * x:128 * x + 128], T.SD[:, 3 - y:131 - y], T.F16[:, G * x + 128 * y:G * x + 128 * y + 128], False, False,
+               ["SD", "F16%d" % x], ["pM"])
+
+    def hops_s(x):
+        act(T.F16[:, G * x:G * x + G], T.FO[:, G * x:G * x + G], ["FO%d" % x], ["F16%d" % x])
 
     def names_h():
-        mm(T.pR[:, 0:256], T.BOw[:, 0:128], T.CMb[:], True, True, ["BOw0", "CMb"], ["pR"])
-        act(T.SN[:, 0:256], T.pR[:, 0:256], ["pR"], ["SN0a", "SN0b"])
+        mm(T.pM[:, 0:256], T.BOw[:, 0:128], T.CMb[:], True, True, ["BOw0", "CMb"], ["pM"])
+
+    def names_s():
+        act(T.SN[:, 0:256], T.pM[:, 0:256], ["pM"], ["SN0a", "SN0b"])
         for t in range(1, N):
             dma("y", T.SN[32 * t:128, 256 * t:256 * t + 256], T.SN[0:128 - 32 * t, 0:256], ["SN0a"], ["SN%da" % t])
             dma("y", T.SN[0:32 * t, 256 * t:256 * t + 256], T.SN[128 - 32 * t:128, 0:256], ["SN0a"], ["SN%db" % t])
 
+    def copy_paths():
+        for x in range(N):
+            dma("y", T.FO[:, G * x:G * x + G], T.F[:, G * x:G * x + G], FK + WK, ["FO%d" % x])
+
     def seekers():
         mm(T.pY[0:32, 0:128], T.Zs[:], T.FX[:], True, False, ["Zs", "FX"], ["pY"])
-        mm(T.pY[0:32, 0:128], T.Idb[0:32, 0:32], T.Yf[0:32, :], False, True, ["Idb", "Yf"], ["pY"])
+        mm(T.pY[0:32, 0:128], T.Id16[0:32, 0:32], T.Yf[0:32, :], False, True, ["Id16", "Yf"], ["pY"])
+
+    def seekers_marks():
         act(T.YfB[0:32, :], T.pY[0:32, 0:128], ["pY", "c_four"], ["YfB"], func=AF.Relu, bias=T.CF[0:32, 29:30])
+        marks("YfB", "NB")
+        act(T.RN[:], T.pQ[:], ["pQ", "c_gs", "c_gb"], ["RN"], func=AF.Identity, scale=col["gs"], bias=col["gb"])
 
     seeker_names()
     routes()
-    like_v(0, 2)
     act(T.RF[:], T.R[:, 0:256], ["RX", "RO", "c_early", "c_late"], ["RF"], func=AF.Identity, scale=col["early"], bias=col["late"])
     hold(0, "Hc")
-    seeker_keys()
     names_h()
+    seeker_keys()
+    names_s()
+    copy_paths()
     other_lists()
     for t in range(RO):
         keys(t)
         look_up(t)
+        if t == 0:
+            seekers_marks()
         decide(t)
         if t < RO - 1:
             hold_a(t + 1)
             lists()
             hold(t + 1, "Hc")
+            for x in SHARES[t][SAT:]:
+                hops_s(x)
     for x in range(N):
-        mm(T.pM[:, 128 * x:128 * x + 128], T.ZD[0:32, 128 * x:128 * x + 128], T.Yf[0:32, :], False, x == N - 1, ["ZD%d" % x, "Yf"], ["pM"])
+        mm(T.pM[:, 128 * x:128 * x + 128], T.ZD[0:32, 128 * x:128 * x + 128], T.Yz[0:32, :], False, x == N - 1, ["ZD%d" % x, "Yz"], ["pM"])
     banks = list(zip(others + [q], ["pK", "pT", "pR", "pO"]))
     for y in range(4):
         cp(T.TR16[:, 128 * y:128 * y + 128], T.TR[:, 128 * y:128 * y + 128], ["TR"], ["TR16%d" % y])

from concourse.bass import DstId, RemoteDMATransfer
from concourse.mybir import AluOpType as A, ActivationFunctionType as AF

N, G, C, K, RO = 4, 512, 2048, 256, 5
NONE = N * G
f32, f16, b16, i32, u16 = "float32", "float16", "bfloat16", "int32", "uint16"
LK = 65536.0
W1, W2 = 176, 128
DEAD = 32768.0
PLAN = [(0, 0, 4, 0)] + [(4, 2, 3, 1)] * 4
CUTS = [0, 8, 10, 12, 14, 16]
MQ = "yyyy"
FV = (1,)
SB = 2
SHARES = [[], [0], [1], [2, 3], []]
DOFF = 1.0
SAT = 1
HAV = 0
GC, CC = 1.56, 1.0
OHV = [8, 8, 8, 8, 8]
OH3 = 6


def sb(names, cols, dtype):
    return {n: ("sbuf", [128, cols], dtype) for n in names.split()}


SCRATCH = {
    **sb("iA", 1, i32), **sb("CC", 12, i32), **sb("CF", 32, f32), **sb("iB", 4, f32), **sb("OFS", 28, u16),
    **sb("iX", 176, b16), **sb("SelR", 176, f16), **sb("ONE", 256, b16), **sb("Zq Z15", 48, f16), **sb("Zs Id32", 32, f32),
    **sb("FX NA NB", 128, f32), **sb("ST SD", 144, f16), **sb("F16", 2048, f16),
    **sb("Id16 Idm Id3 IdS Idk NK Dm TO Yf YfB", 128, f16), **sb("Idb Idn Yz BIG", 128, b16), **sb("KS", 64, f16), **sb("ZD", 512, b16),
    **sb("SM0 Hb DIFF DM SC1", 256, f32), **sb("iC iCa MKa MKb", 256, b16), **sb("BOw CMa CMb Ha Hc", 256, f16),
    **sb("ZER", 128, b16), **sb("SIX CKf BND BN0 ELIG LO SEO LOO", 256, b16), **sb("SMb LOS", 512, b16), **sb("LOD", 768, b16), "OT": ("sbuf", [128, 32, 8], f16),
    **sb("CQ SK NF", 16, f32), **sb("SH", 48, f32), **sb("NI32 BD BI", 16, i32), **sb("XI", 48, i32), **sb("REP", 16, u16),
    **sb("BL", 8, b16), **sb("IND", 8, f16), **sb("R", 1024, f16), **sb("RQ RS", 256, f16), **sb("RF", 256, f32),
    **sb("IN", 352, i32), **sb("TI", 608, i32), **sb("TS", 608, f16), **sb("FB", 512, i32), **sb("FB16 NI YD TR16", 512, f16),
    **sb("X1", N * W1, f16), **sb("X2", N * W2, f16),
    **sb("UL", 160, u16), **sb("O16", 272, u16), **sb("TR RN", 512, f32),
    "OS": ("sbuf", [128, N, 256], f16), "OL": ("sbuf", [128, N, 256], f16), "OF": ("sbuf", [128, N, 256], f32),
    **sb("F FO", 2048, f32), **sb("SelF", 512, f16), **sb("OH", 2048, b16), **sb("E", 4096, b16), **sb("GH GO", 4352, f16),
    **sb("SN", 1024, f32), "TT": ("sbuf", [128, 8, 32], f16),
    **{n: ("psum", [128, 512], f32) for n in "pK pV pQ pY pO pT pR pM".split()},
}
SEMAPHORES = ["cv", "cs", "ct", "cg", "ra", "rb", "rc", "la", "lb", "lc", "lf"] + ["rf%d" % r for r in range(N)] + ["d%d" % i for i in range(60)]


def rank_program(g, core, T, topo):
    q = T.rank_of(core)
    if q is None:
        return
    others = [(q + i) % N for i in (1, 2, 3)]

    def plan(a):
        chip = topo.cores_of(T.cores[a])
        away = [r for r in range(N) if T.cores[r] not in chip]
        near = [r for r in range(N) if r != a and T.cores[r] in chip]
        out = topo.engines(T.cores[a], T.cores[away[0]])
        res = {}
        for n, r in enumerate(away):
            k = len(out) // len(away)
            res[r] = out[n * k:(n + 1) * k]
        for n, r in enumerate(near):
            rest = [e for e in topo.engines(T.cores[a], T.cores[r]) if e not in out]
            k = len(out) // len(away)
            res[r] = rest[n * k:(n + 1) * k]
        return res
    plans = [plan(r) for r in range(N)]
    landing = sum(len(plans[r][q]) for r in others)

    queue = {"v": g.vector, "s": g.scalar, "t": g.tensor, "g": g, "y": g.sync}
    cnt, waited, lastw, readers, total, nd = {}, {}, {}, {}, {}, [0]

    def need(qn, toks):
        best = {}
        for s, v in toks:
            best[s] = max(best.get(s, 0), v)
        for s, v in sorted(best.items()):
            if waited.get((qn, s), 0) < v:
                queue[qn].wait_ge(T.sem[s], v)
                waited[(qn, s)] = v

    def hazards(qn, reads, writes):
        toks = []
        for k in reads + writes:
            ps = k[0] == "p"
            for (oq, s, v, far) in lastw.get(k, []):
                if not (ps and oq == qn):
                    toks.append((s, v))
            if ps or k in writes:
                for (oq, s, v, far) in readers.get(k, []):
                    if far or oq != qn or k[:2] == "c_":
                        toks.append((s, v))
        return toks

    def record(tok, reads, writes):
        for k in reads:
            if k not in writes:
                readers.setdefault(k, []).append(tok)
        for k in writes:
            lastw[k] = [tok]
            readers[k] = []

    def op(qn, fn, reads, writes):
        need(qn, hazards(qn, reads, writes))
        s = "c" + qn
        cnt[s] = cnt.get(s, 0) + 1
        fn().then_inc(T.sem[s], 1)
        total[s] = cnt[s]
        record((qn, s, cnt[s], False), reads, writes)

    def dma(qn, out_, in_, reads, writes):
        need(qn, hazards(qn, reads, writes))
        s = "d%d" % nd[0]
        nd[0] += 1
        queue[qn].dma_start(out_, in_).then_inc(T.sem[s], 16)
        total[s] = 16
        record((qn, s, 16, True), reads, writes)

    def send(src, dst, reads, lands, rsem, lsem):
        need("g", hazards("g", reads, []))
        tr = []
        for r in others:
            rid, pid = topo.addr(T.cores[r], core)
            tr.append(RemoteDMATransfer(dst_ids=[DstId(rid=rid, pnc=pid)], dma_engine_mask=sum(1 << e for e in plans[q][r]),
                                        remote_sem=T.sem[rsem], src=src(r), dst=dst(r)))
        g.remote_dma_fused(tr, local_sem=T.sem[lsem])
        total[lsem] = sum(len(plans[q][r]) for r in others)
        for k in reads:
            readers.setdefault(k, []).append(("g", lsem, total[lsem], True))
        lastw[lands] = [("remote", rsem, landing, True)]
        readers[lands] = []
        total[rsem] = landing

    V, S, E_ = g.vector, g.scalar, g.tensor

    def ts(o, i, s1, s2, a, b, reads, writes):
        if b is None:
            op("v", lambda: V.tensor_scalar(o, i, s1, None, a), reads, writes)
        else:
            op("v", lambda: V.tensor_scalar(o, i, s1, s2, a, b), reads, writes)

    def tt(o, i0, i1, a, reads, writes):
        op("v", lambda: V.tensor_tensor(o, i0, i1, a), reads, writes)

    def cp(o, i, reads, writes):
        op("v", lambda: V.tensor_copy(o, i), reads, writes)

    def fill(o, c, *w):
        op("v", lambda: V.memset(o, c), [], list(w))

    def act(o, i, reads, writes, func=AF.Copy, **kw):
        op("s", lambda: S.activation(o, i, func, **kw), reads, writes)

    def mm(o, l, r, st, sp, reads, writes):
        op("t", lambda: E_.matmul(o, l, r, st, sp), reads, writes)

    def scan(o, d0, d1, a, b, reads, writes):
        op("v", lambda: V.tensor_tensor_scan(o, d0, d1, 0.0, a, b), reads, writes)

    def iota(n, pat, base=0, cm=0):
        o = T[n]
        if n == "iA":
            op("g", lambda: g.iota(o[:], pat, base, cm), [], [n])
        else:
            op("g", lambda: g.iota(o[:], pat, base, cm, allow_small_or_imprecise_dtypes=True), [], [n])

    def number(o, c, key):
        op("g", lambda: g.iota(o, [[0, o.shape[1]]], c, 0, allow_small_or_imprecise_dtypes=True), [], [key])

    def pick(o, i, pat, base, reads, writes):
        op("g", lambda: g.affine_select(o, i, pat, A.is_equal, 0.0, base, -1), reads, writes)

    TAT, CAT = {1: 0, 2: 176, 3: 304, 0: 480}, {1: 128, 2: 128, 3: 432, 0: 128}

    def first(r, part, a, b):
        d = (q - r) % N
        at = (TAT, CAT)[part][d]
        if d == 0:
            return T.TS[:, at + a:at + b], ["TS0", "TC"][part]
        at += W1 * r - min(TAT[d], CAT[d])
        return T.X1[:, at + a:at + b], "X1"

    def second(r, a, b):
        return T.X2[:, W2 * r + a:W2 * r + b], "XR" if r == q else "X2"

    def ul(t, order):
        a = 32 * t + 16 * order
        return T.UL[:, a:a + 16], "UL%d" % (t > 0)

    for d in (1, 2, 3):
        r = (q + d) % N
        dma("ysy"[d - 1], T.TI[:, TAT[d]:TAT[d] + 128], T.trunk[32 * r:32 * r + 32, :], [], ["TI%d" % d])
    dma("s", T.IN[:, 336:352], T.calls[:], [], ["IC"])
    for t in range(RO):
        a = 256 + 16 * ((t - 1) % RO)
        dma("sysys"[t], T.IN[:, a:a + 16], T.routes[t::16, :], [], ["IL%d" % t])
    dma("y", T.IN[:, 0:256], T.routes[:], [], ["IR"])
    INK = ["IL%d" % n for n in range(1, RO)]
    dma("s", T.TI[:, TAT[0]:TAT[0] + 128], T.trunk[32 * q:32 * q + 32, :], [], ["TI0"])
    for x in range(N):
        dma("y", T.FB[:, 128 * x:128 * x + 128], T.paths[32 * q:32 * q + 32, G * x:G * x + G], [], ["FB%d" % x])
    FK = ["F%d" % n for n in range(N)]
    WK = ["W%d" % x for x in range(N)]

    iota("iA", [[0, 1]], 0, 1)
    iota("iB", [[16, 4]])
    iota("iX", [[1, 176]])
    iota("ONE", [[0, 256]], 1)
    bits = [(0, 15), (0, 3), (2, 3), (0, 127), (4, 1), (5, 3), (6, 1), (4, 3), (4, 7), (2, 15)]
    names = "k y z pc n4 o n6 hh gg kk".split()
    col = {n: T.CF[:, i:i + 1] for i, n in enumerate(names + "sw k16 o512 gp tZ eb early late tS u v gs gb rs m3 up dn".split())}

    def parts(a, b):
        for i in range(a, b):
            ts(T.CC[:, i:i + 1], T.iA[:], bits[i][0], bits[i][1], A.logical_shift_right, A.bitwise_and, ["iA"], ["CC%d" % i])
        cp(T.CF[:, a:b], T.CC[:, a:b], ["CC%d" % i for i in range(a, b)], ["c_" + n for n in names[a:b]])

    def num(o, i, s1, s2, a, b):
        rd = ["c_" + x for x in (i, s1, s2) if isinstance(x, str)]
        ts(col[o], col[i], col.get(s1, s1), col.get(s2, s2), a, b, rd, ["c_" + o])

    parts(0, 5)
    num("sw", "y", 4.0, "z", A.mult, A.add)
    num("k16", "k", 16.0, None, A.mult, None)
    ts(T.OFS[:, 0:1], col["k"], 16.0, None, A.add, None, ["c_k"], ["OFc"])
    cp(T.OFS[:, 1:2], col["sw"], ["c_sw"], ["OFd"])
    cp(T.OFS[:, 2:3], col["k"], ["c_k"], ["OFe"])
    ts(T.OFS[:, 12:28], T.iX[:, 0:16], col["k16"], None, A.add, None, ["iX", "c_k16"], ["OFR"])
    ts(T.Id16[:], T.iX[:, 0:128], col["pc"], None, A.is_equal, None, ["iX", "c_pc"], ["Id16"])

    act(T.Idb[:], T.Id16[:], ["Id16"], ["Idb"])
    act(T.NK[:], T.Id16[:], ["Id16"], ["NK"], scale=-32.0)
    act(T.Idm[:], T.Id16[:], ["Id16"], ["Idm"], scale=-1.0)
    act(T.Idn[:], T.Id16[:], ["Id16"], ["Idn"], scale=9.0 * LK)
    act(T.Idk[:], T.Id16[:], ["Id16"], ["Idk"], scale=-DEAD)
    act(T.Id32[:], T.Id16[:, 0:32], ["Id16"], ["Id32"])

    def spread_table(y):
        pick(T.SelF[:, 128 * y:128 * y + 128], T.ONE[:, 0:128], [[64, 2], [0, 4], [4, 16]], y, ["ONE"], ["SelF%d" % y])

    spread_table(0)
    spread_table(1)
    num("u", "n4", 64.0, "k", A.mult, A.add)
    ts(T.OFS[:, 4:12:2], T.iB[:], col["sw"], None, A.add, None, ["iB", "c_sw"], ["OFa"])
    ts(T.SelR[:], T.iX[:], -48.0, col["u"], A.add, A.is_equal, ["iX", "c_u"], ["SelR"])
    ts(T.OFS[:, 5:12:2], T.iB[:], col["k"], None, A.add, None, ["iB", "c_k"], ["OFb"])
    cp(T.TS[:, 0:128], T.TI[:, 0:128], ["TI1"], ["TS1"])
    for d in (1, 3):
        cp(T.TS[:, CAT[d]:CAT[d] + 48], T.IN[:, 320:352].indirect(T.OFS[:, 0:3]), ["IC", "IL0", "OFc", "OFd", "OFe"], ["TC" if d == 1 else "TC3"])
    cp(T.TS[:, 176:432], T.TI[:, 176:432], ["TI2", "TI3"], ["TS2"])
    send(lambda r: T.TS[:, min(TAT[(r - q) % N], CAT[(r - q) % N]):min(TAT[(r - q) % N], CAT[(r - q) % N]) + W1],
         lambda r: T.X1[:, W1 * q:W1 * q + W1], ["TS1", "TS2", "TC", "TC3"], "X1", "ra", "la")
    spread_table(2)
    spread_table(3)
    number(T.CF[:, 30:31], 1 - 16 * NONE, "c_all")
    number(T.CF[:, 31:32], int(DEAD), "c_dead")
    iota("iC", [[1, 16], [0, 16]])
    act(T.RQ[:], T.IN[:, 0:256].indirect(T.OFS[:, 12:28]), ["IR", "OFR"], ["RQ"])
    for r in others + [q]:
        need("t", [("ct", cnt.get("ct", 0))])
        for h in range(4):
            mm(T.pR[:, 64 * r:64 * r + 64], T.SelR[32 * r:32 * r + 32, 48 - 16 * h:176 - 16 * h], T.RQ[32 * r:32 * r + 32, 64 * h:64 * h + 64],
               h == 0, h == 3, ["SelR", "RQ"], ["pR"])
    act(T.RS[:], T.pR[:, 0:256], ["pR"], ["RS"])
    send(lambda r: T.RS[:, 64 * r:64 * r + 64], lambda r: T.R[:, 64 * q:64 * q + 64], ["RS"], "RX", "rb", "lb")
    act(T.R[:, 64 * q:64 * q + 64], T.RS[:, 64 * q:64 * q + 64], ["RS"], ["RO"])
    act(second(q, 0, W2)[0], T.IN[:, 256:320].indirect(T.OFS[:, 4:12]), INK + ["OFa", "OFb"], ["XR"])
    send(lambda r: second(q, 0, W2)[0], lambda r: second(q, 0, W2)[0], ["XR"], "X2", "rc", "lc")
    iota("iCa", [[1, 4], [4, 4], [0, 16]])
    pick(T.OT[:], T.ONE[:], [[1, 32], [0, 2], [32, 4]], 0, ["ONE"], ["OT"])

    def scan_mask(h):
        op("g", lambda: g.affine_select(T.SMb[:, 256 * h:256 * h + 256], T.ONE[:], [[0, 16], [1, 16]], A.not_equal, 0.0, 0, 0), ["ONE"], ["SMb%d" % h])

    scan_mask(0)
    iota("BN0", [[0, 256]])
    iota("CKf", [[0, 16], [-1, 16]], -17)
    number(col["eb"], int(9 * LK) - 16384 - 16, "c_eb")
    iota("SIX", [[0, 256]], 6)
    number(T.CF[:, 29:30], -N * NONE, "c_four")
    for n, (step, cmp, c) in enumerate([(-1, A.is_ge, -17.0), (1, A.is_ge, -1.0), (1, A.not_equal, 16.0)]):
        op("g", lambda: g.affine_select(T.TT[:], T.TT[:] if n else T.ONE[:], [[0, 8], [step, 32]], cmp, c / 2048, -15 * step, 0), ["ONE", "TT"], ["TT"])
    pick(T.TT[:], T.TT[:], [[16, 4], [64, 2], [0, 32]], 15, ["TT"], ["TT"])
    number(T.SH[:, 16:32], 15, "SH1")
    iota("LOD", [[0, 768]], -1)
    scan_mask(1)
    iota("ZER", [[0, 128]])
    op("g", lambda: g.affine_select(T.Dm[:], T.ZER[:, 0:128], [[1, 128]], A.not_equal, DEAD, 0, -1), ["ZER"], ["Dm"])
    op("g", lambda: g.affine_select(T.Dm[:], T.Dm[:], [[1, 128]], A.not_equal, -DEAD, -1, -1), ["Dm"], ["Dm"])
    op("g", lambda: g.affine_select(T.Dm[:], T.Dm[:], [[200, 128]], A.not_equal, DEAD, -127, 1), ["Dm"], ["Dm"])
    op("g", lambda: g.affine_select(T.TO[:], T.ZER[:, 0:128], [[16, 4], [64, 2], [0, 16]], A.not_equal, -32.0 / 2048, 15, -1), ["ZER"], ["TO"])
    number(T.CF[:, 27:28], 1, "c_one")
    number(T.CF[:, 28:29], NONE, "c_none")
    iota("BIG", [[0, 128]], 4096)
    for x in range(N):
        pick(T.ZD[0:32, 128 * x:128 * x + 128], T.BIG[0:32, :], [[16, 2], [0, 16], [1, 4]], 4 * x, ["BIG"], ["ZD%d" % x])
    for o in range(N):
        pick(T.ST[32 * o:32 * o + 32, :], T.ONE[32 * o:32 * o + 32, 0:144], [[1, 36], [100, 4]], -300, ["ONE"], ["ST%d" % o])

    parts(5, 10)
    num("o512", "o", 512.0, None, A.mult, None)
    num("gp", "hh", 2.0, "n6", A.mult, A.add)
    num("tZ", "n6", 16.0, "y", A.mult, A.add)
    num("v", "kk", 15.0, -1.0 / 64, A.is_equal, A.mult)
    num("m3", "kk", 15.0, 4.0, A.is_equal, A.mult)
    num("gb", "k", 15.0, DEAD, A.is_equal, A.mult)
    num("gs", "k", 15.0, -2.0, A.is_equal, A.mult)
    num("rs", "k", 15.0, 1.0 / 64 - 1, A.is_equal, A.mult)
    num("m3", "m3", -3.0, None, A.add, None)
    num("gs", "gs", 1.0, None, A.add, None)
    num("rs", "rs", 1.0, None, A.add, None)
    cp(T.TS[:, 480:608], T.TI[:, 480:608], ["TI0"], ["TS0"])
    ts(T.Zq[:], T.iX[:, 0:48], -12.0, col["tZ"], A.add, A.is_equal, ["iX", "c_tZ"], ["Zq"])
    ts(T.Z15[:], T.Zq[:], col["v"], None, A.mult, None, ["Zq", "c_v"], ["Z15"])
    ts(T.IND[:], T.iX[:, 0:8], col["gg"], None, A.is_equal, None, ["iX", "c_gg"], ["IND"])
    ts(T.BL[:], T.iX[:, 0:8], col["gp"], LK, A.is_equal, A.mult, ["iX", "c_gp"], ["BL"])
    ts(T.REP[:], T.iX[:, 0:16], 0.0, col["k"], A.mult, A.add, ["iX", "c_k"], ["REP"])
    cp(T.FB16[:], T.FB[:], ["FB%d" % x for x in range(N)], ["FB16"])

    def all_none(paths):
        for x in range(N):
            mm(T.pY[0:32, 0:128], T.Zq[:, 12 - 4 * x:44 - 4 * x], T[paths][:, 128 * x:128 * x + 128], x == 0, x == N - 1, ["Zq", paths], ["pY"])

    def dead_flags(flags):
        act(T[flags][0:32, :], T.pY[0:32, 0:128], ["pY", "c_all"], [flags], func=AF.Relu, bias=T.CF[0:32, 30:31])

    def marks(flags, out):
        for x in range(N):
            mm(T.pY[0:32, 0:128], T.Z15[:, 12 - 4 * x:44 - 4 * x], T.FB16[:, 128 * x:128 * x + 128], x == 0, False, ["Z15", "FB16"], ["pY"])
        mm(T.pY[0:32, 0:128], T.Idk[0:32, 0:32], T[flags][0:32, :], False, True, ["Idk", flags], ["pY"])
        act(T[out][0:32, :], T.pY[0:32, 0:128], ["pY", "c_dead"], [out], func=AF.Relu, bias=T.CF[0:32, 31:32])

    def spread_marks():
        for x in range(N):
            dma(MQ[x], T.F[16 * x + 15::64, :], T.NA[0:32, :], ["NA"] + FK, [WK[x]])

    def trunks(o, h):
        src, key = first(o, 0, 0, 128)
        bank = ["pT", "pR"][h]
        for x in range(2):
            mm(T[bank][32 * o:32 * o + 32, 128 * x:128 * x + 128], T.Id16[:, 2 * h + x::4], src, True, True, ["Id16", key], [bank])

    num("u", "n6", 64.0, 3.0, A.mult, A.add)
    num("early", "k", float(RO), None, A.is_lt, None)
    num("u", "k", 4.0, "u", A.mult, A.add)
    num("late", "k", float(RO), float(NONE), A.is_ge, A.mult)
    num("v", "k", 15.0, None, A.is_lt, None)
    num("tS", "n6", 16.0, "k", A.mult, A.add)
    num("late", "late", "v", None, A.mult, None)
    ts(T.SD[:], T.iX[:, 0:144], col["u"], col["v"], A.is_equal, A.mult, ["iX", "c_u", "c_v"], ["SD"])
    ts(T.Id3[:], T.Id16[:], col["m3"], None, A.mult, None, ["Id16", "c_m3"], ["Id3"])
    ts(T.Zs[:], T.iX[:, 0:32], col["tS"], None, A.is_equal, None, ["iX", "c_tS"], ["Zs"])
    ts(T.IdS[:], T.Id16[:], col["rs"], None, A.mult, None, ["Id16", "c_rs"], ["IdS"])
    fill(T.SH[:, 32:48], 127.5, "SH2")
    trunks(q, 0)
    trunks(q, 1)
    all_none("FB16")
    dead_flags("Yf")
    for x, bank in enumerate(["pQ", "pV", "pK", "pM"]):
        for y in range(4):
            mm(T[bank][:, 128 * y:128 * y + 128], T.SelF[:, 128 * y:128 * y + 128], T.FB16[:, 128 * x:128 * x + 128], True, True,
               ["SelF%d" % y, "FB16"], [bank])
        if x == 1:
            marks("Yf", "NA")
        (cp if x in FV else act)(T.F[:, G * x:G * x + G], T[bank][:], [bank], [FK[x]])
    spread_marks()

    def name_masks():
        ts(T.MKa[:], T.iCa[:], col["k"], None, A.is_equal, None, ["iCa", "c_k"], ["MKa"])
        ts(T.MKb[:], T.iC[:], col["k"], None, A.is_equal, None, ["iC", "c_k"], ["MKb"])
        for h in range(2):
            ts(T.BOw[:, 128 * h:128 * h + 128], T.iC[:, 0:128], col["gg"], None, A.is_equal, None, ["iC", "c_gg"], ["BOw%d" % h])

    name_masks()
    mine = T.Id16[:, 32 * q:32 * q + 32]
    for r in [q] + others:
        src, key = first(r, 1, 0, 48)
        mm(T.pO[32 * r:32 * r + 32, 0:48], mine, src, True, True, ["Id16", key], ["pO"])
    cp(T.CQ[:], T.pO[:, 0:16], ["pO"], ["CQ"])
    ts(T.UL[:, 0:32], T.pO[:, 16:48], col["o512"], None, A.subtract, None, ["pO", "c_o512"], ["UL0"])

    def routes():
        act(T.R[:, 256:512], T.R[:, 0:256], ["RX", "RO"], ["R1"])
        mm(T.pQ[:], T.IdS[:], T.R[:, 0:512], True, True, ["IdS", "RX", "RO", "R1"], ["pQ"])

    def hold_a(t):
        L, lk = ul(t, 0)
        for h, way in enumerate([cp, cp if HAV and t else act]):
            way(T.Ha[:, 128 * h:128 * h + 128], T.TR[:].indirect(T.UL[:, 32 * t + 8 * h:32 * t + 8 * h + 8]), ["TR", "TRa", lk], ["Ha%d" % h])
        for jb in range(4):
            for n in range(2):
                mm(T.pO[64 * n:64 * n + 64, jb:256:4], T.Ha[:, 64 * jb:64 * jb + 64], T.OT[:, 16 * n:16 * n + 16, t % N:t % N + N], True, True,
                   ["Ha%d" % (jb // 2), "OT"], ["pO"])

    def lists():
        cp(T.O16[:, 0:256], T.pO[:, 0:256], ["pO"], ["O16"])

    def hold(t, name):
        L, lk = ul(t, 1)
        act(T[name][:], T.TR[:].indirect(L), ["TR", lk], [name])

    def pieces(t):
        for r in range(N):
            o = (r + t) % N
            for h in range(4):
                yield 64 * (r % 2), 128 * (r // 2) + 32 * h, 32 * o, 64 * h

    def keys(t):
        mm(T.pR[:, 256:512], T.Idb[:], T.BND[:], True, False, ["Idb", "BND"], ["pR"])
        for n, (a, b, c, d) in enumerate(pieces(t)):
            mm(T.pR[a:a + 64, 256 + b:288 + b], T.Hc[:, d:d + 64], T.NK[:, c:c + 32], False, n in (11, 15), ["Hc", "NK"], ["pR"])
        a = 32 * (N - t % N)
        mm(T.pR[:, 0:256], T.BOw[:, a:a + 128], T.CMb[:], True, False, ["BOw0", "BOw1", "CMb"], ["pR"])
        mm(T.pR[:, 0:256], T.Idm[:], T.Hc[:], False, True, ["Idm", "Hc"], ["pR"])
        mm(T.pK[:, 0:256], T.Idb[:], T.BND[:], True, False, ["Idb", "BND"], ["pK"])
        mm(T.pK[:, 0:256], T.Idb[:], T.CKf[:], False, False, ["Idb", "CKf"], ["pK"])
        for a, b, c, d in pieces(t):
            mm(T.pK[a:a + 64, b:b + 32], T.Hc[:, d:d + 64], T.NK[:, c:c + 32], False, False, ["Hc", "NK"], ["pK"])
        mm(T.pV[:, 0:256], T.Idb[:], T.SIX[:], True, False, ["Idb", "SIX"], ["pV"])

    def keys_s():
        act(T.ELIG[:], T.pR[:, 256:512], ["pR", "c_eb"], ["ELIG"], func=AF.Sign, bias=col["eb"])

    def gather(way, a, b, old):
        o, win = T[["GH", "GO"][old]][:, 256 * a:256 * b], T[["F", "FO"][old]][:].indirect(T.O16[:, 16 * a:16 * b])
        rd = (["FO%d" % x for x in range(N)] if old else FK + WK) + ["O16", "SL", "c_gs", "c_gb"]
        wr = ["G%s%d" % ("O" * old, p) for p in range(a, b)]
        if way is act:
            act(o, win, rd, wr, func=AF.Identity, scale=col["gs"], bias=col["gb"])
        else:
            ts(o, win, col["gs"], col["gb"], A.mult, A.add, rd, wr)

    def like_v(a, b, old):
        tt(T.E[:, 256 * a:256 * b], T[["GH", "GO"][old]][:, 256 * a:256 * b], T.pQ[:, 0:256 * (b - a)], A.is_equal,
           ["pQ"] + ["G%s%d" % ("O" * old, p) for p in range(a, b)], ["E%d" % p for p in range(a, b)])

    def like_t(p, last):
        for b in range(2):
            mm(T.pK[:, 128 * b + p:128 * b + 128:16], T.E[:, 256 * p + 128 * b:256 * p + 128 * b + 128], T.BL[:], False, last and b == 1,
               ["E%d" % p, "BL"], ["pK"])

    def dead_t(p, last):
        for b in range(2):
            w = T.TT[:, :, 15 - p:31 - p] if p < 16 else T.TO[:]
            mm(T.pV[:, 128 * b:128 * b + 128], T.GH[:, 256 * p + 128 * b:256 * p + 128 * b + 128], w, False, b == 1 and last,
               ["G%d" % p, "TT" if p < 16 else "TO"], ["pV"])

    def pairs(a, b):
        return [(c, min(c + 2, b)) for c in range(a, b, 2)]

    def look_up(t):
        ev, es, nv, vd = PLAN[t]
        early = ev + es
        turns, ready, clock = [], {}, {act: 0.0, ts: 0.0}

        def fetch(way, c, old):
            gather(way, c[0], c[1], old)
            clock[way] += GC * (c[1] - c[0])
            ready[c] = clock[way]
            if not old:
                turns.append((clock[way] + DOFF, 1, c))

        def compare(c, old):
            like_v(c[0], c[1], old)
            clock[ts] = max(clock[ts], ready[c]) + CC * (c[1] - c[0])
            turns.append((clock[ts], 0, c))

        for c in pairs(ev, early):
            fetch(act, c, True)
        if t:
            keys_s()
        for a, b in pairs(0, ev):
            tt(T.E[:, 256 * a:256 * b], T.FO[:].indirect(T.O16[:, 16 * a:16 * b]), T.RN[:, 0:256 * (b - a)], A.is_equal,
               ["FO%d" % x for x in range(N)] + ["O16", "RN"], ["E%d" % p for p in range(a, b)])
            clock[ts] += 2 * CC * (b - a)
            turns.append((clock[ts], 0, (a, b)))
        for c in pairs(ev, early):
            compare(c, True)
        clock[act] = clock[ts] = max(clock[act], clock[ts])
        mine_v, mine_s = pairs(early, early + nv), pairs(early + nv, 15) + [(15, 16)]
        for n, c in enumerate(mine_s):
            if n == 0:
                for d in mine_v:
                    fetch(ts, d, False)
            if t == 0 and n == SB:
                keys_s()
            fetch(act, c, False)
        for c in pairs(vd, early) + [(16, 17)] * (t > 0):
            fetch(act, c, False)
        for n, c in enumerate(mine_v + mine_s):
            compare(c, False)
            if t == 0 and n == 2:
                other_lists_v()
        turns.sort()
        ends = [[x for x in turns if x[1] == kind][-1] for kind in (0, 1)]
        for n, x in enumerate(turns):
            if n == 2:
                for y in SHARES[t - 1]:
                    hops_t(y)
            if n == 8:
                mm(T.pK[:, 0:256], T.Idn[:], T.ELIG[:], False, False, ["Idn", "ELIG"], ["pK"])
            if n == 12 and t == 0:
                seekers()
            if x == ends[1] and vd:
                late.append(x[2])
                continue
            for p in range(*x[2]):
                (dead_t if x[1] else like_t)(p, x in ends and p == x[2][1] - 1)

    late = []

    def piece(t, n):
        if PLAN[t][3]:
            a, b = CUTS[n:n + 2]
            ts(T.GH[:, 16 * a:16 * b], T.F[:].indirect(T.O16[:, a:b]), col["gs"], col["gb"], A.mult, A.add,
               FK + WK + ["O16", "c_gs", "c_gb"], ["G0" if b == 16 else "Gp%d" % n])
            if b == 16:
                need("t", [("cv", cnt["cv"])])
                for p in [0] + list(range(*late[-1])):
                    dead_t(p, p == late[-1][1] - 1)

    def whole():
        ts(T.pV[:, 0:256], T.pV[:, 0:256], 1.5 * 2 ** 27, -1.5 * 2 ** 27, A.add, A.add, ["pV"], ["pV"])

    def onehot(way, a, b):
        for c in range(a, b):
            o, low = T.OH[:, 128 * c:128 * c + 128], T.LOD[:, 512 + 16 * c:513 + 16 * c]
            if way is ts:
                ts(o, T.iX[:, 0:128], 0.5, low, A.add, A.is_equal, ["iX", "LOD"], ["OH%d" % c])
            else:
                act(o, T.iX[:, 1:129], ["iX", "LOD"], ["OH%d" % c], func=AF.Sign, scale=-1.0, bias=low)

    def decide(t):
        piece(t, 0)
        scan(T.SC1[:], T.SMb[:, 0:256], T.pK[:, 0:256], A.mult, A.max, ["SMb0", "pK"], ["SC1"])
        piece(t, 1)
        tt(T.BI[:], T.SC1[:, 15::16], T.SK[:], A.max, ["SC1", "SK"], ["BI"])
        piece(t, 2)
        for n, (sh, m) in enumerate([(12, 15), (0, 31), (5, 127)]):
            ts(T.XI[:, 16 * n:16 * n + 16], T.BI[:], sh, m, A.logical_shift_right, A.bitwise_and, ["BI"], ["XI%d" % n])
        piece(t, 3)
        tt(T.LOD[:, 0::16], T.SH[:], T.XI[:], A.subtract, ["SH0", "SH1", "SH2", "XI0", "XI1", "XI2"], ["LOD"])
        piece(t, 4)
        scan(T.LOS[:], T.SMb[:], T.LOD[:, 0:512], A.mult, A.add, ["SMb0", "SMb1", "LOD"], ["LOS"])
        act(T.DIFF[:], T.pR[:, 0:256], ["pR"], ["DIFF"])
        nv = OHV[t]
        onehot(act, nv, 16)
        for x in SHARES[t][:SAT]:
            hops_s(x)
        onehot(ts, 0, 1)
        ts(T.LO[:], T.LOS[:, 256:512], 0.0, 14.0, A.not_equal, A.mult, ["LOS"], ["LO"])
        onehot(ts, 1, nv - OH3)
        tt(T.SEO[:], T.pV[:, 0:256], T.LO[:], A.is_lt, ["pV", "LO"], ["SEO"])
        for a, b, c, d in pieces(t):
            mm(T.pT[c:c + 32, d:d + 64], T.SEO[a:a + 64, b:b + 32], T.Idb[a:a + 64, a:a + 64], True, True, ["SEO", "Idb"], ["pT"])
        whole()
        onehot(ts, nv - OH3, nv - OH3 + 2)
        need("v", [("cv", cnt["cv"] - 2)])
        tt(T.LOO[:], T.pV[:, 0:256], T.LOS[:, 0:256], A.is_equal, ["pV", "LOS"], ["LOO"])
        onehot(ts, nv - OH3 + 2, nv)
        kills(t)
        tt(T.DM[:], T.pT[:, 0:256], T.DIFF[:], A.mult, ["pT", "DIFF"], ["DM"])
        L, lk = ul(t, 1)
        u = t % N
        tt(T.TR[:].indirect(L), T.SN[:, 256 * u:256 * u + 256], T.DM[:], A.subtract, ["SN%da" % u, "SN%db" % u, "DM", lk], ["TR"])

    def kills(t):
        kinds = [x for x in (range(OHV[t], 16), range(OHV[t])) if len(x)]
        for kind in kinds:
            for n in range(2):
                col0, ss = 16 * n + (32 if kind[0] else 0), [s for s in kind if s % 2 == n]
                for s in ss:
                    mm(T.pO[:, 256 + col0:272 + col0], T.OH[:, 128 * s:128 * s + 128], T.LOO[:, 16 * s:16 * s + 16], s == ss[0], s == ss[-1],
                       ["LOO", "OH%d" % s], ["pO"])
        y = "NA" if t else "NB"
        mm(T.pY[0:32, 0:128], T.Id32[0:32, :], T[y][0:32, :], True, False, ["Id32", y], ["pY"])
        act(T.KS[:, 0:32 * len(kinds)], T.pO[:, 256:256 + 32 * len(kinds)], ["pO"], ["KS"])
        if len(kinds) > 1:
            mm(T.pY[0:32, 0:128], T.KS[:, 32:64], T.Dm[:], False, False, ["Dm", "KS"], ["pY"])
        mm(T.pY[0:32, 0:128], T.KS[:, 0:32], T.Idk[:], False, True, ["Idk", "KS"], ["pY"])
        if t < RO - 1:
            act(T.NA[0:32, :], T.pY[0:32, 0:128], ["pY"], ["NA"], func=AF.Relu)
            spread_marks()
        else:
            act(T.Yz[0:32, :], T.pY[0:32, 0:128], ["pY", "c_one"], ["Yz"], func=AF.Relu, scale=-1.0, bias=T.CF[0:32, 27:28])

    def seeker_names():
        tt(T.CMb[:], T.CQ[:].indirect(T.REP[:]), T.MKb[:], A.mult, ["CQ", "REP", "MKb"], ["CMb"])
        for h in range(2):
            for o in others:
                trunks(o, h)
        act(T.TR[:, 0:256], T.pT[:, 0:256], ["pT"], ["TRa"])
        cp(T.TR[:, 256:512], T.pR[:, 0:256], ["pR"], ["TR"])
        for r in range(N):
            for h in range(4):
                a, s = 64 * (r % 2), 8 * (r // 2) + 2 * h
                mm(T.pT[a:a + 64, s:s + 2], T.CMb[:, 64 * h:64 * h + 64], T.IND[:, 2 * r:2 * r + 2], True, True, ["CMb", "IND"], ["pT"])
        hold_a(0)
        tt(T.CMa[:], T.CQ[:].indirect(T.REP[:]), T.MKa[:], A.mult, ["CQ", "REP", "MKa"], ["CMa"])
        lists()
        for n in range(2):
            for jb in range(4):
                mm(T.pY[64 * n:64 * n + 64, jb:16:4], T.CMa[:, 64 * jb:64 * jb + 64], T.IND[:, n::2], True, True, ["CMa", "IND"], ["pY"])

    def seeker_keys():
        cp(T.NI32[:], T.pT[:, 0:16], ["pT"], ["NI32"])
        cp(T.O16[:, 256:272], T.pY[:, 0:16], ["pY"], ["SL"])
        ts(T.BD[:], T.NI32[:], 1536, None, A.bitwise_and, None, ["NI32"], ["BD"])
        hops_v()
        ts(T.BN0[:, 0::16], T.BD[:], 32.0, 16384 - 9 * LK, A.mult, A.add, ["BD"], ["BN0"])
        tt(T.NF[:], T.BD[:], T.NI32[:], A.subtract, ["BD", "NI32"], ["NF"])
        scan(T.BND[:], T.SMb[:, 0:256], T.BN0[:], A.mult, A.add, ["SMb0", "BN0"], ["BND"])
        ts(T.SK[:], T.NF[:], 32.0, 16368.0, A.mult, A.add, ["NF"], ["SK"])
        ts(T.SH[:, 0:16], T.BD[:], 1.0 / 128, 3.0, A.mult, A.add, ["BD"], ["SH0"])

    def other_lists():
        for r in range(N):
            for t in range(1, RO):
                src, key = second(r, 32 * t - 32, 32 * t)
                o = (r + t) % N
                mm(T.pT[32 * o:32 * o + 32, 32 * t:32 + 32 * t], mine, src, True, True, ["Id16", key], ["pT"])

    def other_lists_v():
        ts(T.UL[:, 32:160], T.pT[:, 32:160], col["o512"], None, A.subtract, None, ["pT", "c_o512"], ["UL1"])

    def hops_v():
        cp(T.F[:].indirect(T.O16[:, 256:272]), T.RF[:], ["RF", "SL"], FK + WK)
        dma("y", T.FX[:], T.F[0::16, :], FK, ["FX"])

    def hops_t(x):
        if x == 0:
            mm(T.pM[:], T.Id3[:], T.FB16[:], True, False, ["Id3", "FB16"], ["pM"])
        for y in range(4):
            mm(T.pM[:, 128 * x:128 * x + 128], T.SD[:, 3 - y:131 - y], T.F16[:, G * x + 128 * y:G * x + 128 * y + 128], False, False,
               ["SD", "F16%d" % x], ["pM"])

    def hops_s(x):
        act(T.F16[:, G * x:G * x + G], T.FO[:, G * x:G * x + G], ["FO%d" % x], ["F16%d" % x])

    def names_h():
        mm(T.pM[:, 0:256], T.BOw[:, 0:128], T.CMb[:], True, True, ["BOw0", "CMb"], ["pM"])

    def names_s():
        act(T.SN[:, 0:256], T.pM[:, 0:256], ["pM"], ["SN0a", "SN0b"])
        for t in range(1, N):
            dma("y", T.SN[32 * t:128, 256 * t:256 * t + 256], T.SN[0:128 - 32 * t, 0:256], ["SN0a"], ["SN%da" % t])
            dma("y", T.SN[0:32 * t, 256 * t:256 * t + 256], T.SN[128 - 32 * t:128, 0:256], ["SN0a"], ["SN%db" % t])

    def copy_paths():
        for x in range(N):
            dma("y", T.FO[:, G * x:G * x + G], T.F[:, G * x:G * x + G], FK + WK, ["FO%d" % x])

    def seekers():
        mm(T.pY[0:32, 0:128], T.Zs[:], T.FX[:], True, False, ["Zs", "FX"], ["pY"])
        mm(T.pY[0:32, 0:128], T.Id16[0:32, 0:32], T.Yf[0:32, :], False, True, ["Id16", "Yf"], ["pY"])

    def seekers_marks():
        act(T.YfB[0:32, :], T.pY[0:32, 0:128], ["pY", "c_four"], ["YfB"], func=AF.Relu, bias=T.CF[0:32, 29:30])
        marks("YfB", "NB")
        act(T.RN[:], T.pQ[:], ["pQ", "c_gs", "c_gb"], ["RN"], func=AF.Identity, scale=col["gs"], bias=col["gb"])

    seeker_names()
    routes()
    act(T.RF[:], T.R[:, 0:256], ["RX", "RO", "c_early", "c_late"], ["RF"], func=AF.Identity, scale=col["early"], bias=col["late"])
    hold(0, "Hc")
    names_h()
    seeker_keys()
    names_s()
    copy_paths()
    other_lists()
    for t in range(RO):
        keys(t)
        look_up(t)
        if t == 0:
            seekers_marks()
        decide(t)
        if t < RO - 1:
            hold_a(t + 1)
            lists()
            hold(t + 1, "Hc")
            for x in SHARES[t][SAT:]:
                hops_s(x)
    for x in range(N):
        mm(T.pM[:, 128 * x:128 * x + 128], T.ZD[0:32, 128 * x:128 * x + 128], T.Yz[0:32, :], False, x == N - 1, ["ZD%d" % x, "Yz"], ["pM"])
    banks = list(zip(others + [q], ["pK", "pT", "pR", "pO"]))
    for y in range(4):
        cp(T.TR16[:, 128 * y:128 * y + 128], T.TR[:, 128 * y:128 * y + 128], ["TR"], ["TR16%d" % y])
    act(T.OS[:, :, 128:256], T.pM[:], ["pM", "c_none"], ["OP"], func=AF.Relu, scale=-1.0, bias=T.CF[:, 28:29])
    for y in range(4):
        for o, bank in banks:
            mm(T[bank][:, 0:128], T.ST[32 * o:32 * o + 32, 3 - y:131 - y], T.TR16[32 * o:32 * o + 32, 128 * y:128 * y + 128], y == 0, y == 3,
               ["ST%d" % o, "TR16%d" % y], [bank])
    for n, (o, bank) in enumerate(banks):
        (act if n == 1 else cp)(T.OS[:, o, 0:128], T[bank][:, 0:128], [bank], ["OY%d" % o])
    send(lambda r: T.OS[:, r, :], lambda r: T.OL[:, q, :], ["OP"] + ["OY%d" % r for r in others], "OL", "rf%d" % q, "lf")
    del total["rf%d" % q]
    near = [r for r in others if T.cores[r] in topo.cores_of(core)]
    for n, r in enumerate([q] + near + [r for r in others if r not in near]):
        if r != q:
            total["rf%d" % r] = len(plans[r][q])
            lastw["OL"] = [("remote", "rf%d" % r, total["rf%d" % r], True)]
        src, keys_ = (T.OS, ["OP", "OY%d" % q]) if r == q else (T.OL, ["OL"])
        cp(T.OF[:, r, 0:128], src[:, r, 0:128], keys_, ["OFy%d" % r])
        act(T.OF[:, r, 128:256], src[:, r, 128:256], keys_ + ["c_none"], ["OFp%d" % r], func=AF.Identity, scale=-1.0, bias=T.CF[:, 28:29])
        dma("y", T.yt[32 * r:32 * r + 32, :], T.OF[:, r, 0:128], ["OFy%d" % r], ["yt%d" % r])
        dma("s", T.yp[32 * r:32 * r + 32, :], T.OF[:, r, 128:256], ["OFp%d" % r], ["yp%d" % r])
    need("g", [(s, v) for s, v in total.items()])
